import numpy as np
import ml_dtypes


def mxq(x, axis, fmt="e4m3"):
    dtype, down = {"e4m3": (ml_dtypes.float8_e4m3fn, 7), "e5m2": (ml_dtypes.float8_e5m2, 14)}[fmt]
    v = np.moveaxis(np.asarray(x, np.float32).astype(ml_dtypes.bfloat16).astype(np.float64), axis, -1)
    blocks = v.reshape(v.shape[:-1] + (-1, 32))
    amax = np.abs(blocks).max(-1, keepdims=True)
    byte = np.maximum(np.where(amax > 0, np.frexp(amax)[1] - 1 + 127, 0) - down, 1)
    scale = np.exp2(byte - 127.0)
    codes = (blocks / scale).astype(np.float32).astype(dtype).astype(np.float64)
    return np.moveaxis((codes * scale).reshape(v.shape), -1, axis)


WIDE = False


def mx_kscale(k):
    if not WIDE:
        return np.ones(k)
    levels = np.array([10, -10, 5, -5, 0])
    if k % 512:
        return np.exp2(np.random.permutation(np.resize(levels, k // 32))).repeat(32)
    a = np.empty((k // 512, 16))
    for p in range(k // 512):
        a[p, :8] = np.random.permutation(np.resize(levels, 8))
        for g in range(8):
            far = levels[np.abs(levels - a[p, g]) >= 10]
            a[p, g + 8] = far[np.random.randint(len(far))]
    return np.exp2(a.ravel()).repeat(32)


def f64(x):
    return np.asarray(x).astype(np.float64)


def striped(idx):
    return np.tile(idx.reshape(-1, 16).T, (8, 1)).astype(np.uint16)


def unstriped(offs):
    return offs[:16].T.reshape(-1).astype(np.int64)


E2M1 = np.array([0.0, 0.5, 1.0, 1.5, 2.0, 3.0, 4.0, 6.0, -0.0, -0.5, -1.0, -1.5, -2.0, -3.0, -4.0, -6.0])


def pack_weight(w, fmt):
    k, n = w.shape
    w = f64(np.asarray(w, np.float32).astype(ml_dtypes.bfloat16)).reshape(k // 32, 32, n)
    amax = np.abs(w).max(1)
    if fmt == "e4m3":
        byte = np.frexp(amax)[1] - 1 + 127 - 7
    else:
        mant, ex = np.frexp(amax / 6.0)
        byte = np.where(mant > 0.5, ex, ex - 1) + 127
    byte = np.clip(np.where(amax > 0, byte, 1), 1, 254)
    scaled = (w * np.exp2(127.0 - byte)[:, None, :]).reshape(k, n).astype(np.float32)
    by_word = np.ascontiguousarray(scaled.reshape(k // 512, 128, 4, n).transpose(0, 1, 3, 2))
    if fmt == "e4m3":
        words = by_word.astype(ml_dtypes.float8_e4m3fn).view(np.uint8)
    else:
        c = by_word.astype(ml_dtypes.float4_e2m1fn).view(np.uint8) & 0xF
        words = (c[..., 0::2] | (c[..., 1::2] << 4)).reshape(k // 512, 128, 2 * n)
    return np.ascontiguousarray(words), np.ascontiguousarray(byte.astype(np.uint8).reshape(k // 512, 16, n))


def unpack_weight(words, scales, fmt):
    g, _, n = scales.shape
    words = np.ascontiguousarray(words).reshape(g, 128, n, -1)
    if fmt == "e4m3":
        vals = words.view(ml_dtypes.float8_e4m3fn).astype(np.float64)
    else:
        nib = np.empty((g, 128, n, 4), np.uint8)
        nib[..., 0::2] = words & 0xF
        nib[..., 1::2] = words >> 4
        vals = E2M1[nib]
    vals = vals * np.repeat(np.exp2(scales.astype(np.float64) - 127.0), 8, axis=1)[..., None]
    return vals.transpose(0, 1, 3, 2).reshape(g * 512, n)


def gelu(v):
    return 0.5 * v * (1.0 + np.tanh(np.sqrt(2.0 / np.pi) * (v + 0.044715 * v**3)))


def bf(x):
    return np.asarray(x, np.float32).astype(ml_dtypes.bfloat16)


def planes(Y):
    n, m = Y.shape
    b = f64(bf(Y)).reshape(n // 32, 32, m)
    amax = np.abs(b).max(1)
    byte = np.clip(np.where(amax > 0, np.frexp(amax)[1] - 1 + 127 - 7, 1), 1, 254)
    codes = (b * np.exp2(127.0 - byte)[:, None, :]).reshape(n, m).astype(np.float32).astype(ml_dtypes.float8_e4m3fn).view(np.uint8)
    words = codes.reshape(n // 512, 128, 4, m).transpose(0, 1, 3, 2)
    return np.ascontiguousarray(words), np.ascontiguousarray(byte.astype(np.uint8).reshape(n // 512, 16, m))


K, H, N, T, S, T2, P = 1024, 1024, 512, 2048, 1024, 2048, 1024

def setup_inputs():
    n = np.random.standard_normal
    s = mx_kscale(K)[:, None]
    u = mx_kscale(H)[:, None]
    tab_words, tab_scales = pack_weight(n((K, T)) * s, "e4m3")
    w1 = (n((K, H)) / np.sqrt(K) / s).astype(np.float32)
    w2_words, w2_scales = pack_weight(0.8 * n((K, H)) / np.sqrt(K) / s, "e2m1")
    beta = np.random.uniform(0.5, 1.5, H).astype(np.float32)
    wgs = np.exp(0.3 * n((128, S))).astype(np.float32)
    given = (n((H, P)) * u).astype(np.float32)
    w5_words, w5_scales = pack_weight(1.5 * n((H, N)) / np.sqrt(H) / u * np.exp(0.8 * n(N)), "e4m3")
    return {"tab_words": tab_words, "tab_scales": tab_scales,
            "offs": striped(np.random.permutation(T)[:S]),
            "offs2": striped(np.random.permutation(T2)[:S]),
            "offs3": striped(np.random.permutation(T2)[:P]),
            "w1": w1, "w2_words": w2_words, "w2_scales": w2_scales,
            "beta": beta, "wgs": wgs, "given": given,
            "w5_words": w5_words, "w5_scales": w5_scales}

def reference(tab_words, tab_scales, offs, offs2, offs3, w1, w2_words, w2_scales,
              beta, wgs, given, w5_words, w5_scales):
    v = unpack_weight(tab_words, tab_scales, "e4m3")[:, unstriped(offs)]
    w2 = unpack_weight(w2_words, w2_scales, "e2m1")
    w5 = unpack_weight(w5_words, w5_scales, "e4m3")
    a = mxq(f64(w1), 0, "e4m3").T @ v
    d = w2.T @ v
    h = a - f64(beta)[:, None] * d
    page = np.zeros((H, T2))
    page[:, unstriped(offs2)] = np.tile(f64(wgs), (H // 128, 1)) * h
    x = page[:, unstriped(offs3)]
    z = f64(given) / (1.0 + x * x)
    y = w5.T @ mxq(z, 0, "e4m3")
    words, scales = planes(y)
    return y, words, scales

@@ -1,0 +1,365 @@
+from contextlib import ExitStack
+
+import concourse.mybir as mybir
+
+K, H, N, T, S, T2, M = 1024, 1024, 512, 2048, 1024, 2048, 1024
+FLOPS = 2 * (2 * K * H * S + H * N * M)
+
+F32 = mybir.dt.float32
+BF16 = mybir.dt.bfloat16
+I32 = mybir.dt.int32
+U32 = mybir.dt.uint32
+U16 = mybir.dt.uint16
+U8 = mybir.dt.uint8
+FP8X4 = mybir.dt.float8_e4m3fn_x4
+FP4X4 = mybir.dt.float4_e2m1fn_x4
+ACT = mybir.ActivationFunctionType
+ALU = mybir.AluOpType
+
+P = 128
+HALF = 512
+QUARTER = 256
+TILES = 8
+AHEAD = 3
+ROOT = 75.0 / 64.0
+
+
+def tile_list_deflated_slots_kernel(
+    tc, tab_words, tab_scales, offs, offs2, offs3, w1, w2_words, w2_scales,
+    beta, wgs, given, w5_words, w5_scales, out_0, out_1, out_2,
+):
+    nc = tc.nc
+    with ExitStack() as ctx:
+        keep = ctx.enter_context(tc.tile_pool(name="keep", bufs=1))
+        big = ctx.enter_context(tc.tile_pool(name="big", bufs=6))
+        ring = ctx.enter_context(tc.tile_pool(name="ring", bufs=2))
+        psum = ctx.enter_context(tc.psum_pool(name="psum", bufs=8))
+
+        def kept(shape, dtype, name):
+            return keep.tile(shape, dtype, name=name, align_bytes=64)
+
+        idx = kept([P, S // 16], U16, "idx")
+        idx2 = kept([P, S // 16], U16, "idx2")
+        idx3 = kept([P, M // 16], U16, "idx3")
+
+        def load_scale_rows(plane, scales, row=0, col=0):
+            for q in range(4):
+                nc.sync.dma_start(
+                    out=plane[32 * q + row : 32 * q + row + 4, :, col : col + scales.shape[2]].bitcast(I32),
+                    in_=scales[:, 4 * q : 4 * q + 4, :].rearrange("a r c -> r a c").bitcast(I32),
+                )
+
+        tab_s = kept([P, T], U8, "tab_s")
+        v_s = kept([P, S], U8, "v_s")
+        v_s1 = kept([P, S], U8, "v_s1")
+        w_s_raw = kept([P, 2, H], U8, "w_s_raw")
+        nc.gpsimd.memset(tab_s[:].bitcast(I32), 0)
+        nc.gpsimd.memset(w_s_raw[:].bitcast(I32), 0)
+        nc.gpsimd.memset(v_s1[:].bitcast(I32), 0)
+        pages = [kept([P, T2], F32, "page%d" % i) for i in range(2)]
+        for page in pages:
+            nc.gpsimd.memset(page[:], 0.0)
+
+        tab_w = [kept([P, T], I32, "tab_w%d" % a) for a in range(2)]
+        w2_w_raw = [kept([P, 2, 2 * HALF], U8, "w2_w_raw%d" % b) for b in range(2)]
+        w1_raw = {}
+
+        def load_tab_words(a):
+            nc.sync.dma_start(out=tab_w[a][:], in_=tab_words[a].rearrange("p t i -> p (t i)").bitcast(I32))
+
+        def load_w2_words(b):
+            nc.sync.dma_start(
+                out=w2_w_raw[b][:].bitcast(I32),
+                in_=w2_words[:, :, 1024 * b : 1024 * (b + 1)].rearrange("a p c -> p a c").bitcast(I32),
+            )
+
+        def load_w1(b, a):
+            raw = big.tile([P, 4, HALF], F32, name="slot", align_bytes=64)
+            nc.sync.dma_start(
+                out=raw[:],
+                in_=w1[512 * a : 512 * (a + 1), 512 * b : 512 * (b + 1)].rearrange("(p i) c -> p i c", i=4),
+            )
+            w1_raw[(b, a)] = raw
+
+        beta_t = kept([P, 2, 4], F32, "beta_t")
+        wgs_first = kept([P, S], F32, "wgs_first")
+        wgs_rest = kept([P, 3, S], F32, "wgs_rest")
+        wgs_rows = wgs.rearrange("(p t) j -> p t j", t=4)
+
+        nc.sync.dma_start(idx[:], offs)
+        for q in range(4):
+            nc.sync.dma_start(
+                out=tab_s[32 * q : 32 * q + 8, :].bitcast(I32),
+                in_=tab_scales[:, 4 * q : 4 * q + 4, :].bitcast(I32),
+            )
+        nc.sync.dma_start(idx2[:], offs2)
+        nc.sync.dma_start(out=beta_t[:], in_=beta.rearrange("(b p t) -> p b t", b=2, t=4))
+        load_tab_words(0)
+        load_w1(0, 0)
+        load_w1(0, 1)
+        load_w2_words(0)
+        load_scale_rows(w_s_raw, w2_scales)
+        load_tab_words(1)
+        nc.vector.tensor_copy(v_s[:], tab_s[:].indirect(idx[:]))
+        for q in range(4):
+            nc.sync.dma_start(
+                out=v_s1[32 * q : 32 * q + 4, :].bitcast(I32),
+                in_=v_s[32 * q + 4 : 32 * q + 8, :].bitcast(I32),
+            )
+        for q in range(4):
+            nc.sync.dma_start(out=wgs_first[32 * q : 32 * (q + 1), :], in_=wgs_rows[:, 0, :])
+        load_w2_words(1)
+        load_scale_rows(w_s_raw, w5_scales, row=4, col=HALF)
+        nc.sync.dma_start(idx3[:], offs3)
+        for q in range(4):
+            nc.sync.dma_start(out=wgs_rest[32 * q : 32 * (q + 1), :, :], in_=wgs_rows[:, 1:4, :])
+        load_w1(1, 0)
+        load_w1(1, 1)
+
+        given_t = {}
+
+        def load_given(b):
+            for h in range(2):
+                g = big.tile([P, 4, HALF], F32, name="slot", align_bytes=64)
+                nc.sync.dma_start(
+                    out=g[:],
+                    in_=given[512 * b : 512 * (b + 1), HALF * h : HALF * (h + 1)].rearrange("(p t) m -> p t m", t=4),
+                )
+                given_t[(b, h)] = g
+
+        load_given(0)
+        w5_w_raw = kept([P, 2, N], I32, "w5_w_raw")
+        nc.sync.dma_start(out=w5_w_raw[:], in_=w5_words.rearrange("a p c i -> p a (c i)").bitcast(I32))
+
+        v_w = {(a, h): kept([P, HALF], U32, "v_w%d%d" % (a, h)) for a in range(2) for h in range(2)}
+
+        def gather_words(a, h):
+            nc.vector.tensor_copy(v_w[(a, h)][:], tab_w[a][:].bitcast(U32).indirect(idx[:, 32 * h : 32 * (h + 1)]))
+
+        w1_w = {
+            (b, a): ring.tile([P, HALF], U32, name="w1_w", tag="quad%d" % (2 * b + a), bufs=1, align_bytes=64)
+            for b in range(2) for a in range(2)
+        }
+        w1_s = {(b, a): kept([P, HALF], U8, "w1_s%d%d" % (b, a)) for b in range(2) for a in range(2)}
+        w2_w = [kept([P, 2, 2 * HALF], U8, "w2_w%d" % b) for b in range(2)]
+        w2_s = [kept([P, 2, HALF], U8, "w2_s%d" % b) for b in range(2)]
+        w1_bf = {}
+        w1_bf_late = ring.tile([P, 2, 4, P, 4], BF16, name="w1_bf_late", tag="late", bufs=1, align_bytes=64)
+
+        def round_w1(b, a):
+            if b == 0:
+                grouped = ring.tile([P, 4, P, 4], BF16, name="w1_bf", align_bytes=64)[:]
+            else:
+                grouped = w1_bf_late[:, a]
+            nc.scalar.copy(
+                out=grouped.rearrange("p t m i -> p m t i"),
+                in_=w1_raw[(b, a)][:].rearrange("p i (m t) -> p m t i", t=4),
+            )
+            w1_bf[(b, a)] = grouped
+
+        def quantise_w1(b, a):
+            nc.vector.quantize_mx(
+                out=w1_w[(b, a)][:].bitcast(FP8X4),
+                scales=w1_s[(b, a)][:],
+                in_=w1_bf[(b, a)].rearrange("p t m i -> p (t m i)"),
+            )
+
+        def deal_w2_words(b):
+            nc.vector.tensor_copy(
+                out=w2_w[b][:].bitcast(U16).rearrange("p a (t m) -> p a t m", t=4),
+                in_=w2_w_raw[b][:].bitcast(U16).rearrange("p a (m t) -> p a t m", t=4),
+            )
+
+        def deal_scales(b, engine):
+            engine.tensor_copy(
+                out=w2_s[b][:].rearrange("p a (t m) -> p a t m", t=4),
+                in_=w_s_raw[:, :, HALF * b : HALF * (b + 1)].rearrange("p a (m t) -> p a t m", t=4),
+            )
+
+        rows = [kept([P, 2, S], F32, "rows%d" % k) for k in range(TILES // 2)]
+
+        def first_stage(i, h):
+            b, t = divmod(i, 4)
+            cols = slice(P * t, P * (t + 1))
+            js = slice(HALF * h, HALF * (h + 1))
+            acc_a = psum.tile([P, HALF], F32, name="acc")
+            acc_d = psum.tile([P, HALF], F32, name="acc")
+            for a in range(2):
+                nc.tensor.matmul_mx(
+                    out=acc_a[:],
+                    lhsT=w1_w[(b, a)][:, cols].bitcast(FP8X4), lhsT_scale=w1_s[(b, a)][:, cols],
+                    rhs=v_w[(a, h)][:].bitcast(FP8X4), rhs_scale=v_s[4 * a :, js],
+                    start=(a == 0), stop=(a == 1),
+                )
+            for a in range(2):
+                nc.tensor.matmul_mx(
+                    out=acc_d[:],
+                    lhsT=w2_w[b][:, a, 2 * P * t : 2 * P * (t + 1)].bitcast(FP4X4),
+                    lhsT_scale=w2_s[b][:, a, cols],
+                    rhs=v_w[(a, h)][:].bitcast(FP8X4), rhs_scale=(v_s, v_s1)[a][:, js],
+                    start=(a == 0), stop=(a == 1),
+                )
+            d_sb = ring.tile([P, HALF], F32, name="d_sb", bufs=6)
+            hs = rows[i // 2][:, i % 2, js]
+            wg = wgs_first[:, js] if t == 0 else wgs_rest[:, t - 1, js]
+            nc.scalar.activation(out=d_sb[:], in_=acc_d[:], func=ACT.Copy, scale=beta_t[:, b, t : t + 1])
+            if i == 0:
+                nc.vector.tensor_tensor(hs, acc_a[:], d_sb[:], ALU.subtract)
+                nc.vector.tensor_tensor(hs, hs, wg, ALU.mult)
+            else:
+                nc.scalar.copy(out=hs, in_=acc_a[:])
+                nc.gpsimd.tensor_tensor(hs, hs, d_sb[:], ALU.subtract)
+                nc.gpsimd.tensor_tensor(hs, hs, wg, ALU.mult)
+
+        def scatter(i, pieces):
+            w = S // pieces
+            for k in range(pieces):
+                nc.vector.tensor_copy(
+                    pages[i % 2][:].indirect(idx2[:, k * w // 16 : (k + 1) * w // 16]),
+                    rows[i // 2][:, i % 2, k * w : (k + 1) * w],
+                )
+
+        z_parts = {0: 2, 1: 4}
+        z_bf = {(b, k): kept([P, M // z_parts[b], 4], BF16, "z_bf%d%d" % (b, k)) for b in range(2) for k in range(z_parts[b])}
+        z_w = {(b, k): kept([P, M // z_parts[b]], U32, "z_w%d%d" % (b, k)) for b in range(2) for k in range(z_parts[b])}
+        z_s = {(b, k): kept([P, M // z_parts[b]], U8, "z_s%d%d" % (b, k)) for b in range(2) for k in range(z_parts[b])}
+
+
+        def fetch(i, x, m0, w):
+            nc.vector.tensor_copy(x, pages[i % 2][:].indirect(idx3[:, m0 // 16 : (m0 + w) // 16]))
+            nc.scalar.activation(out=x, in_=x, func=ACT.Square)
+            nc.scalar.activation(out=x, in_=x, func=ACT.Abs_reciprocal_sqrt, scale=ROOT * ROOT, bias=ROOT * ROOT)
+            nc.scalar.activation(out=x, in_=x, func=ACT.Square, scale=ROOT)
+
+        def damp(pair, k, r):
+            b, u = divmod(pair, 2)
+            part = M // z_parts[b]
+            m = k * part
+            g = given_t[(b, m // HALF)][:, 2 * u : 2 * u + 2, m % HALF : m % HALF + part]
+            nc.gpsimd.tensor_tensor(
+                z_bf[(b, k)][:, :, 2 * u : 2 * u + 2], r.rearrange("p e m -> p m e"), g.rearrange("p e m -> p m e"), ALU.mult
+            )
+
+        def damp_single(t, q, r):
+            m = QUARTER * q
+            g = given_t[(1, m // HALF)][:, t, m % HALF : m % HALF + QUARTER]
+            nc.gpsimd.tensor_tensor(z_bf[(1, q)][:, :, t], r, g, ALU.mult)
+
+        def quantise_z(b, k):
+            nc.vector.quantize_mx(
+                out=z_w[(b, k)][:].bitcast(FP8X4), scales=z_s[(b, k)][:],
+                in_=z_bf[(b, k)][:].rearrange("p m t -> p (m t)"),
+            )
+
+        w5_w = kept([P, 2, N], I32, "w5_w")
+
+        def deal_w5():
+            nc.gpsimd.tensor_copy(
+                out=w5_w[:].rearrange("p a (t m) -> p a t m", t=4),
+                in_=w5_w_raw[:].rearrange("p a (m t) -> p a t m", t=4),
+            )
+
+        gather_words(0, 0)
+        round_w1(0, 0)
+        round_w1(0, 1)
+        deal_w2_words(0)
+        deal_scales(0, nc.vector)
+        quantise_w1(0, 0)
+        quantise_w1(0, 1)
+        gather_words(1, 0)
+        first_stage(0, 0)
+        gather_words(0, 1)
+        gather_words(1, 1)
+        deal_w2_words(1)
+        first_stage(0, 1)
+        for i in range(1, AHEAD):
+            first_stage(i, 0)
+            first_stage(i, 1)
+        deal_scales(1, nc.gpsimd)
+        round_w1(1, 0)
+        round_w1(1, 1)
+        quantise_w1(1, 0)
+        quantise_w1(1, 1)
+        load_given(1)
+
+        y_banks = {}
+
+        def last_stage(b, q):
+            for u in range(2):
+                if b == 0:
+                    y_banks[(q, u)] = psum.tile([P, 2, QUARTER], F32, name="acc")
+                part = M // z_parts[b]
+                k, c0 = divmod(QUARTER * q, part)
+                for e in range(2):
+                    cols = slice(P * (2 * u + e), P * (2 * u + e + 1))
+                    nc.tensor.matmul_mx(
+                        out=y_banks[(q, u)][:, e, :],
+                        lhsT=w5_w[:, b, cols].bitcast(FP8X4), lhsT_scale=w2_s[1][4:, b, cols],
+                        rhs=z_w[(b, k)][:, c0 : c0 + QUARTER].bitcast(FP8X4), rhs_scale=z_s[(b, k)][:, c0 : c0 + QUARTER],
+                        start=(b == 0 and e == 0), stop=(b == 1 and e == 1),
+                    )
+
+        for i in range(TILES):
+            if i + AHEAD < TILES:
+                first_stage(i + AHEAD, 0)
+                first_stage(i + AHEAD, 1)
+            scatter(i, 2 if i == 0 else 1)
+            if i < TILES - 2:
+                if i == 0:
+                    picked = ring.tile([P, 2, M], F32, name="picked", tag="late", bufs=1, align_bytes=64)
+                elif i % 2 == 0:
+                    picked = rows[i // 2]
+                fetch(i, picked[:, i % 2, :], 0, M)
+                if i % 2 == 1:
+                    parts = z_parts[i // 4]
+                    for k in range(parts):
+                        damp(i // 2, k, picked[:, :, k * M // parts : (k + 1) * M // parts])
+            if i == 1:
+                deal_w5()
+            if i == TILES - 2:
+                last_x = [
+                    ring.tile([P, 2, QUARTER], F32, name="last_x", tag="quad%d" % q, bufs=1, align_bytes=64)
+                    for q in range(4)
+                ]
+                for q in range(4):
+                    fetch(i, last_x[q][:, 0, :], QUARTER * q, QUARTER)
+                    damp_single(2, q, last_x[q][:, 0, :])
+                quantise_z(0, 0)
+                quantise_z(0, 1)
+        for q in range(4):
+            last_stage(0, q)
+
+        y_w = kept([P, M], I32, "y_w")
+        y_s = kept([P, M], U8, "y_s")
+        y_rows = out_0.rearrange("(p t) m -> p t m", t=4)
+        words_out = out_1[0].rearrange("p m t -> p (m t)").bitcast(I32)
+
+        def finish(q):
+            ms = slice(QUARTER * q, QUARTER * (q + 1))
+            y = big.tile([P, 4, QUARTER], F32, name="slot", align_bytes=64)
+            for u in range(2):
+                nc.scalar.copy(out=y[:, 2 * u : 2 * u + 2, :], in_=y_banks[(q, u)][:])
+            nc.sync.dma_start(out=y_rows[:, :, ms], in_=y[:])
+            y_bf = ring.tile([P, QUARTER, 4], BF16, name="y_bf", tag="w1_bf", align_bytes=64)
+            nc.vector.tensor_copy(
+                out=y_bf[:].rearrange("p (c i) t -> p c t i", i=4),
+                in_=y[:].rearrange("p t (c i) -> p c t i", i=4),
+            )
+            nc.vector.quantize_mx(
+                out=y_w[:, ms].bitcast(FP8X4), scales=y_s[:, ms], in_=y_bf[:].rearrange("p m t -> p (m t)")
+            )
+            if q >= 2:
+                done = slice(0, 3 * QUARTER) if q == 2 else ms
+                nc.sync.dma_start(out=words_out[:, done], in_=y_w[:, done])
+
+        for q in range(4):
+            fetch(TILES - 1, last_x[q][:, 1, :], QUARTER * q, QUARTER)
+            damp_single(3, q, last_x[q][:, 1, :])
+        for q in range(4):
+            quantise_z(1, q)
+            last_stage(1, q)
+            finish(q)
+        for q in range(4):
+            nc.sync.dma_start(
+                out=out_2[0, 4 * q : 4 * q + 4, :].bitcast(I32), in_=y_s[32 * q : 32 * q + 4, :].bitcast(I32)
+            )

@@ -21,6 +21,7 @@ HALF = 512
 QUARTER = 256
 TILES = 8
 AHEAD = 3
+SPLIT = 768
 ROOT = 75.0 / 64.0
 
 
@@ -42,20 +43,22 @@ def tile_list_deflated_slots_kernel(
         idx2 = kept([P, S // 16], U16, "idx2")
         idx3 = kept([P, M // 16], U16, "idx3")
 
-        def load_scale_rows(plane, scales, row=0, col=0):
+        def load_scale_rows(plane, scales):
             for q in range(4):
                 nc.sync.dma_start(
-                    out=plane[32 * q + row : 32 * q + row + 4, :, col : col + scales.shape[2]].bitcast(I32),
+                    out=plane[32 * q : 32 * q + 4, :, :].bitcast(I32),
                     in_=scales[:, 4 * q : 4 * q + 4, :].rearrange("a r c -> r a c").bitcast(I32),
                 )
 
-        tab_s = kept([P, T], U8, "tab_s")
-        v_s = kept([P, S], U8, "v_s")
-        v_s1 = kept([P, S], U8, "v_s1")
+        tab_s = kept([P, 2, T], U8, "tab_s")
+        v_s = [kept([P, S], U8, "v_s%d" % a) for a in range(2)]
         w_s_raw = kept([P, 2, H], U8, "w_s_raw")
-        nc.gpsimd.memset(tab_s[:].bitcast(I32), 0)
+        tab_s_words = tab_s[:].rearrange("p a t -> p (a t)").bitcast(I32)
+        nc.vector.memset(tab_s_words[:, :SPLIT], 0)
+        nc.gpsimd.memset(tab_s_words[:, SPLIT:], 0)
         nc.gpsimd.memset(w_s_raw[:].bitcast(I32), 0)
-        nc.gpsimd.memset(v_s1[:].bitcast(I32), 0)
+        w5_s_raw = kept([P, N], U8, "w5_s_raw")
+        nc.gpsimd.memset(w5_s_raw[:].bitcast(I32), 0)
         pages = [kept([P, T2], F32, "page%d" % i) for i in range(2)]
         for page in pages:
             nc.gpsimd.memset(page[:], 0.0)
@@ -82,39 +85,35 @@ def tile_list_deflated_slots_kernel(
             w1_raw[(b, a)] = raw
 
         beta_t = kept([P, 2, 4], F32, "beta_t")
-        wgs_first = kept([P, S], F32, "wgs_first")
-        wgs_rest = kept([P, 3, S], F32, "wgs_rest")
+        wgs_t = [kept([P, S], F32, "wgs%d" % t) for t in range(4)]
         wgs_rows = wgs.rearrange("(p t) j -> p t j", t=4)
 
+        def load_wgs(t):
+            for q in range(4):
+                nc.sync.dma_start(out=wgs_t[t][32 * q : 32 * (q + 1), :], in_=wgs_rows[:, t, :])
+
         nc.sync.dma_start(idx[:], offs)
-        for q in range(4):
-            nc.sync.dma_start(
-                out=tab_s[32 * q : 32 * q + 8, :].bitcast(I32),
-                in_=tab_scales[:, 4 * q : 4 * q + 4, :].bitcast(I32),
-            )
-        nc.sync.dma_start(idx2[:], offs2)
-        nc.sync.dma_start(out=beta_t[:], in_=beta.rearrange("(b p t) -> p b t", b=2, t=4))
         load_tab_words(0)
+        load_scale_rows(tab_s, tab_scales)
+        nc.sync.dma_start(out=beta_t[:], in_=beta.rearrange("(b p t) -> p b t", b=2, t=4))
         load_w1(0, 0)
         load_w1(0, 1)
         load_w2_words(0)
         load_scale_rows(w_s_raw, w2_scales)
         load_tab_words(1)
-        nc.vector.tensor_copy(v_s[:], tab_s[:].indirect(idx[:]))
-        for q in range(4):
-            nc.sync.dma_start(
-                out=v_s1[32 * q : 32 * q + 4, :].bitcast(I32),
-                in_=v_s[32 * q + 4 : 32 * q + 8, :].bitcast(I32),
-            )
-        for q in range(4):
-            nc.sync.dma_start(out=wgs_first[32 * q : 32 * (q + 1), :], in_=wgs_rows[:, 0, :])
         load_w2_words(1)
-        load_scale_rows(w_s_raw, w5_scales, row=4, col=HALF)
+        load_wgs(0)
+        nc.sync.dma_start(idx2[:], offs2)
+        load_wgs(1)
         nc.sync.dma_start(idx3[:], offs3)
-        for q in range(4):
-            nc.sync.dma_start(out=wgs_rest[32 * q : 32 * (q + 1), :, :], in_=wgs_rows[:, 1:4, :])
         load_w1(1, 0)
         load_w1(1, 1)
+        for q in range(4):
+            nc.sync.dma_start(
+                out=w5_s_raw[32 * q : 32 * q + 8, :].bitcast(I32),
+                in_=w5_scales[:, 4 * q : 4 * q + 4, :].bitcast(I32),
+            )
+        load_wgs(2)
 
         given_t = {}
 
@@ -127,41 +126,38 @@ def tile_list_deflated_slots_kernel(
                 )
                 given_t[(b, h)] = g
 
+        load_wgs(3)
         load_given(0)
-        w5_w_raw = kept([P, 2, N], I32, "w5_w_raw")
-        nc.sync.dma_start(out=w5_w_raw[:], in_=w5_words.rearrange("a p c i -> p a (c i)").bitcast(I32))
 
         v_w = {(a, h): kept([P, HALF], U32, "v_w%d%d" % (a, h)) for a in range(2) for h in range(2)}
 
         def gather_words(a, h):
             nc.vector.tensor_copy(v_w[(a, h)][:], tab_w[a][:].bitcast(U32).indirect(idx[:, 32 * h : 32 * (h + 1)]))
 
-        w1_w = {
-            (b, a): ring.tile([P, HALF], U32, name="w1_w", tag="quad%d" % (2 * b + a), bufs=1, align_bytes=64)
-            for b in range(2) for a in range(2)
-        }
-        w1_s = {(b, a): kept([P, HALF], U8, "w1_s%d%d" % (b, a)) for b in range(2) for a in range(2)}
+        w1_w = [kept([P, 2 * HALF], U32, "w1_w%d" % b) for b in range(2)]
+        w1_s = [kept([P, 2 * HALF], U8, "w1_s%d" % b) for b in range(2)]
         w2_w = [kept([P, 2, 2 * HALF], U8, "w2_w%d" % b) for b in range(2)]
-        w2_s = [kept([P, 2, HALF], U8, "w2_s%d" % b) for b in range(2)]
+        w2_s = {0: kept([P, 2, HALF], U8, "w2_s0")}
         w1_bf = {}
-        w1_bf_late = ring.tile([P, 2, 4, P, 4], BF16, name="w1_bf_late", tag="late", bufs=1, align_bytes=64)
+        dealt = {}
 
         def round_w1(b, a):
             if b == 0:
                 grouped = ring.tile([P, 4, P, 4], BF16, name="w1_bf", align_bytes=64)[:]
             else:
-                grouped = w1_bf_late[:, a]
+                grouped = w1_bf["late"][:, a]
             nc.scalar.copy(
                 out=grouped.rearrange("p t m i -> p m t i"),
                 in_=w1_raw[(b, a)][:].rearrange("p i (m t) -> p m t i", t=4),
             )
             w1_bf[(b, a)] = grouped
 
-        def quantise_w1(b, a):
+        def quantise_w1(a):
+            cs = slice(HALF * a, HALF * (a + 1))
             nc.vector.quantize_mx(
-                out=w1_w[(b, a)][:].bitcast(FP8X4),
-                scales=w1_s[(b, a)][:],
-                in_=w1_bf[(b, a)].rearrange("p t m i -> p (t m i)"),
+                out=w1_w[0][:, cs].bitcast(FP8X4),
+                scales=w1_s[0][:, cs],
+                in_=w1_bf[(0, a)].rearrange("p t m i -> p (t m i)"),
             )
 
         def deal_w2_words(b):
@@ -187,8 +183,9 @@ def tile_list_deflated_slots_kernel(
             for a in range(2):
                 nc.tensor.matmul_mx(
                     out=acc_a[:],
-                    lhsT=w1_w[(b, a)][:, cols].bitcast(FP8X4), lhsT_scale=w1_s[(b, a)][:, cols],
-                    rhs=v_w[(a, h)][:].bitcast(FP8X4), rhs_scale=v_s[4 * a :, js],
+                    lhsT=w1_w[b][:, HALF * a + P * t : HALF * a + P * (t + 1)].bitcast(FP8X4),
+                    lhsT_scale=w1_s[b][:, HALF * a + P * t : HALF * a + P * (t + 1)],
+                    rhs=v_w[(a, h)][:].bitcast(FP8X4), rhs_scale=v_s[a][:, js],
                     start=(a == 0), stop=(a == 1),
                 )
             for a in range(2):
@@ -196,12 +193,19 @@ def tile_list_deflated_slots_kernel(
                     out=acc_d[:],
                     lhsT=w2_w[b][:, a, 2 * P * t : 2 * P * (t + 1)].bitcast(FP4X4),
                     lhsT_scale=w2_s[b][:, a, cols],
-                    rhs=v_w[(a, h)][:].bitcast(FP8X4), rhs_scale=(v_s, v_s1)[a][:, js],
+                    rhs=v_w[(a, h)][:].bitcast(FP8X4), rhs_scale=v_s[a][:, js],
                     start=(a == 0), stop=(a == 1),
                 )
-            d_sb = ring.tile([P, HALF], F32, name="d_sb", bufs=6)
+            if (i, h) == (1, 1):
+                d_sb = ring.tile([P, HALF], F32, name="d_sb", tag="late", bufs=1, align_bytes=64)
+            elif (i, h) == (2, 0):
+                d_sb = ring.tile([P, HALF], F32, name="d_sb", tag="w2_s1", bufs=1, align_bytes=64)
+            elif (i, h) == (3, 1):
+                d_sb = ring.tile([P, HALF], F32, name="d_sb", tag="w5_s", bufs=1, align_bytes=64)
+            else:
+                d_sb = ring.tile([P, HALF], F32, name="d_sb", bufs=6)
             hs = rows[i // 2][:, i % 2, js]
-            wg = wgs_first[:, js] if t == 0 else wgs_rest[:, t - 1, js]
+            wg = wgs_t[t][:, js]
             nc.scalar.activation(out=d_sb[:], in_=acc_d[:], func=ACT.Copy, scale=beta_t[:, b, t : t + 1])
             if i == 0:
                 nc.vector.tensor_tensor(hs, acc_a[:], d_sb[:], ALU.subtract)
@@ -211,15 +215,10 @@ def tile_list_deflated_slots_kernel(
                 nc.gpsimd.tensor_tensor(hs, hs, d_sb[:], ALU.subtract)
                 nc.gpsimd.tensor_tensor(hs, hs, wg, ALU.mult)
 
-        def scatter(i, pieces):
-            w = S // pieces
-            for k in range(pieces):
-                nc.vector.tensor_copy(
-                    pages[i % 2][:].indirect(idx2[:, k * w // 16 : (k + 1) * w // 16]),
-                    rows[i // 2][:, i % 2, k * w : (k + 1) * w],
-                )
+        def scatter(i):
+            nc.vector.tensor_copy(pages[i % 2][:].indirect(idx2[:]), rows[i // 2][:, i % 2, :])
 
-        z_parts = {0: 2, 1: 4}
+        z_parts = {0: 1, 1: 4}
         z_bf = {(b, k): kept([P, M // z_parts[b], 4], BF16, "z_bf%d%d" % (b, k)) for b in range(2) for k in range(z_parts[b])}
         z_w = {(b, k): kept([P, M // z_parts[b]], U32, "z_w%d%d" % (b, k)) for b in range(2) for k in range(z_parts[b])}
         z_s = {(b, k): kept([P, M // z_parts[b]], U8, "z_s%d%d" % (b, k)) for b in range(2) for k in range(z_parts[b])}
@@ -227,17 +226,22 @@ def tile_list_deflated_slots_kernel(
 
         def fetch(i, x, m0, w):
             nc.vector.tensor_copy(x, pages[i % 2][:].indirect(idx3[:, m0 // 16 : (m0 + w) // 16]))
-            nc.scalar.activation(out=x, in_=x, func=ACT.Square)
-            nc.scalar.activation(out=x, in_=x, func=ACT.Abs_reciprocal_sqrt, scale=ROOT * ROOT, bias=ROOT * ROOT)
-            nc.scalar.activation(out=x, in_=x, func=ACT.Square, scale=ROOT)
 
-        def damp(pair, k, r):
+        def invert(parts):
+            for x in parts:
+                nc.scalar.activation(out=x, in_=x, func=ACT.Square)
+            for x in parts:
+                nc.scalar.activation(out=x, in_=x, func=ACT.Abs_reciprocal_sqrt, scale=ROOT * ROOT, bias=ROOT * ROOT)
+            for x in parts:
+                nc.scalar.activation(out=x, in_=x, func=ACT.Square, scale=ROOT)
+
+        def damp(pair, q, r):
             b, u = divmod(pair, 2)
-            part = M // z_parts[b]
-            m = k * part
-            g = given_t[(b, m // HALF)][:, 2 * u : 2 * u + 2, m % HALF : m % HALF + part]
+            m = q * QUARTER
+            g = given_t[(b, m // HALF)][:, 2 * u : 2 * u + 2, m % HALF : m % HALF + QUARTER]
+            z = z_bf[(0, 0)][:, m : m + QUARTER, :] if b == 0 else z_bf[(1, q)][:]
             nc.gpsimd.tensor_tensor(
-                z_bf[(b, k)][:, :, 2 * u : 2 * u + 2], r.rearrange("p e m -> p m e"), g.rearrange("p e m -> p m e"), ALU.mult
+                z[:, :, 2 * u : 2 * u + 2], r.rearrange("p e m -> p m e"), g.rearrange("p e m -> p m e"), ALU.mult
             )
 
         def damp_single(t, q, r):
@@ -254,18 +258,25 @@ def tile_list_deflated_slots_kernel(
         w5_w = kept([P, 2, N], I32, "w5_w")
 
         def deal_w5():
+            w5_s = ring.tile([P, N], U8, name="w5_s", tag="w5_s", bufs=1, align_bytes=64)
+            dealt["w5_s"] = w5_s
+            nc.gpsimd.tensor_copy(
+                out=w5_s[:].rearrange("p (t m) -> p t m", t=4), in_=w5_s_raw[:].rearrange("p (m t) -> p t m", t=4)
+            )
             nc.gpsimd.tensor_copy(
                 out=w5_w[:].rearrange("p a (t m) -> p a t m", t=4),
                 in_=w5_w_raw[:].rearrange("p a (m t) -> p a t m", t=4),
             )
 
         gather_words(0, 0)
+        for a in range(2):
+            nc.vector.tensor_copy(v_s[a][:], tab_s[:, a, :].indirect(idx[:]))
         round_w1(0, 0)
         round_w1(0, 1)
         deal_w2_words(0)
         deal_scales(0, nc.vector)
-        quantise_w1(0, 0)
-        quantise_w1(0, 1)
+        quantise_w1(0)
+        quantise_w1(1)
         gather_words(1, 0)
         first_stage(0, 0)
         gather_words(0, 1)
@@ -275,12 +286,17 @@ def tile_list_deflated_slots_kernel(
         for i in range(1, AHEAD):
             first_stage(i, 0)
             first_stage(i, 1)
+        w2_s[1] = ring.tile([P, 2, HALF], U8, name="w2_s1", tag="w2_s1", bufs=1, align_bytes=64)
         deal_scales(1, nc.gpsimd)
+        w1_bf["late"] = ring.tile([P, 2, 4, P, 4], BF16, name="w1_bf_late", tag="late", bufs=1, align_bytes=64)
         round_w1(1, 0)
         round_w1(1, 1)
-        quantise_w1(1, 0)
-        quantise_w1(1, 1)
+        nc.vector.quantize_mx(
+            out=w1_w[1][:].bitcast(FP8X4), scales=w1_s[1][:], in_=w1_bf["late"][:].rearrange("p a t m i -> p (a t m i)")
+        )
         load_given(1)
+        w5_w_raw = big.tile([P, 2, N], I32, name="slot", align_bytes=64)
+        nc.sync.dma_start(out=w5_w_raw[:], in_=w5_words.rearrange("a p c i -> p a (c i)").bitcast(I32))
 
         y_banks = {}
 
@@ -294,7 +310,7 @@ def tile_list_deflated_slots_kernel(
                     cols = slice(P * (2 * u + e), P * (2 * u + e + 1))
                     nc.tensor.matmul_mx(
                         out=y_banks[(q, u)][:, e, :],
-                        lhsT=w5_w[:, b, cols].bitcast(FP8X4), lhsT_scale=w2_s[1][4:, b, cols],
+                        lhsT=w5_w[:, b, cols].bitcast(FP8X4), lhsT_scale=dealt["w5_s"][4 * b :, cols],
                         rhs=z_w[(b, k)][:, c0 : c0 + QUARTER].bitcast(FP8X4), rhs_scale=z_s[(b, k)][:, c0 : c0 + QUARTER],
                         start=(b == 0 and e == 0), stop=(b == 1 and e == 1),
                     )
@@ -303,29 +319,25 @@ def tile_list_deflated_slots_kernel(
             if i + AHEAD < TILES:
                 first_stage(i + AHEAD, 0)
                 first_stage(i + AHEAD, 1)
-            scatter(i, 2 if i == 0 else 1)
+            scatter(i)
             if i < TILES - 2:
                 if i == 0:
                     picked = ring.tile([P, 2, M], F32, name="picked", tag="late", bufs=1, align_bytes=64)
                 elif i % 2 == 0:
                     picked = rows[i // 2]
                 fetch(i, picked[:, i % 2, :], 0, M)
+                invert([picked[:, i % 2, HALF * h : HALF * (h + 1)] for h in range(2)])
                 if i % 2 == 1:
-                    parts = z_parts[i // 4]
-                    for k in range(parts):
-                        damp(i // 2, k, picked[:, :, k * M // parts : (k + 1) * M // parts])
+                    for q in range(4):
+                        damp(i // 2, q, picked[:, :, q * QUARTER : (q + 1) * QUARTER])
             if i == 1:
                 deal_w5()
             if i == TILES - 2:
-                last_x = [
-                    ring.tile([P, 2, QUARTER], F32, name="last_x", tag="quad%d" % q, bufs=1, align_bytes=64)
-                    for q in range(4)
-                ]
+                fetch(i, rows[3][:, 0, :], 0, M)
+                invert([rows[3][:, 0, HALF * h : HALF * (h + 1)] for h in range(2)])
                 for q in range(4):
-                    fetch(i, last_x[q][:, 0, :], QUARTER * q, QUARTER)
-                    damp_single(2, q, last_x[q][:, 0, :])
+                    damp_single(2, q, rows[3][:, 0, QUARTER * q : QUARTER * (q + 1)])
                 quantise_z(0, 0)
-                quantise_z(0, 1)
         for q in range(4):
             last_stage(0, q)
 
@@ -339,7 +351,7 @@ def tile_list_deflated_slots_kernel(
             y = big.tile([P, 4, QUARTER], F32, name="slot", align_bytes=64)
             for u in range(2):
                 nc.scalar.copy(out=y[:, 2 * u : 2 * u + 2, :], in_=y_banks[(q, u)][:])
-            nc.sync.dma_start(out=y_rows[:, :, ms], in_=y[:])
+                nc.sync.dma_start(out=y_rows[:, 2 * u : 2 * u + 2, ms], in_=y[:, 2 * u : 2 * u + 2, :])
             y_bf = ring.tile([P, QUARTER, 4], BF16, name="y_bf", tag="w1_bf", align_bytes=64)
             nc.vector.tensor_copy(
                 out=y_bf[:].rearrange("p (c i) t -> p c t i", i=4),
@@ -352,9 +364,13 @@ def tile_list_deflated_slots_kernel(
                 done = slice(0, 3 * QUARTER) if q == 2 else ms
                 nc.sync.dma_start(out=words_out[:, done], in_=y_w[:, done])
 
+        last_x = [rows[3][:, 1, QUARTER * q : QUARTER * (q + 1)] for q in range(4)]
         for q in range(4):
-            fetch(TILES - 1, last_x[q][:, 1, :], QUARTER * q, QUARTER)
-            damp_single(3, q, last_x[q][:, 1, :])
+            fetch(TILES - 1, last_x[q], QUARTER * q, QUARTER)
+        for h in range(2):
+            invert(last_x[2 * h : 2 * h + 2])
+            for q in range(2 * h, 2 * h + 2):
+                damp_single(3, q, last_x[q])
         for q in range(4):
             quantise_z(1, q)
             last_stage(1, q)

@@ -21,7 +21,6 @@ HALF = 512
 QUARTER = 256
 TILES = 8
 AHEAD = 3
-SPLIT = 768
 ROOT = 75.0 / 64.0
 
 
@@ -43,25 +42,23 @@ def tile_list_deflated_slots_kernel(
         idx2 = kept([P, S // 16], U16, "idx2")
         idx3 = kept([P, M // 16], U16, "idx3")
 
-        def load_scale_rows(plane, scales):
+        def load_scale_rows(plane, scales, row=0):
             for q in range(4):
                 nc.sync.dma_start(
-                    out=plane[32 * q : 32 * q + 4, :, :].bitcast(I32),
+                    out=plane[32 * q + row : 32 * q + row + 4, :, :].bitcast(I32),
                     in_=scales[:, 4 * q : 4 * q + 4, :].rearrange("a r c -> r a c").bitcast(I32),
                 )
 
         tab_s = kept([P, 2, T], U8, "tab_s")
         v_s = [kept([P, S], U8, "v_s%d" % a) for a in range(2)]
-        w_s_raw = kept([P, 2, H], U8, "w_s_raw")
-        tab_s_words = tab_s[:].rearrange("p a t -> p (a t)").bitcast(I32)
-        nc.vector.memset(tab_s_words[:, :SPLIT], 0)
-        nc.gpsimd.memset(tab_s_words[:, SPLIT:], 0)
-        nc.gpsimd.memset(w_s_raw[:].bitcast(I32), 0)
-        w5_s_raw = kept([P, N], U8, "w5_s_raw")
-        nc.gpsimd.memset(w5_s_raw[:].bitcast(I32), 0)
+        w_s_raw = [kept([P, 2, HALF], U8, "w_s_raw%d" % b) for b in range(2)]
+        nc.vector.memset(tab_s[:, 0, :].bitcast(I32), 0)
+        nc.gpsimd.memset(tab_s[:, 1, :].bitcast(I32), 0)
+        for raw in w_s_raw:
+            nc.vector.memset(raw[:].bitcast(I32), 0)
         pages = [kept([P, T2], F32, "page%d" % i) for i in range(2)]
         for page in pages:
-            nc.gpsimd.memset(page[:], 0.0)
+            nc.vector.memset(page[:], 0.0)
 
         tab_w = [kept([P, T], I32, "tab_w%d" % a) for a in range(2)]
         w2_w_raw = [kept([P, 2, 2 * HALF], U8, "w2_w_raw%d" % b) for b in range(2)]
@@ -99,20 +96,17 @@ def tile_list_deflated_slots_kernel(
         load_w1(0, 0)
         load_w1(0, 1)
         load_w2_words(0)
-        load_scale_rows(w_s_raw, w2_scales)
+        load_scale_rows(w_s_raw[0], w2_scales[:, :, :HALF])
         load_tab_words(1)
         load_w2_words(1)
+        load_scale_rows(w_s_raw[1], w2_scales[:, :, HALF:])
+        load_scale_rows(w_s_raw[1], w5_scales, row=4)
         load_wgs(0)
         nc.sync.dma_start(idx2[:], offs2)
         load_wgs(1)
         nc.sync.dma_start(idx3[:], offs3)
         load_w1(1, 0)
         load_w1(1, 1)
-        for q in range(4):
-            nc.sync.dma_start(
-                out=w5_s_raw[32 * q : 32 * q + 8, :].bitcast(I32),
-                in_=w5_scales[:, 4 * q : 4 * q + 4, :].bitcast(I32),
-            )
         load_wgs(2)
 
         given_t = {}
@@ -137,7 +131,7 @@ def tile_list_deflated_slots_kernel(
         w1_w = [kept([P, 2 * HALF], U32, "w1_w%d" % b) for b in range(2)]
         w1_s = [kept([P, 2 * HALF], U8, "w1_s%d" % b) for b in range(2)]
         w2_w = [kept([P, 2, 2 * HALF], U8, "w2_w%d" % b) for b in range(2)]
-        w2_s = {0: kept([P, 2, HALF], U8, "w2_s0")}
+        w2_s = [kept([P, 2, HALF], U8, "w2_s%d" % b) for b in range(2)]
         w1_bf = {}
         dealt = {}
 
@@ -166,15 +160,15 @@ def tile_list_deflated_slots_kernel(
                 in_=w2_w_raw[b][:].bitcast(U16).rearrange("p a (m t) -> p a t m", t=4),
             )
 
-        def deal_scales(b, engine):
-            engine.tensor_copy(
+        def deal_scales(b):
+            nc.vector.tensor_copy(
                 out=w2_s[b][:].rearrange("p a (t m) -> p a t m", t=4),
-                in_=w_s_raw[:, :, HALF * b : HALF * (b + 1)].rearrange("p a (m t) -> p a t m", t=4),
+                in_=w_s_raw[b][:].rearrange("p a (m t) -> p a t m", t=4),
             )
 
         rows = [kept([P, 2, S], F32, "rows%d" % k) for k in range(TILES // 2)]
 
-        def first_stage(i, h):
+        def first_stage(i, h, d_sb):
             b, t = divmod(i, 4)
             cols = slice(P * t, P * (t + 1))
             js = slice(HALF * h, HALF * (h + 1))
@@ -196,29 +190,31 @@ def tile_list_deflated_slots_kernel(
                     rhs=v_w[(a, h)][:].bitcast(FP8X4), rhs_scale=v_s[a][:, js],
                     start=(a == 0), stop=(a == 1),
                 )
-            if (i, h) == (1, 1):
-                d_sb = ring.tile([P, HALF], F32, name="d_sb", tag="late", bufs=1, align_bytes=64)
-            elif (i, h) == (2, 0):
-                d_sb = ring.tile([P, HALF], F32, name="d_sb", tag="w2_s1", bufs=1, align_bytes=64)
-            elif (i, h) == (3, 1):
-                d_sb = ring.tile([P, HALF], F32, name="d_sb", tag="w5_s", bufs=1, align_bytes=64)
-            else:
-                d_sb = ring.tile([P, HALF], F32, name="d_sb", bufs=6)
             hs = rows[i // 2][:, i % 2, js]
-            wg = wgs_t[t][:, js]
-            nc.scalar.activation(out=d_sb[:], in_=acc_d[:], func=ACT.Copy, scale=beta_t[:, b, t : t + 1])
+            nc.scalar.activation(out=d_sb[:, js], in_=acc_d[:], func=ACT.Copy, scale=beta_t[:, b, t : t + 1])
             if i == 0:
-                nc.vector.tensor_tensor(hs, acc_a[:], d_sb[:], ALU.subtract)
-                nc.vector.tensor_tensor(hs, hs, wg, ALU.mult)
+                nc.vector.tensor_tensor(hs, acc_a[:], d_sb[:, js], ALU.subtract)
+                nc.vector.tensor_tensor(hs, hs, wgs_t[t][:, js], ALU.mult)
             else:
                 nc.scalar.copy(out=hs, in_=acc_a[:])
-                nc.gpsimd.tensor_tensor(hs, hs, d_sb[:], ALU.subtract)
-                nc.gpsimd.tensor_tensor(hs, hs, wg, ALU.mult)
+
+        def make_rows(i):
+            if i == 1:
+                d_sb = ring.tile([P, S], F32, name="d_sb", tag="late", bufs=1, align_bytes=64)
+            elif i == 5:
+                d_sb = ring.tile([P, S], F32, name="d_sb", tag="w5_w", bufs=1, align_bytes=64)
+            else:
+                d_sb = ring.tile([P, S], F32, name="d_sb", bufs=3)
+            for h in range(2):
+                first_stage(i, h, d_sb)
+            hs = rows[i // 2][:, i % 2, :]
+            nc.gpsimd.tensor_tensor(hs, hs, d_sb[:], ALU.subtract)
+            nc.gpsimd.tensor_tensor(hs, hs, wgs_t[i % 4][:], ALU.mult)
 
         def scatter(i):
             nc.vector.tensor_copy(pages[i % 2][:].indirect(idx2[:]), rows[i // 2][:, i % 2, :])
 
-        z_parts = {0: 1, 1: 4}
+        z_parts = {0: 2, 1: 4}
         z_bf = {(b, k): kept([P, M // z_parts[b], 4], BF16, "z_bf%d%d" % (b, k)) for b in range(2) for k in range(z_parts[b])}
         z_w = {(b, k): kept([P, M // z_parts[b]], U32, "z_w%d%d" % (b, k)) for b in range(2) for k in range(z_parts[b])}
         z_s = {(b, k): kept([P, M // z_parts[b]], U8, "z_s%d%d" % (b, k)) for b in range(2) for k in range(z_parts[b])}
@@ -235,13 +231,13 @@ def tile_list_deflated_slots_kernel(
             for x in parts:
                 nc.scalar.activation(out=x, in_=x, func=ACT.Square, scale=ROOT)
 
-        def damp(pair, q, r):
+        def damp(pair, k, r):
             b, u = divmod(pair, 2)
-            m = q * QUARTER
-            g = given_t[(b, m // HALF)][:, 2 * u : 2 * u + 2, m % HALF : m % HALF + QUARTER]
-            z = z_bf[(0, 0)][:, m : m + QUARTER, :] if b == 0 else z_bf[(1, q)][:]
+            part = M // z_parts[b]
+            m = k * part
+            g = given_t[(b, m // HALF)][:, 2 * u : 2 * u + 2, m % HALF : m % HALF + part]
             nc.gpsimd.tensor_tensor(
-                z[:, :, 2 * u : 2 * u + 2], r.rearrange("p e m -> p m e"), g.rearrange("p e m -> p m e"), ALU.mult
+                z_bf[(b, k)][:, :, 2 * u : 2 * u + 2], r.rearrange("p e m -> p m e"), g.rearrange("p e m -> p m e"), ALU.mult
             )
 
         def damp_single(t, q, r):
@@ -255,14 +251,9 @@ def tile_list_deflated_slots_kernel(
                 in_=z_bf[(b, k)][:].rearrange("p m t -> p (m t)"),
             )
 
-        w5_w = kept([P, 2, N], I32, "w5_w")
-
         def deal_w5():
-            w5_s = ring.tile([P, N], U8, name="w5_s", tag="w5_s", bufs=1, align_bytes=64)
-            dealt["w5_s"] = w5_s
-            nc.gpsimd.tensor_copy(
-                out=w5_s[:].rearrange("p (t m) -> p t m", t=4), in_=w5_s_raw[:].rearrange("p (m t) -> p t m", t=4)
-            )
+            w5_w = ring.tile([P, 2, N], I32, name="w5_w", tag="w5_w", bufs=1, align_bytes=64)
+            dealt["w5_w"] = w5_w
             nc.gpsimd.tensor_copy(
                 out=w5_w[:].rearrange("p a (t m) -> p a t m", t=4),
                 in_=w5_w_raw[:].rearrange("p a (m t) -> p a t m", t=4),
@@ -274,20 +265,19 @@ def tile_list_deflated_slots_kernel(
         round_w1(0, 0)
         round_w1(0, 1)
         deal_w2_words(0)
-        deal_scales(0, nc.vector)
+        deal_scales(0)
         quantise_w1(0)
         quantise_w1(1)
         gather_words(1, 0)
-        first_stage(0, 0)
+        d_first = ring.tile([P, S], F32, name="d_sb", bufs=3)
+        first_stage(0, 0, d_first)
         gather_words(0, 1)
         gather_words(1, 1)
         deal_w2_words(1)
-        first_stage(0, 1)
+        deal_scales(1)
+        first_stage(0, 1, d_first)
         for i in range(1, AHEAD):
-            first_stage(i, 0)
-            first_stage(i, 1)
-        w2_s[1] = ring.tile([P, 2, HALF], U8, name="w2_s1", tag="w2_s1", bufs=1, align_bytes=64)
-        deal_scales(1, nc.gpsimd)
+            make_rows(i)
         w1_bf["late"] = ring.tile([P, 2, 4, P, 4], BF16, name="w1_bf_late", tag="late", bufs=1, align_bytes=64)
         round_w1(1, 0)
         round_w1(1, 1)
@@ -310,15 +300,14 @@ def tile_list_deflated_slots_kernel(
                     cols = slice(P * (2 * u + e), P * (2 * u + e + 1))
                     nc.tensor.matmul_mx(
                         out=y_banks[(q, u)][:, e, :],
-                        lhsT=w5_w[:, b, cols].bitcast(FP8X4), lhsT_scale=dealt["w5_s"][4 * b :, cols],
+                        lhsT=dealt["w5_w"][:, b, cols].bitcast(FP8X4), lhsT_scale=w2_s[1][4:, b, cols],
                         rhs=z_w[(b, k)][:, c0 : c0 + QUARTER].bitcast(FP8X4), rhs_scale=z_s[(b, k)][:, c0 : c0 + QUARTER],
                         start=(b == 0 and e == 0), stop=(b == 1 and e == 1),
                     )
 
         for i in range(TILES):
             if i + AHEAD < TILES:
-                first_stage(i + AHEAD, 0)
-                first_stage(i + AHEAD, 1)
+                make_rows(i + AHEAD)
             scatter(i)
             if i < TILES - 2:
                 if i == 0:
@@ -328,9 +317,10 @@ def tile_list_deflated_slots_kernel(
                 fetch(i, picked[:, i % 2, :], 0, M)
                 invert([picked[:, i % 2, HALF * h : HALF * (h + 1)] for h in range(2)])
                 if i % 2 == 1:
-                    for q in range(4):
-                        damp(i // 2, q, picked[:, :, q * QUARTER : (q + 1) * QUARTER])
-            if i == 1:
+                    parts = z_parts[i // 4]
+                    for k in range(parts):
+                        damp(i // 2, k, picked[:, :, k * M // parts : (k + 1) * M // parts])
+            if i == 3:
                 deal_w5()
             if i == TILES - 2:
                 fetch(i, rows[3][:, 0, :], 0, M)
@@ -338,6 +328,7 @@ def tile_list_deflated_slots_kernel(
                 for q in range(4):
                     damp_single(2, q, rows[3][:, 0, QUARTER * q : QUARTER * (q + 1)])
                 quantise_z(0, 0)
+                quantise_z(0, 1)
         for q in range(4):
             last_stage(0, q)
 

@@ -20,7 +20,6 @@ P = 128
 HALF = 512
 QUARTER = 256
 TILES = 8
-AHEAD = 3
 ROOT = 75.0 / 64.0
 
 
@@ -33,6 +32,7 @@ def tile_list_deflated_slots_kernel(
         keep = ctx.enter_context(tc.tile_pool(name="keep", bufs=1))
         big = ctx.enter_context(tc.tile_pool(name="big", bufs=6))
         ring = ctx.enter_context(tc.tile_pool(name="ring", bufs=2))
+        late = ctx.enter_context(tc.tile_pool(name="late", bufs=1))
         psum = ctx.enter_context(tc.psum_pool(name="psum", bufs=8))
 
         def kept(shape, dtype, name):
@@ -49,19 +49,21 @@ def tile_list_deflated_slots_kernel(
                     in_=scales[:, 4 * q : 4 * q + 4, :].rearrange("a r c -> r a c").bitcast(I32),
                 )
 
-        tab_s = kept([P, 2, T], U8, "tab_s")
-        v_s = [kept([P, S], U8, "v_s%d" % a) for a in range(2)]
-        w_s_raw = [kept([P, 2, HALF], U8, "w_s_raw%d" % b) for b in range(2)]
-        nc.vector.memset(tab_s[:, 0, :].bitcast(I32), 0)
-        nc.gpsimd.memset(tab_s[:, 1, :].bitcast(I32), 0)
-        for raw in w_s_raw:
-            nc.vector.memset(raw[:].bitcast(I32), 0)
-        pages = [kept([P, T2], F32, "page%d" % i) for i in range(2)]
+        tab_s = kept([P, T], U8, "tab_s")
+        v_s = kept([P, S], U8, "v_s")
+        v_s_second = kept([P, S], U8, "v_s_second")
+        w_s_raw = [kept([P, 2, HALF], U8, "w_s_raw0"), late.tile([P, 2, HALF], U8, name="w_s_raw1", offset=8192, align_bytes=64)]
+        nc.vector.memset(tab_s[:, : T // 2].bitcast(I32), 0)
+        nc.gpsimd.memset(tab_s[:, T // 2 :].bitcast(I32), 0)
+        nc.gpsimd.memset(w_s_raw[0][:].bitcast(I32), 0)
+        nc.gpsimd.memset(v_s_second[:].bitcast(I32), 0)
+        nc.gpsimd.memset(w_s_raw[1][:].bitcast(I32), 0)
+        pages = [kept([P, T2], F32, "page%d" % i) for i in range(3)]
         for page in pages:
-            nc.vector.memset(page[:], 0.0)
+            nc.gpsimd.memset(page[:], 0.0)
 
         tab_w = [kept([P, T], I32, "tab_w%d" % a) for a in range(2)]
-        w2_w_raw = [kept([P, 2, 2 * HALF], U8, "w2_w_raw%d" % b) for b in range(2)]
+        w2_w_raw = [kept([P, 2, 2 * HALF], U8, "w2_w_raw0"), late.tile([P, 2, 2 * HALF], U8, name="w2_w_raw1", offset=4096, align_bytes=64)]
         w1_raw = {}
 
         def load_tab_words(a):
@@ -82,32 +84,11 @@ def tile_list_deflated_slots_kernel(
             w1_raw[(b, a)] = raw
 
         beta_t = kept([P, 2, 4], F32, "beta_t")
-        wgs_t = [kept([P, S], F32, "wgs%d" % t) for t in range(4)]
+        wgs_first = kept([P, S], F32, "wgs_first")
+        wgs_second = kept([P, S], F32, "wgs_second")
+        wgs_rest = kept([P, 2, S], F32, "wgs_rest")
+        wgs_t = [wgs_first[:], wgs_second[:]] + [wgs_rest[:, t, :] for t in range(2)]
         wgs_rows = wgs.rearrange("(p t) j -> p t j", t=4)
-
-        def load_wgs(t):
-            for q in range(4):
-                nc.sync.dma_start(out=wgs_t[t][32 * q : 32 * (q + 1), :], in_=wgs_rows[:, t, :])
-
-        nc.sync.dma_start(idx[:], offs)
-        load_tab_words(0)
-        load_scale_rows(tab_s, tab_scales)
-        nc.sync.dma_start(out=beta_t[:], in_=beta.rearrange("(b p t) -> p b t", b=2, t=4))
-        load_w1(0, 0)
-        load_w1(0, 1)
-        load_w2_words(0)
-        load_scale_rows(w_s_raw[0], w2_scales[:, :, :HALF])
-        load_tab_words(1)
-        load_w2_words(1)
-        load_scale_rows(w_s_raw[1], w2_scales[:, :, HALF:])
-        load_scale_rows(w_s_raw[1], w5_scales, row=4)
-        load_wgs(0)
-        nc.sync.dma_start(idx2[:], offs2)
-        load_wgs(1)
-        nc.sync.dma_start(idx3[:], offs3)
-        load_w1(1, 0)
-        load_w1(1, 1)
-        load_wgs(2)
 
         given_t = {}
 
@@ -120,108 +101,138 @@ def tile_list_deflated_slots_kernel(
                 )
                 given_t[(b, h)] = g
 
-        load_wgs(3)
+        nc.sync.dma_start(idx[:], offs)
+        load_tab_words(0)
+        for q in range(4):
+            nc.sync.dma_start(
+                out=tab_s[32 * q : 32 * q + 8, :].bitcast(I32), in_=tab_scales[:, 4 * q : 4 * q + 4, :].bitcast(I32)
+            )
+        load_tab_words(1)
+        load_w1(0, 0)
+        load_w2_words(0)
+        load_scale_rows(w_s_raw[0], w2_scales[:, :, :HALF])
+        load_w1(0, 1)
+        nc.sync.dma_start(out=beta_t[:], in_=beta.rearrange("(b p t) -> p b t", b=2, t=4))
+        for q in range(4):
+            nc.sync.dma_start(out=wgs_first[32 * q : 32 * (q + 1), :], in_=wgs_rows[:, 0, :])
+        nc.sync.dma_start(idx2[:], offs2)
+        nc.sync.dma_start(idx3[:], offs3)
+        load_w1(1, 0)
+        for q in range(4):
+            nc.sync.dma_start(out=wgs_second[32 * q : 32 * (q + 1), :], in_=wgs_rows[:, 1, :])
+        load_w1(1, 1)
+        for q in range(4):
+            nc.sync.dma_start(out=wgs_rest[32 * q : 32 * (q + 1), :, :], in_=wgs_rows[:, 2:, :])
+        load_w2_words(1)
+        load_scale_rows(w_s_raw[1], w2_scales[:, :, HALF:])
+        load_scale_rows(w_s_raw[1], w5_scales, row=4)
         load_given(0)
 
-        v_w = {(a, h): kept([P, HALF], U32, "v_w%d%d" % (a, h)) for a in range(2) for h in range(2)}
+        v_w = [ring.tile([P, 2, HALF], U32, name="v_w", tag="v_w", align_bytes=64) for h in range(2)]
 
         def gather_words(a, h):
-            nc.vector.tensor_copy(v_w[(a, h)][:], tab_w[a][:].bitcast(U32).indirect(idx[:, 32 * h : 32 * (h + 1)]))
+            nc.vector.tensor_copy(v_w[h][:, a, :], tab_w[a][:].bitcast(U32).indirect(idx[:, 32 * h : 32 * (h + 1)]))
 
-        w1_w = [kept([P, 2 * HALF], U32, "w1_w%d" % b) for b in range(2)]
-        w1_s = [kept([P, 2 * HALF], U8, "w1_s%d" % b) for b in range(2)]
-        w2_w = [kept([P, 2, 2 * HALF], U8, "w2_w%d" % b) for b in range(2)]
-        w2_s = [kept([P, 2, HALF], U8, "w2_s%d" % b) for b in range(2)]
+        w1_w = {0: kept([P, 2 * HALF], U32, "w1_w0")}
+        w1_s = {0: kept([P, 2 * HALF], U8, "w1_s0")}
+        w2_w = {0: kept([P, 2, 2 * HALF], U8, "w2_w0")}
+        w2_s = {0: kept([P, 2, HALF], U8, "w2_s0")}
         w1_bf = {}
-        dealt = {}
 
-        def round_w1(b, a):
-            if b == 0:
-                grouped = ring.tile([P, 4, P, 4], BF16, name="w1_bf", align_bytes=64)[:]
-            else:
-                grouped = w1_bf["late"][:, a]
+        def round_w1(b, a, t0, t1):
             nc.scalar.copy(
-                out=grouped.rearrange("p t m i -> p m t i"),
-                in_=w1_raw[(b, a)][:].rearrange("p i (m t) -> p m t i", t=4),
+                out=w1_bf[(b, a)][:, t0:t1].rearrange("p t m i -> p m t i"),
+                in_=w1_raw[(b, a)][:].rearrange("p i (m t) -> p m t i", t=4)[:, :, t0:t1, :],
             )
-            w1_bf[(b, a)] = grouped
 
-        def quantise_w1(a):
-            cs = slice(HALF * a, HALF * (a + 1))
+        def quantise_w1(a, t0, t1):
+            cs = slice(HALF * a + P * t0, HALF * a + P * t1)
             nc.vector.quantize_mx(
                 out=w1_w[0][:, cs].bitcast(FP8X4),
                 scales=w1_s[0][:, cs],
-                in_=w1_bf[(0, a)].rearrange("p t m i -> p (t m i)"),
+                in_=w1_bf[(0, a)][:, t0:t1].rearrange("p t m i -> p (t m i)"),
             )
 
-        def deal_w2_words(b):
+        def deal_w2(b):
             nc.vector.tensor_copy(
                 out=w2_w[b][:].bitcast(U16).rearrange("p a (t m) -> p a t m", t=4),
                 in_=w2_w_raw[b][:].bitcast(U16).rearrange("p a (m t) -> p a t m", t=4),
             )
-
-        def deal_scales(b):
             nc.vector.tensor_copy(
                 out=w2_s[b][:].rearrange("p a (t m) -> p a t m", t=4),
                 in_=w_s_raw[b][:].rearrange("p a (m t) -> p a t m", t=4),
             )
 
-        rows = [kept([P, 2, S], F32, "rows%d" % k) for k in range(TILES // 2)]
+        shared = kept([P, 3, M], F32, "shared")
+        pairs = [shared[:, :2, :]] + [kept([P, 2, M], F32, "pair%d" % u)[:] for u in range(1, 3)]
+        d_of = {4: pairs[1][:, 1, :], 5: pairs[2][:, 0, :], 7: pairs[2][:, 1, :]}
+        h_of = {}
+        a_of = {}
 
-        def first_stage(i, h, d_sb):
+        def first_stage(i, h):
             b, t = divmod(i, 4)
             cols = slice(P * t, P * (t + 1))
             js = slice(HALF * h, HALF * (h + 1))
-            acc_a = psum.tile([P, HALF], F32, name="acc")
             acc_d = psum.tile([P, HALF], F32, name="acc")
-            for a in range(2):
-                nc.tensor.matmul_mx(
-                    out=acc_a[:],
-                    lhsT=w1_w[b][:, HALF * a + P * t : HALF * a + P * (t + 1)].bitcast(FP8X4),
-                    lhsT_scale=w1_s[b][:, HALF * a + P * t : HALF * a + P * (t + 1)],
-                    rhs=v_w[(a, h)][:].bitcast(FP8X4), rhs_scale=v_s[a][:, js],
-                    start=(a == 0), stop=(a == 1),
-                )
+            acc_a = psum.tile([P, HALF], F32, name="acc")
             for a in range(2):
                 nc.tensor.matmul_mx(
                     out=acc_d[:],
                     lhsT=w2_w[b][:, a, 2 * P * t : 2 * P * (t + 1)].bitcast(FP4X4),
                     lhsT_scale=w2_s[b][:, a, cols],
-                    rhs=v_w[(a, h)][:].bitcast(FP8X4), rhs_scale=v_s[a][:, js],
+                    rhs=v_w[h][:, a, :].bitcast(FP8X4), rhs_scale=(v_s, v_s_second)[a][:, js],
                     start=(a == 0), stop=(a == 1),
                 )
-            hs = rows[i // 2][:, i % 2, js]
-            nc.scalar.activation(out=d_sb[:, js], in_=acc_d[:], func=ACT.Copy, scale=beta_t[:, b, t : t + 1])
+            for a in range(2):
+                nc.tensor.matmul_mx(
+                    out=acc_a[:],
+                    lhsT=w1_w[b][:, HALF * a + P * t : HALF * a + P * (t + 1)].bitcast(FP8X4),
+                    lhsT_scale=w1_s[b][:, HALF * a + P * t : HALF * a + P * (t + 1)],
+                    rhs=v_w[h][:, a, :].bitcast(FP8X4), rhs_scale=v_s[4 * a :, js],
+                    start=(a == 0), stop=(a == 1),
+                )
+            nc.scalar.activation(out=d_of[i][:, js], in_=acc_d[:], func=ACT.Copy, scale=beta_t[:, b, t : t + 1])
+            hs = h_of[i][:, js]
             if i == 0:
-                nc.vector.tensor_tensor(hs, acc_a[:], d_sb[:, js], ALU.subtract)
+                nc.vector.tensor_tensor(hs, acc_a[:], d_of[i][:, js], ALU.subtract)
                 nc.vector.tensor_tensor(hs, hs, wgs_t[t][:, js], ALU.mult)
             else:
-                nc.scalar.copy(out=hs, in_=acc_a[:])
+                nc.scalar.copy(out=a_of[i][:, js], in_=acc_a[:])
+
+        def new_rows(i):
+            if i == 3:
+                h_of[i] = ring.tile([P, S], F32, name="a_rows3", tag="w5_w", bufs=1, align_bytes=64)[:]
+            else:
+                h_of[i] = ring.tile([P, S], F32, name="h_rows", bufs=5)[:]
+            a_of[i] = pairs[i // 2 - 1][:, 0, :] if i in (2, 4) else h_of[i]
+            if i in (0, 1, 3, 6):
+                d_of[i] = ring.tile([P, S], F32, name="d_rows", bufs=2)[:]
+            if i == 2:
+                d_of[i] = late.tile([P, S], F32, name="d_rows2", offset=0, align_bytes=64)[:]
+
+        def deflate(i):
+            new_rows(i)
+            for h in range(2):
+                first_stage(i, h)
+            nc.gpsimd.tensor_tensor(d_of[i], a_of[i], d_of[i], ALU.subtract)
+
+        def weigh(i):
+            nc.gpsimd.tensor_tensor(h_of[i], d_of[i], wgs_t[i % 4], ALU.mult)
 
         def make_rows(i):
-            if i == 1:
-                d_sb = ring.tile([P, S], F32, name="d_sb", tag="late", bufs=1, align_bytes=64)
-            elif i == 5:
-                d_sb = ring.tile([P, S], F32, name="d_sb", tag="w5_w", bufs=1, align_bytes=64)
-            else:
-                d_sb = ring.tile([P, S], F32, name="d_sb", bufs=3)
-            for h in range(2):
-                first_stage(i, h, d_sb)
-            hs = rows[i // 2][:, i % 2, :]
-            nc.gpsimd.tensor_tensor(hs, hs, d_sb[:], ALU.subtract)
-            nc.gpsimd.tensor_tensor(hs, hs, wgs_t[i % 4][:], ALU.mult)
+            deflate(i)
+            weigh(i)
 
-        def scatter(i):
-            nc.vector.tensor_copy(pages[i % 2][:].indirect(idx2[:]), rows[i // 2][:, i % 2, :])
+        def scatter(i, j0=0, w=S):
+            nc.vector.tensor_copy(pages[i % 3][:].indirect(idx2[:, j0 // 16 : (j0 + w) // 16]), h_of[i][:, j0 : j0 + w])
 
+        z_bf = {}
         z_parts = {0: 2, 1: 4}
-        z_bf = {(b, k): kept([P, M // z_parts[b], 4], BF16, "z_bf%d%d" % (b, k)) for b in range(2) for k in range(z_parts[b])}
         z_w = {(b, k): kept([P, M // z_parts[b]], U32, "z_w%d%d" % (b, k)) for b in range(2) for k in range(z_parts[b])}
         z_s = {(b, k): kept([P, M // z_parts[b]], U8, "z_s%d%d" % (b, k)) for b in range(2) for k in range(z_parts[b])}
 
-
-        def fetch(i, x, m0, w):
-            nc.vector.tensor_copy(x, pages[i % 2][:].indirect(idx3[:, m0 // 16 : (m0 + w) // 16]))
+        def fetch(i, x, m0=0, w=M):
+            nc.vector.tensor_copy(x, pages[i % 3][:].indirect(idx3[:, m0 // 16 : (m0 + w) // 16]))
 
         def invert(parts):
             for x in parts:
@@ -231,62 +242,109 @@ def tile_list_deflated_slots_kernel(
             for x in parts:
                 nc.scalar.activation(out=x, in_=x, func=ACT.Square, scale=ROOT)
 
-        def damp(pair, k, r):
-            b, u = divmod(pair, 2)
-            part = M // z_parts[b]
-            m = k * part
-            g = given_t[(b, m // HALF)][:, 2 * u : 2 * u + 2, m % HALF : m % HALF + part]
-            nc.gpsimd.tensor_tensor(
-                z_bf[(b, k)][:, :, 2 * u : 2 * u + 2], r.rearrange("p e m -> p m e"), g.rearrange("p e m -> p m e"), ALU.mult
-            )
+        def pick(i, x):
+            fetch(i, x)
+            invert([x[:, HALF * h : HALF * (h + 1)] for h in range(2)])
 
-        def damp_single(t, q, r):
-            m = QUARTER * q
-            g = given_t[(1, m // HALF)][:, t, m % HALF : m % HALF + QUARTER]
-            nc.gpsimd.tensor_tensor(z_bf[(1, q)][:, :, t], r, g, ALU.mult)
+        def damp_pair(pair):
+            b, u = divmod(pair, 2)
+            for h in range(2):
+                nc.gpsimd.tensor_tensor(
+                    z_bf[(b, h)][:, :, 2 * u : 2 * u + 2],
+                    pairs[pair][:, :, HALF * h : HALF * (h + 1)].rearrange("p e m -> p m e"),
+                    given_t[(b, h)][:, 2 * u : 2 * u + 2, :].rearrange("p e m -> p m e"),
+                    ALU.mult,
+                )
+
+        def damp_single(t, r, m0, w):
+            h, c0 = divmod(m0, HALF)
+            nc.gpsimd.tensor_tensor(z_bf[(1, h)][:, c0 : c0 + w, t], r, given_t[(1, h)][:, t, c0 : c0 + w], ALU.mult)
 
         def quantise_z(b, k):
+            w = M // z_parts[b]
+            h, c0 = divmod(k * w, HALF)
             nc.vector.quantize_mx(
                 out=z_w[(b, k)][:].bitcast(FP8X4), scales=z_s[(b, k)][:],
-                in_=z_bf[(b, k)][:].rearrange("p m t -> p (m t)"),
+                in_=z_bf[(b, h)][:, c0 : c0 + w, :].rearrange("p m t -> p (m t)"),
             )
 
-        def deal_w5():
-            w5_w = ring.tile([P, 2, N], I32, name="w5_w", tag="w5_w", bufs=1, align_bytes=64)
-            dealt["w5_w"] = w5_w
-            nc.gpsimd.tensor_copy(
-                out=w5_w[:].rearrange("p a (t m) -> p a t m", t=4),
-                in_=w5_w_raw[:].rearrange("p a (m t) -> p a t m", t=4),
-            )
-
-        gather_words(0, 0)
         for a in range(2):
-            nc.vector.tensor_copy(v_s[a][:], tab_s[:, a, :].indirect(idx[:]))
-        round_w1(0, 0)
-        round_w1(0, 1)
-        deal_w2_words(0)
-        deal_scales(0)
-        quantise_w1(0)
-        quantise_w1(1)
+            w1_bf[(0, a)] = ring.tile([P, 4, P, 4], BF16, name="w1_bf", align_bytes=64)[:]
+        gather_words(0, 0)
+        nc.vector.tensor_copy(v_s[:], tab_s[:].indirect(idx[:]))
+        nc.gpsimd.dma_start(out=v_s_second[0:100, :].bitcast(I32), in_=v_s[4:104, :].bitcast(I32))
         gather_words(1, 0)
-        d_first = ring.tile([P, S], F32, name="d_sb", bufs=3)
-        first_stage(0, 0, d_first)
+        round_w1(0, 0, 0, 4)
+        round_w1(0, 1, 0, 1)
+        deal_w2(0)
+        quantise_w1(0, 0, 4)
+        quantise_w1(1, 0, 1)
+        new_rows(0)
+        first_stage(0, 0)
+        round_w1(0, 1, 1, 2)
+        round_w1(0, 1, 2, 4)
         gather_words(0, 1)
         gather_words(1, 1)
-        deal_w2_words(1)
-        deal_scales(1)
-        first_stage(0, 1, d_first)
-        for i in range(1, AHEAD):
-            make_rows(i)
-        w1_bf["late"] = ring.tile([P, 2, 4, P, 4], BF16, name="w1_bf_late", tag="late", bufs=1, align_bytes=64)
-        round_w1(1, 0)
-        round_w1(1, 1)
-        nc.vector.quantize_mx(
-            out=w1_w[1][:].bitcast(FP8X4), scales=w1_s[1][:], in_=w1_bf["late"][:].rearrange("p a t m i -> p (a t m i)")
-        )
+        scatter(0, 0, HALF)
+        quantise_w1(1, 1, 2)
+        quantise_w1(1, 2, 4)
+        first_stage(0, 1)
+        scatter(0, HALF, HALF)
+        make_rows(1)
+        make_rows(2)
+        w1_late = shared[:, 1:, :].bitcast(BF16).rearrange("p a (t m i) -> p a t m i", t=4, i=4)
+        for a in range(2):
+            w1_bf[(1, a)] = w1_late[:, a]
+            round_w1(1, a, 0, 4)
+        deflate(3)
         load_given(1)
         w5_w_raw = big.tile([P, 2, N], I32, name="slot", align_bytes=64)
         nc.sync.dma_start(out=w5_w_raw[:], in_=w5_words.rearrange("a p c i -> p a (c i)").bitcast(I32))
+        w5_w = ring.tile([P, 2, N], I32, name="w5_w", tag="w5_w", bufs=1, align_bytes=64)
+        nc.gpsimd.tensor_copy(
+            out=w5_w[:].rearrange("p a (t m) -> p a t m", t=4),
+            in_=w5_w_raw[:].rearrange("p a (m t) -> p a t m", t=4),
+        )
+        scatter(1)
+        pick(0, pairs[0][:, 0, :])
+        scatter(2)
+
+        w2_w[1] = late.tile([P, 2, 2 * HALF], U8, name="w2_w1", offset=0, align_bytes=64)
+        w2_s[1] = late.tile([P, 2, HALF], U8, name="w2_s1", offset=2048, align_bytes=64)
+        deal_w2(1)
+        w1_w[1] = late.tile([P, 2 * HALF], U32, name="w1_w1", offset=4096, align_bytes=64)
+        w1_s[1] = late.tile([P, 2 * HALF], U8, name="w1_s1", offset=8192, align_bytes=64)
+        nc.vector.quantize_mx(
+            out=w1_w[1][:].bitcast(FP8X4), scales=w1_s[1][:], in_=w1_late.rearrange("p a t m i -> p (a t m i)")
+        )
+        h_of[3] = shared[:, 2, :]
+        weigh(3)
+        for i in range(4, TILES - 1):
+            make_rows(i)
+        deflate(TILES - 1)
+        pick(1, pairs[0][:, 1, :])
+        scatter(3)
+        pick(2, pairs[1][:, 0, :])
+        scatter(4)
+        pick(3, pairs[1][:, 1, :])
+        for h in range(2):
+            z_bf[(0, h)] = ring.tile([P, HALF, 4], BF16, name="z_bf0", tag="v_w", align_bytes=64)
+            z_bf[(1, h)] = kept([P, HALF, 4], BF16, "z_bf1%d" % h)
+        damp_pair(0)
+        damp_pair(1)
+        h_of[7] = pairs[1][:, 0, :]
+        weigh(7)
+        scatter(5)
+        pick(4, pairs[2][:, 0, :])
+        scatter(6)
+        quantise_z(0, 0)
+        quantise_z(0, 1)
+        pick(5, pairs[2][:, 1, :])
+        pick(6, wgs_t[3])
+        scatter(7)
+        damp_pair(2)
+        for h in range(2):
+            damp_single(2, wgs_t[3][:, HALF * h : HALF * (h + 1)], HALF * h, HALF)
 
         y_banks = {}
 
@@ -300,35 +358,11 @@ def tile_list_deflated_slots_kernel(
                     cols = slice(P * (2 * u + e), P * (2 * u + e + 1))
                     nc.tensor.matmul_mx(
                         out=y_banks[(q, u)][:, e, :],
-                        lhsT=dealt["w5_w"][:, b, cols].bitcast(FP8X4), lhsT_scale=w2_s[1][4:, b, cols],
+                        lhsT=w5_w[:, b, cols].bitcast(FP8X4), lhsT_scale=w2_s[1][4:, b, cols],
                         rhs=z_w[(b, k)][:, c0 : c0 + QUARTER].bitcast(FP8X4), rhs_scale=z_s[(b, k)][:, c0 : c0 + QUARTER],
                         start=(b == 0 and e == 0), stop=(b == 1 and e == 1),
                     )
 
-        for i in range(TILES):
-            if i + AHEAD < TILES:
-                make_rows(i + AHEAD)
-            scatter(i)
-            if i < TILES - 2:
-                if i == 0:
-                    picked = ring.tile([P, 2, M], F32, name="picked", tag="late", bufs=1, align_bytes=64)
-                elif i % 2 == 0:
-                    picked = rows[i // 2]
-                fetch(i, picked[:, i % 2, :], 0, M)
-                invert([picked[:, i % 2, HALF * h : HALF * (h + 1)] for h in range(2)])
-                if i % 2 == 1:
-                    parts = z_parts[i // 4]
-                    for k in range(parts):
-                        damp(i // 2, k, picked[:, :, k * M // parts : (k + 1) * M // parts])
-            if i == 3:
-                deal_w5()
-            if i == TILES - 2:
-                fetch(i, rows[3][:, 0, :], 0, M)
-                invert([rows[3][:, 0, HALF * h : HALF * (h + 1)] for h in range(2)])
-                for q in range(4):
-                    damp_single(2, q, rows[3][:, 0, QUARTER * q : QUARTER * (q + 1)])
-                quantise_z(0, 0)
-                quantise_z(0, 1)
         for q in range(4):
             last_stage(0, q)
 
@@ -355,13 +389,12 @@ def tile_list_deflated_slots_kernel(
                 done = slice(0, 3 * QUARTER) if q == 2 else ms
                 nc.sync.dma_start(out=words_out[:, done], in_=y_w[:, done])
 
-        last_x = [rows[3][:, 1, QUARTER * q : QUARTER * (q + 1)] for q in range(4)]
+        last_x = [d_of[6][:, QUARTER * q : QUARTER * (q + 1)] for q in range(4)]
         for q in range(4):
             fetch(TILES - 1, last_x[q], QUARTER * q, QUARTER)
-        for h in range(2):
-            invert(last_x[2 * h : 2 * h + 2])
-            for q in range(2 * h, 2 * h + 2):
-                damp_single(3, q, last_x[q])
+        for q in range(4):
+            invert([last_x[q]])
+            damp_single(3, last_x[q], QUARTER * q, QUARTER)
         for q in range(4):
             quantise_z(1, q)
             last_stage(1, q)

@@ -30,7 +30,7 @@ def tile_list_deflated_slots_kernel(
     nc = tc.nc
     with ExitStack() as ctx:
         keep = ctx.enter_context(tc.tile_pool(name="keep", bufs=1))
-        big = ctx.enter_context(tc.tile_pool(name="big", bufs=6))
+        big = ctx.enter_context(tc.tile_pool(name="big", bufs=5))
         ring = ctx.enter_context(tc.tile_pool(name="ring", bufs=2))
         late = ctx.enter_context(tc.tile_pool(name="late", bufs=1))
         psum = ctx.enter_context(tc.psum_pool(name="psum", bufs=8))
@@ -49,14 +49,11 @@ def tile_list_deflated_slots_kernel(
                     in_=scales[:, 4 * q : 4 * q + 4, :].rearrange("a r c -> r a c").bitcast(I32),
                 )
 
-        tab_s = kept([P, T], U8, "tab_s")
-        v_s = kept([P, S], U8, "v_s")
-        v_s_second = kept([P, S], U8, "v_s_second")
+        tab_s = kept([P, 2, T], U8, "tab_s")
+        v_s = [kept([P, S], U8, "v_s%d" % a) for a in range(2)]
         w_s_raw = [kept([P, 2, HALF], U8, "w_s_raw0"), late.tile([P, 2, HALF], U8, name="w_s_raw1", offset=8192, align_bytes=64)]
-        nc.vector.memset(tab_s[:, : T // 2].bitcast(I32), 0)
-        nc.gpsimd.memset(tab_s[:, T // 2 :].bitcast(I32), 0)
+        nc.gpsimd.memset(tab_s[:].bitcast(I32), 0)
         nc.gpsimd.memset(w_s_raw[0][:].bitcast(I32), 0)
-        nc.gpsimd.memset(v_s_second[:].bitcast(I32), 0)
         nc.gpsimd.memset(w_s_raw[1][:].bitcast(I32), 0)
         pages = [kept([P, T2], F32, "page%d" % i) for i in range(3)]
         for page in pages:
@@ -84,11 +81,12 @@ def tile_list_deflated_slots_kernel(
             w1_raw[(b, a)] = raw
 
         beta_t = kept([P, 2, 4], F32, "beta_t")
-        wgs_first = kept([P, S], F32, "wgs_first")
-        wgs_second = kept([P, S], F32, "wgs_second")
-        wgs_rest = kept([P, 2, S], F32, "wgs_rest")
-        wgs_t = [wgs_first[:], wgs_second[:]] + [wgs_rest[:, t, :] for t in range(2)]
+        wgs_t = [kept([P, S], F32, "wgs%d" % t)[:] for t in range(4)]
         wgs_rows = wgs.rearrange("(p t) j -> p t j", t=4)
+
+        def load_wgs(t):
+            for q in range(4):
+                nc.sync.dma_start(out=wgs_t[t][32 * q : 32 * (q + 1), :], in_=wgs_rows[:, t, :])
 
         given_t = {}
 
@@ -102,30 +100,25 @@ def tile_list_deflated_slots_kernel(
                 given_t[(b, h)] = g
 
         nc.sync.dma_start(idx[:], offs)
+        nc.sync.dma_start(idx2[:], offs2)
+        nc.sync.dma_start(out=beta_t[:], in_=beta.rearrange("(b p t) -> p b t", b=2, t=4))
+        load_scale_rows(tab_s, tab_scales)
         load_tab_words(0)
-        for q in range(4):
-            nc.sync.dma_start(
-                out=tab_s[32 * q : 32 * q + 8, :].bitcast(I32), in_=tab_scales[:, 4 * q : 4 * q + 4, :].bitcast(I32)
-            )
-        load_tab_words(1)
         load_w1(0, 0)
+        load_w1(0, 1)
         load_w2_words(0)
         load_scale_rows(w_s_raw[0], w2_scales[:, :, :HALF])
-        load_w1(0, 1)
-        nc.sync.dma_start(out=beta_t[:], in_=beta.rearrange("(b p t) -> p b t", b=2, t=4))
-        for q in range(4):
-            nc.sync.dma_start(out=wgs_first[32 * q : 32 * (q + 1), :], in_=wgs_rows[:, 0, :])
-        nc.sync.dma_start(idx2[:], offs2)
+        load_tab_words(1)
+        load_wgs(0)
         nc.sync.dma_start(idx3[:], offs3)
+        load_wgs(1)
         load_w1(1, 0)
-        for q in range(4):
-            nc.sync.dma_start(out=wgs_second[32 * q : 32 * (q + 1), :], in_=wgs_rows[:, 1, :])
+        load_wgs(2)
         load_w1(1, 1)
-        for q in range(4):
-            nc.sync.dma_start(out=wgs_rest[32 * q : 32 * (q + 1), :, :], in_=wgs_rows[:, 2:, :])
         load_w2_words(1)
         load_scale_rows(w_s_raw[1], w2_scales[:, :, HALF:])
         load_scale_rows(w_s_raw[1], w5_scales, row=4)
+        load_wgs(3)
         load_given(0)
 
         v_w = [ring.tile([P, 2, HALF], U32, name="v_w", tag="v_w", align_bytes=64) for h in range(2)]
@@ -163,11 +156,10 @@ def tile_list_deflated_slots_kernel(
                 in_=w_s_raw[b][:].rearrange("p a (m t) -> p a t m", t=4),
             )
 
-        shared = kept([P, 3, M], F32, "shared")
-        pairs = [shared[:, :2, :]] + [kept([P, 2, M], F32, "pair%d" % u)[:] for u in range(1, 3)]
-        d_of = {4: pairs[1][:, 1, :], 5: pairs[2][:, 0, :], 7: pairs[2][:, 1, :]}
-        h_of = {}
-        a_of = {}
+        w1_late = kept([P, 2, M], F32, "w1_late")
+        d_of, a_of, h_of, x_of, r_of = {}, {}, {}, {}, {}
+        reused = {3: w1_late[:, 0, :]}
+        halves = [slice(0, HALF), slice(HALF, S)]
 
         def first_stage(i, h):
             b, t = divmod(i, 4)
@@ -180,7 +172,7 @@ def tile_list_deflated_slots_kernel(
                     out=acc_d[:],
                     lhsT=w2_w[b][:, a, 2 * P * t : 2 * P * (t + 1)].bitcast(FP4X4),
                     lhsT_scale=w2_s[b][:, a, cols],
-                    rhs=v_w[h][:, a, :].bitcast(FP8X4), rhs_scale=(v_s, v_s_second)[a][:, js],
+                    rhs=v_w[h][:, a, :].bitcast(FP8X4), rhs_scale=v_s[a][:, js],
                     start=(a == 0), stop=(a == 1),
                 )
             for a in range(2):
@@ -188,77 +180,76 @@ def tile_list_deflated_slots_kernel(
                     out=acc_a[:],
                     lhsT=w1_w[b][:, HALF * a + P * t : HALF * a + P * (t + 1)].bitcast(FP8X4),
                     lhsT_scale=w1_s[b][:, HALF * a + P * t : HALF * a + P * (t + 1)],
-                    rhs=v_w[h][:, a, :].bitcast(FP8X4), rhs_scale=v_s[4 * a :, js],
+                    rhs=v_w[h][:, a, :].bitcast(FP8X4), rhs_scale=v_s[a][:, js],
                     start=(a == 0), stop=(a == 1),
                 )
             nc.scalar.activation(out=d_of[i][:, js], in_=acc_d[:], func=ACT.Copy, scale=beta_t[:, b, t : t + 1])
-            hs = h_of[i][:, js]
             if i == 0:
+                hs = h_of[i][:, js]
                 nc.vector.tensor_tensor(hs, acc_a[:], d_of[i][:, js], ALU.subtract)
                 nc.vector.tensor_tensor(hs, hs, wgs_t[t][:, js], ALU.mult)
             else:
                 nc.scalar.copy(out=a_of[i][:, js], in_=acc_a[:])
 
-        def new_rows(i):
-            if i == 3:
-                h_of[i] = ring.tile([P, S], F32, name="a_rows3", tag="w5_w", bufs=1, align_bytes=64)[:]
-            else:
-                h_of[i] = ring.tile([P, S], F32, name="h_rows", bufs=5)[:]
-            a_of[i] = pairs[i // 2 - 1][:, 0, :] if i in (2, 4) else h_of[i]
-            if i in (0, 1, 3, 6):
-                d_of[i] = ring.tile([P, S], F32, name="d_rows", bufs=2)[:]
-            if i == 2:
-                d_of[i] = late.tile([P, S], F32, name="d_rows2", offset=0, align_bytes=64)[:]
+        def rows(name="d_rows"):
+            return ring.tile([P, S], F32, name=name, bufs={"h_rows": 3, "a_rows": 4, "d_rows": 5}[name])[:]
 
-        def deflate(i):
-            new_rows(i)
+        def multiply(i):
+            a_of[i] = w1_late[:, 1, :] if i == 1 else rows("a_rows")
+            d_of[i] = late.tile([P, S], F32, name="d_rows3", offset=0, align_bytes=64)[:] if i == 3 else rows()
             for h in range(2):
                 first_stage(i, h)
-            nc.gpsimd.tensor_tensor(d_of[i], a_of[i], d_of[i], ALU.subtract)
+
+        def pieces(i):
+            w = HALF if i in (4, 6) else S
+            return [slice(j0, j0 + w) for j0 in range(0, S, w)]
+
+        def deflate(i):
+            x_of[i - 1] = d_of[i - 1] if i in (2, 3) else d_of[i]
+            for js in pieces(i):
+                nc.gpsimd.tensor_tensor(x_of[i - 1][:, js], a_of[i][:, js], d_of[i][:, js], ALU.subtract)
 
         def weigh(i):
-            nc.gpsimd.tensor_tensor(h_of[i], d_of[i], wgs_t[i % 4], ALU.mult)
+            h_of[i] = reused[i] if i in reused else rows("h_rows")
+            for js in pieces(i):
+                nc.gpsimd.tensor_tensor(h_of[i][:, js], x_of[i - 1][:, js], wgs_t[i % 4][:, js], ALU.mult)
 
-        def make_rows(i):
-            deflate(i)
-            weigh(i)
+        def page_of(i):
+            return pages[(0, 1, 1, 0, 2, 1, 0, 0)[i]]
 
         def scatter(i, j0=0, w=S):
-            nc.vector.tensor_copy(pages[i % 3][:].indirect(idx2[:, j0 // 16 : (j0 + w) // 16]), h_of[i][:, j0 : j0 + w])
+            nc.vector.tensor_copy(page_of(i)[:].indirect(idx2[:, j0 // 16 : (j0 + w) // 16]), h_of[i][:, j0 : j0 + w])
 
         z_bf = {}
-        z_parts = {0: 2, 1: 4}
+        z_parts = {0: 1, 1: 4}
         z_w = {(b, k): kept([P, M // z_parts[b]], U32, "z_w%d%d" % (b, k)) for b in range(2) for k in range(z_parts[b])}
         z_s = {(b, k): kept([P, M // z_parts[b]], U8, "z_s%d%d" % (b, k)) for b in range(2) for k in range(z_parts[b])}
 
         def fetch(i, x, m0=0, w=M):
-            nc.vector.tensor_copy(x, pages[i % 3][:].indirect(idx3[:, m0 // 16 : (m0 + w) // 16]))
+            nc.vector.tensor_copy(x, page_of(i)[:].indirect(idx3[:, m0 // 16 : (m0 + w) // 16]))
 
-        def invert(parts):
-            for x in parts:
-                nc.scalar.activation(out=x, in_=x, func=ACT.Square)
+        def invert(parts, picked):
+            for x, p in zip(parts, picked):
+                nc.scalar.activation(out=x, in_=p, func=ACT.Square)
             for x in parts:
                 nc.scalar.activation(out=x, in_=x, func=ACT.Abs_reciprocal_sqrt, scale=ROOT * ROOT, bias=ROOT * ROOT)
             for x in parts:
                 nc.scalar.activation(out=x, in_=x, func=ACT.Square, scale=ROOT)
 
-        def pick(i, x):
-            fetch(i, x)
-            invert([x[:, HALF * h : HALF * (h + 1)] for h in range(2)])
-
-        def damp_pair(pair):
-            b, u = divmod(pair, 2)
-            for h in range(2):
-                nc.gpsimd.tensor_tensor(
-                    z_bf[(b, h)][:, :, 2 * u : 2 * u + 2],
-                    pairs[pair][:, :, HALF * h : HALF * (h + 1)].rearrange("p e m -> p m e"),
-                    given_t[(b, h)][:, 2 * u : 2 * u + 2, :].rearrange("p e m -> p m e"),
-                    ALU.mult,
-                )
-
-        def damp_single(t, r, m0, w):
+        def damp(i, r, m0, w):
+            b, t = divmod(i, 4)
             h, c0 = divmod(m0, HALF)
-            nc.gpsimd.tensor_tensor(z_bf[(1, h)][:, c0 : c0 + w, t], r, given_t[(1, h)][:, t, c0 : c0 + w], ALU.mult)
+            nc.gpsimd.tensor_tensor(z_bf[(b, h)][:, c0 : c0 + w, t], r, given_t[(b, h)][:, t, c0 : c0 + w], ALU.mult)
+
+        def pick(i):
+            if i > 1:
+                fetch(i, x_of[i])
+            r_of[i] = a_of[i + 3] if i + 3 < TILES else x_of[i - 1]
+            invert([r_of[i][:, js] for js in halves], [x_of[i][:, js] for js in halves])
+
+        def damp_rows(i):
+            for h in range(2):
+                damp(i, r_of[i][:, HALF * h : HALF * (h + 1)], HALF * h, HALF)
 
         def quantise_z(b, k):
             w = M // z_parts[b]
@@ -270,16 +261,16 @@ def tile_list_deflated_slots_kernel(
 
         for a in range(2):
             w1_bf[(0, a)] = ring.tile([P, 4, P, 4], BF16, name="w1_bf", align_bytes=64)[:]
+        for a in range(2):
+            nc.vector.tensor_copy(v_s[a][:], tab_s[:, a, :].indirect(idx[:]))
         gather_words(0, 0)
-        nc.vector.tensor_copy(v_s[:], tab_s[:].indirect(idx[:]))
-        nc.gpsimd.dma_start(out=v_s_second[0:100, :].bitcast(I32), in_=v_s[4:104, :].bitcast(I32))
         gather_words(1, 0)
         round_w1(0, 0, 0, 4)
         round_w1(0, 1, 0, 1)
         deal_w2(0)
         quantise_w1(0, 0, 4)
         quantise_w1(1, 0, 1)
-        new_rows(0)
+        h_of[0], d_of[0] = rows("h_rows"), rows()
         first_stage(0, 0)
         round_w1(0, 1, 1, 2)
         round_w1(0, 1, 2, 4)
@@ -290,61 +281,73 @@ def tile_list_deflated_slots_kernel(
         quantise_w1(1, 2, 4)
         first_stage(0, 1)
         scatter(0, HALF, HALF)
-        make_rows(1)
-        make_rows(2)
-        w1_late = shared[:, 1:, :].bitcast(BF16).rearrange("p a (t m i) -> p a t m i", t=4, i=4)
+        multiply(1)
+        deflate(1)
+        weigh(1)
         for a in range(2):
-            w1_bf[(1, a)] = w1_late[:, a]
+            w1_bf[(1, a)] = w1_late[:, a, :].bitcast(BF16).rearrange("p (t m i) -> p t m i", t=4, i=4)
             round_w1(1, a, 0, 4)
+        multiply(2)
+        multiply(3)
+        x_of[0] = d_of[0]
+        fetch(0, x_of[0])
+        deflate(2)
+        weigh(2)
         deflate(3)
+        scatter(1)
         load_given(1)
         w5_w_raw = big.tile([P, 2, N], I32, name="slot", align_bytes=64)
         nc.sync.dma_start(out=w5_w_raw[:], in_=w5_words.rearrange("a p c i -> p a (c i)").bitcast(I32))
-        w5_w = ring.tile([P, 2, N], I32, name="w5_w", tag="w5_w", bufs=1, align_bytes=64)
-        nc.gpsimd.tensor_copy(
-            out=w5_w[:].rearrange("p a (t m) -> p a t m", t=4),
-            in_=w5_w_raw[:].rearrange("p a (m t) -> p a t m", t=4),
-        )
-        scatter(1)
-        pick(0, pairs[0][:, 0, :])
-        scatter(2)
-
         w2_w[1] = late.tile([P, 2, 2 * HALF], U8, name="w2_w1", offset=0, align_bytes=64)
         w2_s[1] = late.tile([P, 2, HALF], U8, name="w2_s1", offset=2048, align_bytes=64)
         deal_w2(1)
         w1_w[1] = late.tile([P, 2 * HALF], U32, name="w1_w1", offset=4096, align_bytes=64)
         w1_s[1] = late.tile([P, 2 * HALF], U8, name="w1_s1", offset=8192, align_bytes=64)
         nc.vector.quantize_mx(
-            out=w1_w[1][:].bitcast(FP8X4), scales=w1_s[1][:], in_=w1_late.rearrange("p a t m i -> p (a t m i)")
+            out=w1_w[1][:].bitcast(FP8X4), scales=w1_s[1][:], in_=w1_late[:].rearrange("p a c -> p (a c)").bitcast(BF16)
         )
-        h_of[3] = shared[:, 2, :]
-        weigh(3)
-        for i in range(4, TILES - 1):
-            make_rows(i)
-        deflate(TILES - 1)
-        pick(1, pairs[0][:, 1, :])
-        scatter(3)
-        pick(2, pairs[1][:, 0, :])
-        scatter(4)
-        pick(3, pairs[1][:, 1, :])
+        z_first = kept([P, M, 4], BF16, "z_first")
         for h in range(2):
-            z_bf[(0, h)] = ring.tile([P, HALF, 4], BF16, name="z_bf0", tag="v_w", align_bytes=64)
+            z_bf[(0, h)] = z_first[:, HALF * h : HALF * (h + 1), :]
             z_bf[(1, h)] = kept([P, HALF, 4], BF16, "z_bf1%d" % h)
-        damp_pair(0)
-        damp_pair(1)
-        h_of[7] = pairs[1][:, 0, :]
-        weigh(7)
+        weigh(3)
+        multiply(4)
+        pick(0)
+        x_of[1] = w1_late[:, 1, :]
+        fetch(1, x_of[1])
+        for i in range(2, 5):
+            multiply(i + 3)
+            deflate(i + 2)
+            if i < 4:
+                weigh(i + 2)
+            damp_rows(i - 2)
+            scatter(i)
+            pick(i - 1)
+        deflate(7)
+        damp_rows(3)
+        reused[6] = a_of[6]
+        weigh(6)
         scatter(5)
-        pick(4, pairs[2][:, 0, :])
+        pick(4)
+        x_of[5] = rows("h_rows")
+        pick(5)
+        w5_w = big.tile([P, 2, N], I32, name="slot", align_bytes=64)
+        nc.vector.tensor_copy(
+            out=w5_w[:].rearrange("p a (t m) -> p a t m", t=4),
+            in_=w5_w_raw[:].rearrange("p a (m t) -> p a t m", t=4),
+        )
+        nc.vector.quantize_mx(
+            out=z_w[(0, 0)][:].bitcast(FP8X4), scales=z_s[(0, 0)][:], in_=z_first[:].rearrange("p m t -> p (m t)")
+        )
+        reused[7] = z_first[:].rearrange("p m t -> p (m t)").bitcast(F32)[:, :S]
+        weigh(7)
         scatter(6)
-        quantise_z(0, 0)
-        quantise_z(0, 1)
-        pick(5, pairs[2][:, 1, :])
-        pick(6, wgs_t[3])
+        damp_rows(4)
+        damp_rows(5)
+        pick(6)
         scatter(7)
-        damp_pair(2)
-        for h in range(2):
-            damp_single(2, wgs_t[3][:, HALF * h : HALF * (h + 1)], HALF * h, HALF)
+        damp_rows(6)
+        x7 = rows("h_rows")
 
         y_banks = {}
 
@@ -389,12 +392,12 @@ def tile_list_deflated_slots_kernel(
                 done = slice(0, 3 * QUARTER) if q == 2 else ms
                 nc.sync.dma_start(out=words_out[:, done], in_=y_w[:, done])
 
-        last_x = [d_of[6][:, QUARTER * q : QUARTER * (q + 1)] for q in range(4)]
+        last_x = [x7[:, QUARTER * q : QUARTER * (q + 1)] for q in range(4)]
         for q in range(4):
             fetch(TILES - 1, last_x[q], QUARTER * q, QUARTER)
         for q in range(4):
-            invert([last_x[q]])
-            damp_single(3, last_x[q], QUARTER * q, QUARTER)
+            invert([last_x[q]], [last_x[q]])
+            damp(TILES - 1, last_x[q], QUARTER * q, QUARTER)
         for q in range(4):
             quantise_z(1, q)
             last_stage(1, q)

@@ -33,7 +33,7 @@ def tile_list_deflated_slots_kernel(
         big = ctx.enter_context(tc.tile_pool(name="big", bufs=5))
         ring = ctx.enter_context(tc.tile_pool(name="ring", bufs=2))
         late = ctx.enter_context(tc.tile_pool(name="late", bufs=1))
-        psum = ctx.enter_context(tc.psum_pool(name="psum", bufs=8))
+        psum = ctx.enter_context(tc.psum_pool(name="psum", bufs=4))
 
         def kept(shape, dtype, name):
             return keep.tile(shape, dtype, name=name, align_bytes=64)
@@ -53,11 +53,11 @@ def tile_list_deflated_slots_kernel(
         v_s = [kept([P, S], U8, "v_s%d" % a) for a in range(2)]
         w_s_raw = [kept([P, 2, HALF], U8, "w_s_raw0"), late.tile([P, 2, HALF], U8, name="w_s_raw1", offset=8192, align_bytes=64)]
         nc.gpsimd.memset(tab_s[:].bitcast(I32), 0)
-        nc.gpsimd.memset(w_s_raw[0][:].bitcast(I32), 0)
-        nc.gpsimd.memset(w_s_raw[1][:].bitcast(I32), 0)
-        pages = [kept([P, T2], F32, "page%d" % i) for i in range(3)]
+        nc.vector.memset(w_s_raw[0][:].bitcast(I32), 0)
+        nc.vector.memset(w_s_raw[1][:].bitcast(I32), 0)
+        pages = [kept([P, T2], F32, "page%d" % i) for i in range(2)]
         for page in pages:
-            nc.gpsimd.memset(page[:], 0.0)
+            nc.vector.memset(page[:], 0.0)
 
         tab_w = [kept([P, T], I32, "tab_w%d" % a) for a in range(2)]
         w2_w_raw = [kept([P, 2, 2 * HALF], U8, "w2_w_raw0"), late.tile([P, 2, 2 * HALF], U8, name="w2_w_raw1", offset=4096, align_bytes=64)]
@@ -105,16 +105,16 @@ def tile_list_deflated_slots_kernel(
         load_scale_rows(tab_s, tab_scales)
         load_tab_words(0)
         load_w1(0, 0)
-        load_w1(0, 1)
         load_w2_words(0)
         load_scale_rows(w_s_raw[0], w2_scales[:, :, :HALF])
+        load_w1(0, 1)
         load_tab_words(1)
         load_wgs(0)
         nc.sync.dma_start(idx3[:], offs3)
-        load_wgs(1)
         load_w1(1, 0)
-        load_wgs(2)
+        load_wgs(1)
         load_w1(1, 1)
+        load_wgs(2)
         load_w2_words(1)
         load_scale_rows(w_s_raw[1], w2_scales[:, :, HALF:])
         load_scale_rows(w_s_raw[1], w5_scales, row=4)
@@ -165,8 +165,9 @@ def tile_list_deflated_slots_kernel(
             b, t = divmod(i, 4)
             cols = slice(P * t, P * (t + 1))
             js = slice(HALF * h, HALF * (h + 1))
-            acc_d = psum.tile([P, HALF], F32, name="acc")
-            acc_a = psum.tile([P, HALF], F32, name="acc")
+            group = "acc%d" % (max(i - 1, 0) % 2)
+            acc_d = psum.tile([P, HALF], F32, name=group)
+            acc_a = psum.tile([P, HALF], F32, name=group)
             for a in range(2):
                 nc.tensor.matmul_mx(
                     out=acc_d[:],
@@ -186,8 +187,13 @@ def tile_list_deflated_slots_kernel(
             nc.scalar.activation(out=d_of[i][:, js], in_=acc_d[:], func=ACT.Copy, scale=beta_t[:, b, t : t + 1])
             if i == 0:
                 hs = h_of[i][:, js]
-                nc.vector.tensor_tensor(hs, acc_a[:], d_of[i][:, js], ALU.subtract)
-                nc.vector.tensor_tensor(hs, hs, wgs_t[t][:, js], ALU.mult)
+                if h == 0:
+                    nc.vector.tensor_tensor(hs, acc_a[:], d_of[i][:, js], ALU.subtract)
+                    nc.vector.tensor_tensor(hs, hs, wgs_t[t][:, js], ALU.mult)
+                else:
+                    nc.scalar.copy(out=hs, in_=acc_a[:])
+                    nc.gpsimd.tensor_tensor(d_of[i][:, js], hs, d_of[i][:, js], ALU.subtract)
+                    nc.gpsimd.tensor_tensor(hs, d_of[i][:, js], wgs_t[t][:, js], ALU.mult)
             else:
                 nc.scalar.copy(out=a_of[i][:, js], in_=acc_a[:])
 
@@ -205,7 +211,7 @@ def tile_list_deflated_slots_kernel(
             return [slice(j0, j0 + w) for j0 in range(0, S, w)]
 
         def deflate(i):
-            x_of[i - 1] = d_of[i - 1] if i in (2, 3) else d_of[i]
+            x_of[i - 1] = {1: d_of[0], 2: d_of[0], 3: d_of.get(2)}.get(i, d_of[i])
             for js in pieces(i):
                 nc.gpsimd.tensor_tensor(x_of[i - 1][:, js], a_of[i][:, js], d_of[i][:, js], ALU.subtract)
 
@@ -215,7 +221,7 @@ def tile_list_deflated_slots_kernel(
                 nc.gpsimd.tensor_tensor(h_of[i][:, js], x_of[i - 1][:, js], wgs_t[i % 4][:, js], ALU.mult)
 
         def page_of(i):
-            return pages[(0, 1, 1, 0, 2, 1, 0, 0)[i]]
+            return pages[(0, 1, 1, 0, 1, 0, 0, 0)[i]]
 
         def scatter(i, j0=0, w=S):
             nc.vector.tensor_copy(page_of(i)[:].indirect(idx2[:, j0 // 16 : (j0 + w) // 16]), h_of[i][:, j0 : j0 + w])
@@ -289,7 +295,7 @@ def tile_list_deflated_slots_kernel(
             round_w1(1, a, 0, 4)
         multiply(2)
         multiply(3)
-        x_of[0] = d_of[0]
+        x_of[0] = d_of[1]
         fetch(0, x_of[0])
         deflate(2)
         weigh(2)
@@ -354,7 +360,7 @@ def tile_list_deflated_slots_kernel(
         def last_stage(b, q):
             for u in range(2):
                 if b == 0:
-                    y_banks[(q, u)] = psum.tile([P, 2, QUARTER], F32, name="acc")
+                    y_banks[(q, u)] = psum.tile([P, 2, QUARTER], F32, name="acc%d" % u)
                 part = M // z_parts[b]
                 k, c0 = divmod(QUARTER * q, part)
                 for e in range(2):

@@ -198,11 +198,16 @@ def tile_list_deflated_slots_kernel(
                 nc.scalar.copy(out=a_of[i][:, js], in_=acc_a[:])
 
         def rows(name="d_rows"):
-            return ring.tile([P, S], F32, name=name, bufs={"h_rows": 3, "a_rows": 4, "d_rows": 5}[name])[:]
+            return ring.tile([P, S], F32, name=name, bufs={"h_rows": 3, "a_rows": 4, "d_rows": 4}[name])[:]
 
         def multiply(i):
             a_of[i] = w1_late[:, 1, :] if i == 1 else rows("a_rows")
-            d_of[i] = late.tile([P, S], F32, name="d_rows3", offset=0, align_bytes=64)[:] if i == 3 else rows()
+            if i == 3:
+                d_of[i] = late.tile([P, S], F32, name="d_rows3", offset=0, align_bytes=64)[:]
+            elif i == 5:
+                d_of[i] = ring.tile([P, S], F32, name="d_rows5", tag="w5_w", bufs=1, align_bytes=64)[:]
+            else:
+                d_of[i] = rows()
             for h in range(2):
                 first_stage(i, h)
 
@@ -337,11 +342,6 @@ def tile_list_deflated_slots_kernel(
         pick(4)
         x_of[5] = rows("h_rows")
         pick(5)
-        w5_w = big.tile([P, 2, N], I32, name="slot", align_bytes=64)
-        nc.vector.tensor_copy(
-            out=w5_w[:].rearrange("p a (t m) -> p a t m", t=4),
-            in_=w5_w_raw[:].rearrange("p a (m t) -> p a t m", t=4),
-        )
         nc.vector.quantize_mx(
             out=z_w[(0, 0)][:].bitcast(FP8X4), scales=z_s[(0, 0)][:], in_=z_first[:].rearrange("p m t -> p (m t)")
         )
@@ -350,6 +350,11 @@ def tile_list_deflated_slots_kernel(
         scatter(6)
         damp_rows(4)
         damp_rows(5)
+        w5_w = ring.tile([P, 2, N], I32, name="w5_w", tag="w5_w", bufs=1, align_bytes=64)
+        nc.gpsimd.tensor_copy(
+            out=w5_w[:].rearrange("p a (t m) -> p a t m", t=4),
+            in_=w5_w_raw[:].rearrange("p a (m t) -> p a t m", t=4),
+        )
         pick(6)
         scatter(7)
         damp_rows(6)
@@ -409,6 +414,6 @@ def tile_list_deflated_slots_kernel(
             last_stage(1, q)
             finish(q)
         for q in range(4):
-            nc.sync.dma_start(
+            nc.scalar.dma_start(
                 out=out_2[0, 4 * q : 4 * q + 4, :].bitcast(I32), in_=y_s[32 * q : 32 * q + 4, :].bitcast(I32)
             )

@@ -19,8 +19,14 @@ ALU = mybir.AluOpType
 P = 128
 HALF = 512
 QUARTER = 256
-TILES = 8
 ROOT = 75.0 / 64.0
+KB = 1024
+
+PLACES = [
+    ("page0", 8), ("page1", 8), ("page2", 8), ("raw0", 8), ("raw1", 8), ("raw2", 8), ("raw3", 8),
+    ("round0", 8), ("late_words", 2), ("late_scales", 1), ("d0", 4), ("w_lo", 4), ("w_hi", 4), ("d1", 4), ("d2", 4),
+    ("d3", 4), ("a2", 4), ("a3", 4), ("h0", 4), ("h1", 4), ("h2", 4), ("pairs", 8),
+]
 
 
 def tile_list_deflated_slots_kernel(
@@ -30,13 +36,23 @@ def tile_list_deflated_slots_kernel(
     nc = tc.nc
     with ExitStack() as ctx:
         keep = ctx.enter_context(tc.tile_pool(name="keep", bufs=1))
-        big = ctx.enter_context(tc.tile_pool(name="big", bufs=5))
-        ring = ctx.enter_context(tc.tile_pool(name="ring", bufs=2))
-        late = ctx.enter_context(tc.tile_pool(name="late", bufs=1))
-        psum = ctx.enter_context(tc.psum_pool(name="psum", bufs=4))
+        arena = ctx.enter_context(tc.tile_pool(name="arena", bufs=1))
+        psum = ctx.enter_context(tc.psum_pool(name="psum", bufs=1))
+
+        start = {}
+        end = 0
+        for place, size in PLACES:
+            start[place] = end
+            end = end + size * KB
 
         def kept(shape, dtype, name):
             return keep.tile(shape, dtype, name=name, align_bytes=64)
+
+        def at(place, shape, dtype, name, skip=0):
+            return arena.tile(shape, dtype, name=name, offset=start[place] + skip, align_bytes=64)
+
+        def rows(place, name, skip=0):
+            return at(place, [P, S], F32, name, skip)[:]
 
         idx = kept([P, S // 16], U16, "idx")
         idx2 = kept([P, S // 16], U16, "idx2")
@@ -49,18 +65,18 @@ def tile_list_deflated_slots_kernel(
                     in_=scales[:, 4 * q : 4 * q + 4, :].rearrange("a r c -> r a c").bitcast(I32),
                 )
 
-        tab_s = kept([P, 2, T], U8, "tab_s")
+        tab_s = at("page2", [P, 2, T], U8, "tab_s")
         v_s = [kept([P, S], U8, "v_s%d" % a) for a in range(2)]
-        w_s_raw = [kept([P, 2, HALF], U8, "w_s_raw0"), late.tile([P, 2, HALF], U8, name="w_s_raw1", offset=8192, align_bytes=64)]
-        nc.gpsimd.memset(tab_s[:].bitcast(I32), 0)
+        w_s_raw = [kept([P, 2, HALF], U8, "w_s_raw0"), at("late_scales", [P, 2, HALF], U8, "w_s_raw1")]
+        nc.vector.memset(tab_s[:].bitcast(I32), 0)
         nc.vector.memset(w_s_raw[0][:].bitcast(I32), 0)
         nc.vector.memset(w_s_raw[1][:].bitcast(I32), 0)
-        pages = [kept([P, T2], F32, "page%d" % i) for i in range(2)]
+        pages = [at("page%d" % i, [P, T2], F32, "page%d" % i) for i in range(2)]
         for page in pages:
             nc.vector.memset(page[:], 0.0)
 
         tab_w = [kept([P, T], I32, "tab_w%d" % a) for a in range(2)]
-        w2_w_raw = [kept([P, 2, 2 * HALF], U8, "w2_w_raw0"), late.tile([P, 2, 2 * HALF], U8, name="w2_w_raw1", offset=4096, align_bytes=64)]
+        w2_w_raw = [kept([P, 2, 2 * HALF], U8, "w2_w_raw0"), at("late_words", [P, 2, 2 * HALF], U8, "w2_w_raw1")]
         w1_raw = {}
 
         def load_tab_words(a):
@@ -73,7 +89,7 @@ def tile_list_deflated_slots_kernel(
             )
 
         def load_w1(b, a):
-            raw = big.tile([P, 4, HALF], F32, name="slot", align_bytes=64)
+            raw = at("raw%d" % (2 * b + a), [P, 4, HALF], F32, "w1_raw%d%d" % (b, a))
             nc.sync.dma_start(
                 out=raw[:],
                 in_=w1[512 * a : 512 * (a + 1), 512 * b : 512 * (b + 1)].rearrange("(p i) c -> p i c", i=4),
@@ -85,19 +101,22 @@ def tile_list_deflated_slots_kernel(
         wgs_rows = wgs.rearrange("(p t) j -> p t j", t=4)
 
         def load_wgs(t):
-            for q in range(4):
+            for q in (0, 2, 1, 3):
                 nc.sync.dma_start(out=wgs_t[t][32 * q : 32 * (q + 1), :], in_=wgs_rows[:, t, :])
 
         given_t = {}
 
         def load_given(b):
-            for h in range(2):
-                g = big.tile([P, 4, HALF], F32, name="slot", align_bytes=64)
+            for u in range(2):
+                g = at("raw%d" % (2 * b + u), [P, 2, M], F32, "given%d%d" % (b, u))
                 nc.sync.dma_start(
                     out=g[:],
-                    in_=given[512 * b : 512 * (b + 1), HALF * h : HALF * (h + 1)].rearrange("(p t) m -> p t m", t=4),
+                    in_=given[512 * b : 512 * (b + 1), :].rearrange("(p t) m -> p t m", t=4)[:, 2 * u : 2 * u + 2, :],
                 )
-                given_t[(b, h)] = g
+                for e in range(2):
+                    given_t[4 * b + 2 * u + e] = g[:, e, :]
+
+        w5_w_raw = kept([P, 2, N], I32, "w5_w_raw")
 
         nc.sync.dma_start(idx[:], offs)
         nc.sync.dma_start(idx2[:], offs2)
@@ -111,17 +130,17 @@ def tile_list_deflated_slots_kernel(
         load_tab_words(1)
         load_wgs(0)
         nc.sync.dma_start(idx3[:], offs3)
-        load_w1(1, 0)
         load_wgs(1)
-        load_w1(1, 1)
-        load_wgs(2)
+        load_w1(1, 0)
         load_w2_words(1)
         load_scale_rows(w_s_raw[1], w2_scales[:, :, HALF:])
         load_scale_rows(w_s_raw[1], w5_scales, row=4)
+        load_w1(1, 1)
+        load_wgs(2)
         load_wgs(3)
-        load_given(0)
+        nc.sync.dma_start(out=w5_w_raw[:], in_=w5_words.rearrange("a p c i -> p a (c i)").bitcast(I32))
 
-        v_w = [ring.tile([P, 2, HALF], U32, name="v_w", tag="v_w", align_bytes=64) for h in range(2)]
+        v_w = [kept([P, 2, HALF], U32, "v_w%d" % h) for h in range(2)]
 
         def gather_words(a, h):
             nc.vector.tensor_copy(v_w[h][:, a, :], tab_w[a][:].bitcast(U32).indirect(idx[:, 32 * h : 32 * (h + 1)]))
@@ -130,21 +149,15 @@ def tile_list_deflated_slots_kernel(
         w1_s = {0: kept([P, 2 * HALF], U8, "w1_s0")}
         w2_w = {0: kept([P, 2, 2 * HALF], U8, "w2_w0")}
         w2_s = {0: kept([P, 2, HALF], U8, "w2_s0")}
-        w1_bf = {}
 
-        def round_w1(b, a, t0, t1):
+        def round_w1(b, a, out):
             nc.scalar.copy(
-                out=w1_bf[(b, a)][:, t0:t1].rearrange("p t m i -> p m t i"),
-                in_=w1_raw[(b, a)][:].rearrange("p i (m t) -> p m t i", t=4)[:, :, t0:t1, :],
+                out=out.rearrange("p (t m i) -> p m t i", t=4, i=4),
+                in_=w1_raw[(b, a)][:].rearrange("p i (m t) -> p m t i", t=4),
             )
 
-        def quantise_w1(a, t0, t1):
-            cs = slice(HALF * a + P * t0, HALF * a + P * t1)
-            nc.vector.quantize_mx(
-                out=w1_w[0][:, cs].bitcast(FP8X4),
-                scales=w1_s[0][:, cs],
-                in_=w1_bf[(0, a)][:, t0:t1].rearrange("p t m i -> p (t m i)"),
-            )
+        def quantise(words, scales, values):
+            nc.vector.quantize_mx(out=words.bitcast(FP8X4), scales=scales, in_=values)
 
         def deal_w2(b):
             nc.vector.tensor_copy(
@@ -156,18 +169,16 @@ def tile_list_deflated_slots_kernel(
                 in_=w_s_raw[b][:].rearrange("p a (m t) -> p a t m", t=4),
             )
 
-        w1_late = kept([P, 2, M], F32, "w1_late")
-        d_of, a_of, h_of, x_of, r_of = {}, {}, {}, {}, {}
-        reused = {3: w1_late[:, 0, :]}
         halves = [slice(0, HALF), slice(HALF, S)]
+        a_of, d_of, t_of, h_of, x_of, r_of = {}, {}, {}, {}, {}, {}
 
-        def first_stage(i, h):
+        def products(i, h):
             b, t = divmod(i, 4)
             cols = slice(P * t, P * (t + 1))
-            js = slice(HALF * h, HALF * (h + 1))
-            group = "acc%d" % (max(i - 1, 0) % 2)
-            acc_d = psum.tile([P, HALF], F32, name=group)
-            acc_a = psum.tile([P, HALF], F32, name=group)
+            js = halves[h]
+            bank = 4 * (i % 2) + 2 * h
+            acc_d = psum.tile([P, HALF], F32, name="bank%d" % bank)
+            acc_a = psum.tile([P, HALF], F32, name="bank%d" % (bank + 1))
             for a in range(2):
                 nc.tensor.matmul_mx(
                     out=acc_d[:],
@@ -185,195 +196,157 @@ def tile_list_deflated_slots_kernel(
                     start=(a == 0), stop=(a == 1),
                 )
             nc.scalar.activation(out=d_of[i][:, js], in_=acc_d[:], func=ACT.Copy, scale=beta_t[:, b, t : t + 1])
-            if i == 0:
-                hs = h_of[i][:, js]
-                if h == 0:
-                    nc.vector.tensor_tensor(hs, acc_a[:], d_of[i][:, js], ALU.subtract)
-                    nc.vector.tensor_tensor(hs, hs, wgs_t[t][:, js], ALU.mult)
-                else:
-                    nc.scalar.copy(out=hs, in_=acc_a[:])
-                    nc.gpsimd.tensor_tensor(d_of[i][:, js], hs, d_of[i][:, js], ALU.subtract)
-                    nc.gpsimd.tensor_tensor(hs, d_of[i][:, js], wgs_t[t][:, js], ALU.mult)
-            else:
-                nc.scalar.copy(out=a_of[i][:, js], in_=acc_a[:])
+            return acc_a
 
-        def rows(name="d_rows"):
-            return ring.tile([P, S], F32, name=name, bufs={"h_rows": 3, "a_rows": 4, "d_rows": 4}[name])[:]
-
-        def multiply(i):
-            a_of[i] = w1_late[:, 1, :] if i == 1 else rows("a_rows")
-            if i == 3:
-                d_of[i] = late.tile([P, S], F32, name="d_rows3", offset=0, align_bytes=64)[:]
-            elif i == 5:
-                d_of[i] = ring.tile([P, S], F32, name="d_rows5", tag="w5_w", bufs=1, align_bytes=64)[:]
-            else:
-                d_of[i] = rows()
+        def multiply(i, a_rows, d_rows):
+            a_of[i], d_of[i] = a_rows, d_rows
             for h in range(2):
-                first_stage(i, h)
+                nc.scalar.copy(out=a_of[i][:, halves[h]], in_=products(i, h)[:])
 
-        def pieces(i):
-            w = HALF if i in (4, 6) else S
-            return [slice(j0, j0 + w) for j0 in range(0, S, w)]
+        def deflate(i, t_rows):
+            t_of[i] = t_rows
+            nc.gpsimd.tensor_tensor(t_of[i], a_of[i], d_of[i], ALU.subtract)
 
-        def deflate(i):
-            x_of[i - 1] = {1: d_of[0], 2: d_of[0], 3: d_of.get(2)}.get(i, d_of[i])
-            for js in pieces(i):
-                nc.gpsimd.tensor_tensor(x_of[i - 1][:, js], a_of[i][:, js], d_of[i][:, js], ALU.subtract)
-
-        def weigh(i):
-            h_of[i] = reused[i] if i in reused else rows("h_rows")
-            for js in pieces(i):
-                nc.gpsimd.tensor_tensor(h_of[i][:, js], x_of[i - 1][:, js], wgs_t[i % 4][:, js], ALU.mult)
-
-        def page_of(i):
-            return pages[(0, 1, 1, 0, 1, 0, 0, 0)[i]]
+        def weigh(i, h_rows):
+            h_of[i] = h_rows
+            nc.gpsimd.tensor_tensor(h_of[i], t_of[i], wgs_t[i % 4], ALU.mult)
 
         def scatter(i, j0=0, w=S):
-            nc.vector.tensor_copy(page_of(i)[:].indirect(idx2[:, j0 // 16 : (j0 + w) // 16]), h_of[i][:, j0 : j0 + w])
-
-        z_bf = {}
-        z_parts = {0: 1, 1: 4}
-        z_w = {(b, k): kept([P, M // z_parts[b]], U32, "z_w%d%d" % (b, k)) for b in range(2) for k in range(z_parts[b])}
-        z_s = {(b, k): kept([P, M // z_parts[b]], U8, "z_s%d%d" % (b, k)) for b in range(2) for k in range(z_parts[b])}
+            nc.vector.tensor_copy(pages[i % 3][:].indirect(idx2[:, j0 // 16 : (j0 + w) // 16]), h_of[i][:, j0 : j0 + w])
 
         def fetch(i, x, m0=0, w=M):
-            nc.vector.tensor_copy(x, page_of(i)[:].indirect(idx3[:, m0 // 16 : (m0 + w) // 16]))
+            nc.vector.tensor_copy(x[:, m0 : m0 + w], pages[i % 3][:].indirect(idx3[:, m0 // 16 : (m0 + w) // 16]))
 
-        def invert(parts, picked):
-            for x, p in zip(parts, picked):
-                nc.scalar.activation(out=x, in_=p, func=ACT.Square)
-            for x in parts:
-                nc.scalar.activation(out=x, in_=x, func=ACT.Abs_reciprocal_sqrt, scale=ROOT * ROOT, bias=ROOT * ROOT)
-            for x in parts:
-                nc.scalar.activation(out=x, in_=x, func=ACT.Square, scale=ROOT)
+        def invert(x, u, r, parts):
+            for js in parts:
+                nc.scalar.activation(out=u[:, js], in_=x[:, js], func=ACT.Square)
+            for js in parts:
+                nc.scalar.activation(
+                    out=u[:, js], in_=u[:, js], func=ACT.Abs_reciprocal_sqrt, scale=ROOT * ROOT, bias=ROOT * ROOT
+                )
+            for js in parts:
+                nc.scalar.activation(out=r[:, js], in_=u[:, js], func=ACT.Square, scale=ROOT)
 
-        def damp(i, r, m0, w):
-            b, t = divmod(i, 4)
-            h, c0 = divmod(m0, HALF)
-            nc.gpsimd.tensor_tensor(z_bf[(b, h)][:, c0 : c0 + w, t], r, given_t[(b, h)][:, t, c0 : c0 + w], ALU.mult)
+        pairs = at("pairs", [P, 2, M, 2], BF16, "pairs")
+        z_bf = [kept([P, M, 4], BF16, "z_bf%d" % b) for b in range(2)]
 
-        def pick(i):
-            if i > 1:
-                fetch(i, x_of[i])
-            r_of[i] = a_of[i + 3] if i + 3 < TILES else x_of[i - 1]
-            invert([r_of[i][:, js] for js in halves], [x_of[i][:, js] for js in halves])
+        def damp(i, ms=slice(0, M)):
+            out = pairs[:, i // 2, ms, i % 2] if i < 4 else z_bf[1][:, ms, i - 4]
+            nc.gpsimd.tensor_tensor(out, r_of[i][:, ms], given_t[i][:, ms], ALU.mult)
 
-        def damp_rows(i):
-            for h in range(2):
-                damp(i, r_of[i][:, HALF * h : HALF * (h + 1)], HALF * h, HALF)
+        def pick(i, place):
+            x_of[i] = rows(place, "x%d" % i)
+            fetch(i, x_of[i])
 
-        def quantise_z(b, k):
-            w = M // z_parts[b]
-            h, c0 = divmod(k * w, HALF)
-            nc.vector.quantize_mx(
-                out=z_w[(b, k)][:].bitcast(FP8X4), scales=z_s[(b, k)][:],
-                in_=z_bf[(b, h)][:, c0 : c0 + w, :].rearrange("p m t -> p (m t)"),
-            )
+        def invert_into(i, place):
+            r_of[i] = rows(place, "r%d" % i)
+            invert(x_of[i], r_of[i], r_of[i], halves)
 
-        for a in range(2):
-            w1_bf[(0, a)] = ring.tile([P, 4, P, 4], BF16, name="w1_bf", align_bytes=64)[:]
+        def invert_back(i, parts):
+            r_of[i] = x_of[i]
+            invert(x_of[i], rows("w_hi", "u%d" % i), r_of[i], parts)
+
         for a in range(2):
             nc.vector.tensor_copy(v_s[a][:], tab_s[:, a, :].indirect(idx[:]))
-        gather_words(0, 0)
-        gather_words(1, 0)
-        round_w1(0, 0, 0, 4)
-        round_w1(0, 1, 0, 1)
-        deal_w2(0)
-        quantise_w1(0, 0, 4)
-        quantise_w1(1, 0, 1)
-        h_of[0], d_of[0] = rows("h_rows"), rows()
-        first_stage(0, 0)
-        round_w1(0, 1, 1, 2)
-        round_w1(0, 1, 2, 4)
-        gather_words(0, 1)
-        gather_words(1, 1)
-        scatter(0, 0, HALF)
-        quantise_w1(1, 1, 2)
-        quantise_w1(1, 2, 4)
-        first_stage(0, 1)
-        scatter(0, HALF, HALF)
-        multiply(1)
-        deflate(1)
-        weigh(1)
+        pages.append(at("page2", [P, T2], F32, "page2"))
+        nc.gpsimd.memset(pages[2][:], 0.0)
+        rounded = [at("round0", [P, 4 * HALF], BF16, "rounded0%d" % a, skip=4 * KB * a) for a in range(2)]
         for a in range(2):
-            w1_bf[(1, a)] = w1_late[:, a, :].bitcast(BF16).rearrange("p (t m i) -> p t m i", t=4, i=4)
-            round_w1(1, a, 0, 4)
-        multiply(2)
-        multiply(3)
-        x_of[0] = d_of[1]
-        fetch(0, x_of[0])
-        deflate(2)
-        weigh(2)
-        deflate(3)
-        scatter(1)
+            round_w1(0, a, rounded[a][:])
+        load_given(0)
+        gather_words(0, 0)
+        gather_words(0, 1)
+        deal_w2(0)
+        quantise(w1_w[0][:, :HALF], w1_s[0][:, :HALF], rounded[0][:])
+        gather_words(1, 0)
+        quantise(w1_w[0][:, HALF:], w1_s[0][:, HALF:], rounded[1][:])
+        gather_words(1, 1)
+
+        d_of[0], h_of[0] = rows("d0", "d_rows0"), rows("h0", "h_rows0")
+        first, second = halves
+        nc.vector.tensor_tensor(h_of[0][:, first], products(0, 0)[:], d_of[0][:, first], ALU.subtract)
+        nc.vector.tensor_tensor(h_of[0][:, first], h_of[0][:, first], wgs_t[0][:, first], ALU.mult)
+        scatter(0, 0, HALF)
+        nc.scalar.copy(out=h_of[0][:, second], in_=products(0, 1)[:])
+        nc.gpsimd.tensor_tensor(d_of[0][:, second], h_of[0][:, second], d_of[0][:, second], ALU.subtract)
+        nc.gpsimd.tensor_tensor(h_of[0][:, second], d_of[0][:, second], wgs_t[0][:, second], ALU.mult)
+        scatter(0, HALF, HALF)
+
+        multiply(1, rows("w_lo", "a_rows1", skip=2 * KB), rows("d1", "d_rows1"))
+        deflate(1, rows("d0", "t_rows1"))
+        weigh(1, rows("h1", "h_rows1"))
+        multiply(2, rows("a2", "a_rows2"), rows("d2", "d_rows2"))
+        late = at("w_lo", [P, 2, 4 * HALF], BF16, "rounded1")
+        for a in range(2):
+            round_w1(1, a, late[:, a, :])
         load_given(1)
-        w5_w_raw = big.tile([P, 2, N], I32, name="slot", align_bytes=64)
-        nc.sync.dma_start(out=w5_w_raw[:], in_=w5_words.rearrange("a p c i -> p a (c i)").bitcast(I32))
-        w2_w[1] = late.tile([P, 2, 2 * HALF], U8, name="w2_w1", offset=0, align_bytes=64)
-        w2_s[1] = late.tile([P, 2, HALF], U8, name="w2_s1", offset=2048, align_bytes=64)
+        deflate(2, rows("d0", "t_rows2"))
+        weigh(2, rows("h2", "h_rows2"))
+        multiply(3, rows("a3", "a_rows3"), rows("d3", "d_rows3"))
+        scatter(1)
+        pick(0, "d2")
+        w2_w[1] = at("a2", [P, 2, 2 * HALF], U8, "w2_w1")
+        w2_s[1] = at("a2", [P, 2, HALF], U8, "w2_s1", skip=2 * KB)
         deal_w2(1)
-        w1_w[1] = late.tile([P, 2 * HALF], U32, name="w1_w1", offset=4096, align_bytes=64)
-        w1_s[1] = late.tile([P, 2 * HALF], U8, name="w1_s1", offset=8192, align_bytes=64)
-        nc.vector.quantize_mx(
-            out=w1_w[1][:].bitcast(FP8X4), scales=w1_s[1][:], in_=w1_late[:].rearrange("p a c -> p (a c)").bitcast(BF16)
-        )
-        z_first = kept([P, M, 4], BF16, "z_first")
-        for h in range(2):
-            z_bf[(0, h)] = z_first[:, HALF * h : HALF * (h + 1), :]
-            z_bf[(1, h)] = kept([P, HALF, 4], BF16, "z_bf1%d" % h)
-        weigh(3)
-        multiply(4)
-        pick(0)
-        x_of[1] = w1_late[:, 1, :]
-        fetch(1, x_of[1])
-        for i in range(2, 5):
-            multiply(i + 3)
-            deflate(i + 2)
-            if i < 4:
-                weigh(i + 2)
-            damp_rows(i - 2)
-            scatter(i)
-            pick(i - 1)
-        deflate(7)
-        damp_rows(3)
-        reused[6] = a_of[6]
-        weigh(6)
-        scatter(5)
-        pick(4)
-        x_of[5] = rows("h_rows")
-        pick(5)
-        nc.vector.quantize_mx(
-            out=z_w[(0, 0)][:].bitcast(FP8X4), scales=z_s[(0, 0)][:], in_=z_first[:].rearrange("p m t -> p (m t)")
-        )
-        reused[7] = z_first[:].rearrange("p m t -> p (m t)").bitcast(F32)[:, :S]
-        weigh(7)
-        scatter(6)
-        damp_rows(4)
-        damp_rows(5)
-        w5_w = ring.tile([P, 2, N], I32, name="w5_w", tag="w5_w", bufs=1, align_bytes=64)
+        w1_w[1] = at("round0", [P, 2 * HALF], U32, "w1_w1")
+        w1_s[1] = at("late_words", [P, 2 * HALF], U8, "w1_s1", skip=3 * HALF)
+        quantise(w1_w[1][:], w1_s[1][:], late[:].rearrange("p a c -> p (a c)"))
+        scatter(2)
+        pick(1, "w_hi")
+        deflate(3, rows("d0", "t_rows3", skip=2 * KB))
+        weigh(3, rows("h0", "h_rows3"))
+
+        a_place = {3: "a3", 4: "d1", 5: "w_lo", 6: "d3", 7: "a3"}
+        d_place = {3: "d0", 4: "d2", 5: "w_hi", 6: "d0", 7: "d2"}
+        h_place = {4: "h1", 5: "h2", 6: "h0", 7: "pairs"}
+        for i in range(4):
+            invert_into(i, a_place[i + 3])
+            multiply(i + 4, rows(a_place[i + 4], "a_rows%d" % (i + 4)), rows(d_place[i + 4], "d_rows%d" % (i + 4)))
+            damp(i)
+            if i == 3:
+                nc.scalar.copy(
+                    out=z_bf[0][:].rearrange("p m t -> p (m t)").bitcast(U32).rearrange("p (m u) -> p m u", u=2),
+                    in_=pairs[:].rearrange("p u m e -> p u (m e)").bitcast(U32).rearrange("p u m -> p m u"),
+                )
+            scatter(i + 3)
+            if i < 3:
+                pick(i + 2, d_place[i + 3])
+            if i == 2:
+                pick(5, "h2")
+            if i == 3:
+                pick(6, "d0")
+            deflate(i + 4, d_of[i + 4])
+            weigh(i + 4, rows(h_place[i + 4], "h_rows%d" % (i + 4)))
+
+        invert_into(4, "a3")
+        damp(4)
+        invert_back(5, halves)
+        w5_w = at("a3", [P, 2, N], I32, "w5_w")
         nc.gpsimd.tensor_copy(
             out=w5_w[:].rearrange("p a (t m) -> p a t m", t=4),
             in_=w5_w_raw[:].rearrange("p a (m t) -> p a t m", t=4),
         )
-        pick(6)
+        damp(5)
+        invert_back(6, halves)
+        damp(6)
         scatter(7)
-        damp_rows(6)
-        x7 = rows("h_rows")
 
+        quarters = [slice(QUARTER * q, QUARTER * (q + 1)) for q in range(4)]
+        z_w = [at("d2", [P, M], U32, "z_w0"), kept([P, M], U32, "z_w1")]
+        z_s = [kept([P, M], U8, "z_s%d" % b) for b in range(2)]
+        quantise(z_w[0][:], z_s[0][:], z_bf[0][:].rearrange("p m t -> p (m t)"))
         y_banks = {}
 
         def last_stage(b, q):
             for u in range(2):
                 if b == 0:
-                    y_banks[(q, u)] = psum.tile([P, 2, QUARTER], F32, name="acc%d" % u)
-                part = M // z_parts[b]
-                k, c0 = divmod(QUARTER * q, part)
+                    y_banks[(q, u)] = psum.tile([P, 2, QUARTER], F32, name="bank%d" % (2 * q + u))
                 for e in range(2):
                     cols = slice(P * (2 * u + e), P * (2 * u + e + 1))
                     nc.tensor.matmul_mx(
                         out=y_banks[(q, u)][:, e, :],
                         lhsT=w5_w[:, b, cols].bitcast(FP8X4), lhsT_scale=w2_s[1][4:, b, cols],
-                        rhs=z_w[(b, k)][:, c0 : c0 + QUARTER].bitcast(FP8X4), rhs_scale=z_s[(b, k)][:, c0 : c0 + QUARTER],
+                        rhs=z_w[b][:, quarters[q]].bitcast(FP8X4), rhs_scale=z_s[b][:, quarters[q]],
                         start=(b == 0 and e == 0), stop=(b == 1 and e == 1),
                     )
 
@@ -386,31 +359,32 @@ def tile_list_deflated_slots_kernel(
         words_out = out_1[0].rearrange("p m t -> p (m t)").bitcast(I32)
 
         def finish(q):
-            ms = slice(QUARTER * q, QUARTER * (q + 1))
-            y = big.tile([P, 4, QUARTER], F32, name="slot", align_bytes=64)
+            ms = quarters[q]
+            y = at("raw0", [P, 4, QUARTER], F32, "y%d" % q, skip=4 * KB * q)
             for u in range(2):
                 nc.scalar.copy(out=y[:, 2 * u : 2 * u + 2, :], in_=y_banks[(q, u)][:])
                 nc.sync.dma_start(out=y_rows[:, 2 * u : 2 * u + 2, ms], in_=y[:, 2 * u : 2 * u + 2, :])
-            y_bf = ring.tile([P, QUARTER, 4], BF16, name="y_bf", tag="w1_bf", align_bytes=64)
+            y_bf = at("round0", [P, QUARTER, 4], BF16, "y_bf%d" % q, skip=4 * KB + 2 * KB * (q % 2))
             nc.vector.tensor_copy(
                 out=y_bf[:].rearrange("p (c i) t -> p c t i", i=4),
                 in_=y[:].rearrange("p t (c i) -> p c t i", i=4),
             )
-            nc.vector.quantize_mx(
-                out=y_w[:, ms].bitcast(FP8X4), scales=y_s[:, ms], in_=y_bf[:].rearrange("p m t -> p (m t)")
-            )
+            quantise(y_w[:, ms], y_s[:, ms], y_bf[:].rearrange("p m t -> p (m t)"))
             if q >= 2:
                 done = slice(0, 3 * QUARTER) if q == 2 else ms
                 nc.sync.dma_start(out=words_out[:, done], in_=y_w[:, done])
 
-        last_x = [x7[:, QUARTER * q : QUARTER * (q + 1)] for q in range(4)]
+        x_of[7] = rows("h0", "x7")
+        for ms in quarters:
+            fetch(7, x_of[7], ms.start, QUARTER)
+        r_of[7] = x_of[7]
+        u7 = rows("w_hi", "u7")
+        for u in range(2):
+            invert(x_of[7], u7, r_of[7], quarters[2 * u : 2 * u + 2])
+            for ms in quarters[2 * u : 2 * u + 2]:
+                damp(7, ms)
         for q in range(4):
-            fetch(TILES - 1, last_x[q], QUARTER * q, QUARTER)
-        for q in range(4):
-            invert([last_x[q]], [last_x[q]])
-            damp(TILES - 1, last_x[q], QUARTER * q, QUARTER)
-        for q in range(4):
-            quantise_z(1, q)
+            quantise(z_w[1][:, quarters[q]], z_s[1][:, quarters[q]], z_bf[1][:, quarters[q], :].rearrange("p m t -> p (m t)"))
             last_stage(1, q)
             finish(q)
         for q in range(4):

@@ -23,9 +23,9 @@ ROOT = 75.0 / 64.0
 KB = 1024
 
 PLACES = [
-    ("page0", 8), ("page1", 8), ("page2", 8), ("raw0", 8), ("raw1", 8), ("raw2", 8), ("raw3", 8),
-    ("round0", 8), ("late_words", 2), ("late_scales", 1), ("d0", 4), ("w_lo", 4), ("w_hi", 4), ("d1", 4), ("d2", 4),
-    ("d3", 4), ("a2", 4), ("a3", 4), ("h0", 4), ("h1", 4), ("h2", 4), ("pairs", 8),
+    ("page0", 8), ("page1", 8), ("page2", 8), ("spare", 8), ("raw0", 8), ("raw1", 8), ("raw2", 8), ("raw3", 8),
+    ("round0", 8), ("late_words", 2), ("late_scales", 1), ("d0", 4), ("w_lo", 4), ("w_hi", 4), ("s1", 4), ("s2", 4),
+    ("s3", 4), ("s4", 4), ("s5", 4), ("h0", 4), ("h1", 4), ("w5_raw", 4), ("tab1", 8),
 ]
 
 
@@ -65,17 +65,16 @@ def tile_list_deflated_slots_kernel(
                     in_=scales[:, 4 * q : 4 * q + 4, :].rearrange("a r c -> r a c").bitcast(I32),
                 )
 
-        tab_s = at("page2", [P, 2, T], U8, "tab_s")
+        tab_s = at("spare", [P, 2, T], U8, "tab_s")
         v_s = [kept([P, S], U8, "v_s%d" % a) for a in range(2)]
         w_s_raw = [kept([P, 2, HALF], U8, "w_s_raw0"), at("late_scales", [P, 2, HALF], U8, "w_s_raw1")]
         nc.vector.memset(tab_s[:].bitcast(I32), 0)
         nc.vector.memset(w_s_raw[0][:].bitcast(I32), 0)
         nc.vector.memset(w_s_raw[1][:].bitcast(I32), 0)
-        pages = [at("page%d" % i, [P, T2], F32, "page%d" % i) for i in range(2)]
-        for page in pages:
-            nc.vector.memset(page[:], 0.0)
+        pages = [at("page0", [P, T2], F32, "page0")]
+        nc.vector.memset(pages[0][:], 0.0)
 
-        tab_w = [kept([P, T], I32, "tab_w%d" % a) for a in range(2)]
+        tab_w = [at("page1", [P, T], I32, "tab_w0", skip=4 * KB), at("tab1", [P, T], I32, "tab_w1")]
         w2_w_raw = [kept([P, 2, 2 * HALF], U8, "w2_w_raw0"), at("late_words", [P, 2, 2 * HALF], U8, "w2_w_raw1")]
         w1_raw = {}
 
@@ -108,7 +107,7 @@ def tile_list_deflated_slots_kernel(
 
         def load_given(b):
             for u in range(2):
-                g = at("raw%d" % (2 * b + u), [P, 2, M], F32, "given%d%d" % (b, u))
+                g = at((("raw0", "raw1"), ("spare", "tab1"))[b][u], [P, 2, M], F32, "given%d%d" % (b, u))
                 nc.sync.dma_start(
                     out=g[:],
                     in_=given[512 * b : 512 * (b + 1), :].rearrange("(p t) m -> p t m", t=4)[:, 2 * u : 2 * u + 2, :],
@@ -116,18 +115,18 @@ def tile_list_deflated_slots_kernel(
                 for e in range(2):
                     given_t[4 * b + 2 * u + e] = g[:, e, :]
 
-        w5_w_raw = kept([P, 2, N], I32, "w5_w_raw")
+        w5_w_raw = at("w5_raw", [P, 2, N], I32, "w5_w_raw")
 
-        nc.sync.dma_start(idx[:], offs)
-        nc.sync.dma_start(idx2[:], offs2)
-        nc.sync.dma_start(out=beta_t[:], in_=beta.rearrange("(b p t) -> p b t", b=2, t=4))
-        load_scale_rows(tab_s, tab_scales)
         load_tab_words(0)
+        nc.sync.dma_start(idx[:], offs)
+        load_scale_rows(tab_s, tab_scales)
         load_w1(0, 0)
         load_w2_words(0)
         load_scale_rows(w_s_raw[0], w2_scales[:, :, :HALF])
         load_w1(0, 1)
         load_tab_words(1)
+        nc.sync.dma_start(out=beta_t[:], in_=beta.rearrange("(b p t) -> p b t", b=2, t=4))
+        nc.sync.dma_start(idx2[:], offs2)
         load_wgs(0)
         nc.sync.dma_start(idx3[:], offs3)
         load_wgs(1)
@@ -136,9 +135,9 @@ def tile_list_deflated_slots_kernel(
         load_scale_rows(w_s_raw[1], w2_scales[:, :, HALF:])
         load_scale_rows(w_s_raw[1], w5_scales, row=4)
         load_w1(1, 1)
+        nc.sync.dma_start(out=w5_w_raw[:], in_=w5_words.rearrange("a p c i -> p a (c i)").bitcast(I32))
         load_wgs(2)
         load_wgs(3)
-        nc.sync.dma_start(out=w5_w_raw[:], in_=w5_words.rearrange("a p c i -> p a (c i)").bitcast(I32))
 
         v_w = [kept([P, 2, HALF], U32, "v_w%d" % h) for h in range(2)]
 
@@ -227,12 +226,10 @@ def tile_list_deflated_slots_kernel(
             for js in parts:
                 nc.scalar.activation(out=r[:, js], in_=u[:, js], func=ACT.Square, scale=ROOT)
 
-        pairs = at("pairs", [P, 2, M, 2], BF16, "pairs")
         z_bf = [kept([P, M, 4], BF16, "z_bf%d" % b) for b in range(2)]
 
         def damp(i, ms=slice(0, M)):
-            out = pairs[:, i // 2, ms, i % 2] if i < 4 else z_bf[1][:, ms, i - 4]
-            nc.gpsimd.tensor_tensor(out, r_of[i][:, ms], given_t[i][:, ms], ALU.mult)
+            nc.gpsimd.tensor_tensor(z_bf[i // 4][:, ms, i % 4], r_of[i][:, ms], given_t[i][:, ms], ALU.mult)
 
         def pick(i, place):
             x_of[i] = rows(place, "x%d" % i)
@@ -244,18 +241,19 @@ def tile_list_deflated_slots_kernel(
 
         def invert_back(i, parts):
             r_of[i] = x_of[i]
-            invert(x_of[i], rows("w_hi", "u%d" % i), r_of[i], parts)
+            invert(x_of[i], rows("s5", "u%d" % i), r_of[i], parts)
 
+        gather_words(0, 0)
+        gather_words(0, 1)
         for a in range(2):
             nc.vector.tensor_copy(v_s[a][:], tab_s[:, a, :].indirect(idx[:]))
-        pages.append(at("page2", [P, T2], F32, "page2"))
-        nc.gpsimd.memset(pages[2][:], 0.0)
+        for i in (1, 2):
+            pages.append(at("page%d" % i, [P, T2], F32, "page%d" % i))
+            nc.gpsimd.memset(pages[i][:], 0.0)
         rounded = [at("round0", [P, 4 * HALF], BF16, "rounded0%d" % a, skip=4 * KB * a) for a in range(2)]
         for a in range(2):
             round_w1(0, a, rounded[a][:])
         load_given(0)
-        gather_words(0, 0)
-        gather_words(0, 1)
         deal_w2(0)
         quantise(w1_w[0][:, :HALF], w1_s[0][:, :HALF], rounded[0][:])
         gather_words(1, 0)
@@ -267,72 +265,73 @@ def tile_list_deflated_slots_kernel(
         nc.vector.tensor_tensor(h_of[0][:, first], products(0, 0)[:], d_of[0][:, first], ALU.subtract)
         nc.vector.tensor_tensor(h_of[0][:, first], h_of[0][:, first], wgs_t[0][:, first], ALU.mult)
         scatter(0, 0, HALF)
-        nc.scalar.copy(out=h_of[0][:, second], in_=products(0, 1)[:])
-        nc.gpsimd.tensor_tensor(d_of[0][:, second], h_of[0][:, second], d_of[0][:, second], ALU.subtract)
+        a_half = at("w_hi", [P, HALF], F32, "a_half")
+        nc.scalar.copy(out=a_half[:], in_=products(0, 1)[:])
+        nc.gpsimd.tensor_tensor(d_of[0][:, second], a_half[:], d_of[0][:, second], ALU.subtract)
         nc.gpsimd.tensor_tensor(h_of[0][:, second], d_of[0][:, second], wgs_t[0][:, second], ALU.mult)
         scatter(0, HALF, HALF)
 
-        multiply(1, rows("w_lo", "a_rows1", skip=2 * KB), rows("d1", "d_rows1"))
+        multiply(1, rows("w_lo", "a_rows1"), rows("s2", "d_rows1"))
+        late = [at("w_hi", [P, 4 * HALF], BF16, "rounded10")]
+        round_w1(1, 0, late[0][:])
         deflate(1, rows("d0", "t_rows1"))
         weigh(1, rows("h1", "h_rows1"))
-        multiply(2, rows("a2", "a_rows2"), rows("d2", "d_rows2"))
-        late = at("w_lo", [P, 2, 4 * HALF], BF16, "rounded1")
-        for a in range(2):
-            round_w1(1, a, late[:, a, :])
-        load_given(1)
+        multiply(2, rows("s1", "a_rows2"), rows("s3", "d_rows2"))
+        late.append(at("w_lo", [P, 4 * HALF], BF16, "rounded11"))
+        round_w1(1, 1, late[1][:])
         deflate(2, rows("d0", "t_rows2"))
-        weigh(2, rows("h2", "h_rows2"))
-        multiply(3, rows("a3", "a_rows3"), rows("d3", "d_rows3"))
+        weigh(2, rows("raw3", "h_rows2"))
+        multiply(3, rows("s4", "a_rows3"), rows("s5", "d_rows3"))
         scatter(1)
-        pick(0, "d2")
-        w2_w[1] = at("a2", [P, 2, 2 * HALF], U8, "w2_w1")
-        w2_s[1] = at("a2", [P, 2, HALF], U8, "w2_s1", skip=2 * KB)
+        pick(0, "s3")
+        w2_w[1] = at("raw3", [P, 2, 2 * HALF], U8, "w2_w1", skip=4 * KB)
+        w2_s[1] = at("raw3", [P, 2, HALF], U8, "w2_s1", skip=6 * KB)
         deal_w2(1)
-        w1_w[1] = at("round0", [P, 2 * HALF], U32, "w1_w1")
-        w1_s[1] = at("late_words", [P, 2 * HALF], U8, "w1_s1", skip=3 * HALF)
-        quantise(w1_w[1][:], w1_s[1][:], late[:].rearrange("p a c -> p (a c)"))
-        scatter(2)
-        pick(1, "w_hi")
-        deflate(3, rows("d0", "t_rows3", skip=2 * KB))
-        weigh(3, rows("h0", "h_rows3"))
-
-        a_place = {3: "a3", 4: "d1", 5: "w_lo", 6: "d3", 7: "a3"}
-        d_place = {3: "d0", 4: "d2", 5: "w_hi", 6: "d0", 7: "d2"}
-        h_place = {4: "h1", 5: "h2", 6: "h0", 7: "pairs"}
-        for i in range(4):
-            invert_into(i, a_place[i + 3])
-            multiply(i + 4, rows(a_place[i + 4], "a_rows%d" % (i + 4)), rows(d_place[i + 4], "d_rows%d" % (i + 4)))
-            damp(i)
-            if i == 3:
-                nc.scalar.copy(
-                    out=z_bf[0][:].rearrange("p m t -> p (m t)").bitcast(U32).rearrange("p (m u) -> p m u", u=2),
-                    in_=pairs[:].rearrange("p u m e -> p u (m e)").bitcast(U32).rearrange("p u m -> p m u"),
-                )
-            scatter(i + 3)
-            if i < 3:
-                pick(i + 2, d_place[i + 3])
-            if i == 2:
-                pick(5, "h2")
-            if i == 3:
-                pick(6, "d0")
-            deflate(i + 4, d_of[i + 4])
-            weigh(i + 4, rows(h_place[i + 4], "h_rows%d" % (i + 4)))
-
-        invert_into(4, "a3")
-        damp(4)
-        invert_back(5, halves)
-        w5_w = at("a3", [P, 2, N], I32, "w5_w")
-        nc.gpsimd.tensor_copy(
+        w5_w = at("raw2", [P, 2, N], I32, "w5_w")
+        nc.vector.tensor_copy(
             out=w5_w[:].rearrange("p a (t m) -> p a t m", t=4),
             in_=w5_w_raw[:].rearrange("p a (m t) -> p a t m", t=4),
         )
+        w1_w[1] = at("w5_raw", [P, 2 * HALF], U32, "w1_w1")
+        w1_s[1] = at("late_words", [P, 2 * HALF], U8, "w1_s1", skip=3 * HALF)
+        for a in range(2):
+            quantise(w1_w[1][:, halves[a]], w1_s[1][:, halves[a]], late[a][:])
+        scatter(2)
+        load_given(1)
+        deflate(3, rows("d0", "t_rows3", skip=2 * KB))
+        weigh(3, rows("h0", "h_rows3"))
+        pick(1, "s5")
+
+        a_place = {3: "s4", 4: "s2", 5: "w_lo", 6: "s3", 7: "s4"}
+        d_place = {4: "s1", 5: "w_hi", 6: "s5", 7: "s1"}
+        h_place = {4: "h1", 5: "raw3", 6: "h0", 7: "s3"}
+        for i in range(4):
+            multiply(i + 4, rows(a_place[i + 4], "a_rows%d" % (i + 4)), rows(d_place[i + 4], "d_rows%d" % (i + 4)))
+            invert_into(i, a_place[i + 3])
+            damp(i)
+            scatter(i + 3)
+            deflate(i + 4, rows("d0", "t_rows%d" % (i + 4)))
+            weigh(i + 4, rows(h_place[i + 4], "h_rows%d" % (i + 4)))
+            if i < 3:
+                pick(i + 2, d_place[i + 4])
+            if i == 2:
+                pick(5, "raw3")
+            if i == 3:
+                x_of[6] = rows("w_hi", "x6")
+                for js in halves:
+                    fetch(6, x_of[6], js.start, HALF)
+
+        invert_into(4, "s4")
+        damp(4)
+        invert_back(5, halves)
         damp(5)
         invert_back(6, halves)
-        damp(6)
+        for js in halves:
+            damp(6, js)
         scatter(7)
 
         quarters = [slice(QUARTER * q, QUARTER * (q + 1)) for q in range(4)]
-        z_w = [at("d2", [P, M], U32, "z_w0"), kept([P, M], U32, "z_w1")]
+        z_w = [at("d0", [P, M], U32, "z_w0"), kept([P, M], U32, "z_w1")]
         z_s = [kept([P, M], U8, "z_s%d" % b) for b in range(2)]
         quantise(z_w[0][:], z_s[0][:], z_bf[0][:].rearrange("p m t -> p (m t)"))
         y_banks = {}
@@ -378,7 +377,7 @@ def tile_list_deflated_slots_kernel(
         for ms in quarters:
             fetch(7, x_of[7], ms.start, QUARTER)
         r_of[7] = x_of[7]
-        u7 = rows("w_hi", "u7")
+        u7 = rows("s5", "u7")
         for u in range(2):
             invert(x_of[7], u7, r_of[7], quarters[2 * u : 2 * u + 2])
             for ms in quarters[2 * u : 2 * u + 2]:

@@ -25,7 +25,7 @@ KB = 1024
 PLACES = [
     ("page0", 8), ("page1", 8), ("page2", 8), ("spare", 8), ("raw0", 8), ("raw1", 8), ("raw2", 8), ("raw3", 8),
     ("round0", 8), ("late_words", 2), ("late_scales", 1), ("d0", 4), ("w_lo", 4), ("w_hi", 4), ("s1", 4), ("s2", 4),
-    ("s3", 4), ("s4", 4), ("s5", 4), ("h0", 4), ("h1", 4), ("w5_raw", 4), ("tab1", 8),
+    ("s3", 4), ("s4", 4), ("s5", 4), ("s6", 4), ("s7", 4), ("x4", 2), ("d6", 2), ("x5", 4), ("h0", 4), ("h1", 4), ("w5_raw", 4), ("z0", 8), ("z_rows", 8), ("tab1", 8),
 ]
 
 
@@ -149,10 +149,10 @@ def tile_list_deflated_slots_kernel(
         w2_w = {0: kept([P, 2, 2 * HALF], U8, "w2_w0")}
         w2_s = {0: kept([P, 2, HALF], U8, "w2_s0")}
 
-        def round_w1(b, a, out):
+        def round_w1(b, a, out, t0=0, t1=4):
             nc.scalar.copy(
-                out=out.rearrange("p (t m i) -> p m t i", t=4, i=4),
-                in_=w1_raw[(b, a)][:].rearrange("p i (m t) -> p m t i", t=4),
+                out=out.rearrange("p (t m i) -> p m t i", t=4, i=4)[:, :, t0:t1, :],
+                in_=w1_raw[(b, a)][:].rearrange("p i (m t) -> p m t i", t=4)[:, :, t0:t1, :],
             )
 
         def quantise(words, scales, values):
@@ -176,23 +176,24 @@ def tile_list_deflated_slots_kernel(
             cols = slice(P * t, P * (t + 1))
             js = halves[h]
             bank = 4 * (i % 2) + 2 * h
+            passes = (0, 1) if i == 0 else (1, 0)
             acc_d = psum.tile([P, HALF], F32, name="bank%d" % bank)
             acc_a = psum.tile([P, HALF], F32, name="bank%d" % (bank + 1))
-            for a in range(2):
+            for a in passes:
                 nc.tensor.matmul_mx(
                     out=acc_d[:],
                     lhsT=w2_w[b][:, a, 2 * P * t : 2 * P * (t + 1)].bitcast(FP4X4),
                     lhsT_scale=w2_s[b][:, a, cols],
                     rhs=v_w[h][:, a, :].bitcast(FP8X4), rhs_scale=v_s[a][:, js],
-                    start=(a == 0), stop=(a == 1),
+                    start=(a == passes[0]), stop=(a == passes[1]),
                 )
-            for a in range(2):
+            for a in passes:
                 nc.tensor.matmul_mx(
                     out=acc_a[:],
                     lhsT=w1_w[b][:, HALF * a + P * t : HALF * a + P * (t + 1)].bitcast(FP8X4),
                     lhsT_scale=w1_s[b][:, HALF * a + P * t : HALF * a + P * (t + 1)],
                     rhs=v_w[h][:, a, :].bitcast(FP8X4), rhs_scale=v_s[a][:, js],
-                    start=(a == 0), stop=(a == 1),
+                    start=(a == passes[0]), stop=(a == passes[1]),
                 )
             nc.scalar.activation(out=d_of[i][:, js], in_=acc_d[:], func=ACT.Copy, scale=beta_t[:, b, t : t + 1])
             return acc_a
@@ -202,13 +203,13 @@ def tile_list_deflated_slots_kernel(
             for h in range(2):
                 nc.scalar.copy(out=a_of[i][:, halves[h]], in_=products(i, h)[:])
 
-        def deflate(i, t_rows):
+        def deflate(i, t_rows, js=slice(0, S)):
             t_of[i] = t_rows
-            nc.gpsimd.tensor_tensor(t_of[i], a_of[i], d_of[i], ALU.subtract)
+            nc.gpsimd.tensor_tensor(t_of[i][:, js], a_of[i][:, js], d_of[i][:, js], ALU.subtract)
 
-        def weigh(i, h_rows):
+        def weigh(i, h_rows, js=slice(0, S)):
             h_of[i] = h_rows
-            nc.gpsimd.tensor_tensor(h_of[i], t_of[i], wgs_t[i % 4], ALU.mult)
+            nc.gpsimd.tensor_tensor(h_of[i][:, js], t_of[i][:, js], wgs_t[i % 4][:, js], ALU.mult)
 
         def scatter(i, j0=0, w=S):
             nc.vector.tensor_copy(pages[i % 3][:].indirect(idx2[:, j0 // 16 : (j0 + w) // 16]), h_of[i][:, j0 : j0 + w])
@@ -226,10 +227,19 @@ def tile_list_deflated_slots_kernel(
             for js in parts:
                 nc.scalar.activation(out=r[:, js], in_=u[:, js], func=ACT.Square, scale=ROOT)
 
-        z_bf = [kept([P, M, 4], BF16, "z_bf%d" % b) for b in range(2)]
+        z_bf = [at("z0", [P, M, 4], BF16, "z_bf0"), kept([P, M, 4], BF16, "z_bf1")]
+
+        z_rows = at("z_rows", [P, 4, M], BF16, "z_rows")
 
         def damp(i, ms=slice(0, M)):
-            nc.gpsimd.tensor_tensor(z_bf[i // 4][:, ms, i % 4], r_of[i][:, ms], given_t[i][:, ms], ALU.mult)
+            out = z_rows[:, i, ms] if i < 4 else z_bf[1][:, ms, i - 4]
+            (nc.gpsimd if i < 7 else nc.vector).tensor_tensor(out, r_of[i][:, ms], given_t[i][:, ms], ALU.mult)
+
+        def weave(t0, t1):
+            nc.scalar.copy(
+                out=z_bf[0][:, :, t0:t1].rearrange("p (c i) t -> p c t i", i=4),
+                in_=z_rows[:, t0:t1, :].rearrange("p t (c i) -> p c t i", i=4),
+            )
 
         def pick(i, place):
             x_of[i] = rows(place, "x%d" % i)
@@ -241,7 +251,7 @@ def tile_list_deflated_slots_kernel(
 
         def invert_back(i, parts):
             r_of[i] = x_of[i]
-            invert(x_of[i], rows("s5", "u%d" % i), r_of[i], parts)
+            invert(x_of[i], rows("x5", "u%d" % i), r_of[i], parts)
 
         gather_words(0, 0)
         gather_words(0, 1)
@@ -251,14 +261,18 @@ def tile_list_deflated_slots_kernel(
             pages.append(at("page%d" % i, [P, T2], F32, "page%d" % i))
             nc.gpsimd.memset(pages[i][:], 0.0)
         rounded = [at("round0", [P, 4 * HALF], BF16, "rounded0%d" % a, skip=4 * KB * a) for a in range(2)]
-        for a in range(2):
-            round_w1(0, a, rounded[a][:])
+        round_w1(0, 0, rounded[0][:])
+        for t in (0, 2):
+            round_w1(0, 1, rounded[1][:], t, t + 2)
         load_given(0)
         deal_w2(0)
         quantise(w1_w[0][:, :HALF], w1_s[0][:, :HALF], rounded[0][:])
+        third = slice(HALF, HALF + QUARTER)
+        fourth = slice(HALF + QUARTER, 2 * HALF)
+        quantise(w1_w[0][:, third], w1_s[0][:, third], rounded[1][:, : 2 * HALF])
         gather_words(1, 0)
-        quantise(w1_w[0][:, HALF:], w1_s[0][:, HALF:], rounded[1][:])
         gather_words(1, 1)
+        quantise(w1_w[0][:, fourth], w1_s[0][:, fourth], rounded[1][:, 2 * HALF :])
 
         d_of[0], h_of[0] = rows("d0", "d_rows0"), rows("h0", "h_rows0")
         first, second = halves
@@ -274,25 +288,24 @@ def tile_list_deflated_slots_kernel(
         multiply(1, rows("w_lo", "a_rows1"), rows("s2", "d_rows1"))
         late = [at("w_hi", [P, 4 * HALF], BF16, "rounded10")]
         round_w1(1, 0, late[0][:])
-        deflate(1, rows("d0", "t_rows1"))
-        weigh(1, rows("h1", "h_rows1"))
+        t_rows1, h_rows1 = at("d0", [P, HALF], F32, "t_rows1", skip=2 * KB), rows("h1", "h_rows1")
+        for js in halves:
+            nc.gpsimd.tensor_tensor(t_rows1[:], a_of[1][:, js], d_of[1][:, js], ALU.subtract)
+            nc.gpsimd.tensor_tensor(h_rows1[:, js], t_rows1[:], wgs_t[1][:, js], ALU.mult)
+        h_of[1] = h_rows1
         multiply(2, rows("s1", "a_rows2"), rows("s3", "d_rows2"))
         late.append(at("w_lo", [P, 4 * HALF], BF16, "rounded11"))
         round_w1(1, 1, late[1][:])
         deflate(2, rows("d0", "t_rows2"))
         weigh(2, rows("raw3", "h_rows2"))
         multiply(3, rows("s4", "a_rows3"), rows("s5", "d_rows3"))
-        scatter(1)
+        for js in halves:
+            scatter(1, js.start, HALF)
         pick(0, "s3")
         w2_w[1] = at("raw3", [P, 2, 2 * HALF], U8, "w2_w1", skip=4 * KB)
         w2_s[1] = at("raw3", [P, 2, HALF], U8, "w2_s1", skip=6 * KB)
         deal_w2(1)
-        w5_w = at("raw2", [P, 2, N], I32, "w5_w")
-        nc.vector.tensor_copy(
-            out=w5_w[:].rearrange("p a (t m) -> p a t m", t=4),
-            in_=w5_w_raw[:].rearrange("p a (m t) -> p a t m", t=4),
-        )
-        w1_w[1] = at("w5_raw", [P, 2 * HALF], U32, "w1_w1")
+        w1_w[1] = at("raw2", [P, 2 * HALF], U32, "w1_w1")
         w1_s[1] = at("late_words", [P, 2 * HALF], U8, "w1_s1", skip=3 * HALF)
         for a in range(2):
             quantise(w1_w[1][:, halves[a]], w1_s[1][:, halves[a]], late[a][:])
@@ -302,28 +315,40 @@ def tile_list_deflated_slots_kernel(
         weigh(3, rows("h0", "h_rows3"))
         pick(1, "s5")
 
-        a_place = {3: "s4", 4: "s2", 5: "w_lo", 6: "s3", 7: "s4"}
-        d_place = {4: "s1", 5: "w_hi", 6: "s5", 7: "s1"}
-        h_place = {4: "h1", 5: "raw3", 6: "h0", 7: "s3"}
+        a_place = {3: "s4", 4: "s2", 5: "w_lo", 6: "s3", 7: "s6"}
+        d_place = {4: "s1", 5: "d6", 6: "z0", 7: "s7"}
+        h_place = {4: "h1", 5: "raw3", 6: "h0", 7: "z_rows"}
         for i in range(4):
             multiply(i + 4, rows(a_place[i + 4], "a_rows%d" % (i + 4)), rows(d_place[i + 4], "d_rows%d" % (i + 4)))
             invert_into(i, a_place[i + 3])
             damp(i)
+            if i == 3:
+                weave(2, 4)
             scatter(i + 3)
-            deflate(i + 4, rows("d0", "t_rows%d" % (i + 4)))
-            weigh(i + 4, rows(h_place[i + 4], "h_rows%d" % (i + 4)))
-            if i < 3:
-                pick(i + 2, d_place[i + 4])
             if i == 2:
                 pick(5, "raw3")
+            deflate(i + 4, rows("d0", "t_rows%d" % (i + 4)))
+            weigh(i + 4, rows(h_place[i + 4], "h_rows%d" % (i + 4)))
+            if i == 2:
+                weave(0, 2)
+            if i == 0:
+                pick(2, "s1")
+            if i == 1:
+                pick(3, "x4")
+                pick(4, "x5")
             if i == 3:
                 x_of[6] = rows("w_hi", "x6")
                 for js in halves:
                     fetch(6, x_of[6], js.start, HALF)
 
-        invert_into(4, "s4")
+        invert_into(4, "s6")
         damp(4)
         invert_back(5, halves)
+        w5_w = at("s6", [P, 2, N], I32, "w5_w")
+        nc.gpsimd.tensor_copy(
+            out=w5_w[:].rearrange("p a (t m) -> p a t m", t=4),
+            in_=w5_w_raw[:].rearrange("p a (m t) -> p a t m", t=4),
+        )
         damp(5)
         invert_back(6, halves)
         for js in halves:
@@ -331,8 +356,11 @@ def tile_list_deflated_slots_kernel(
         scatter(7)
 
         quarters = [slice(QUARTER * q, QUARTER * (q + 1)) for q in range(4)]
-        z_w = [at("d0", [P, M], U32, "z_w0"), kept([P, M], U32, "z_w1")]
+        z_w = [at("z_rows", [P, M], U32, "z_w0"), kept([P, M], U32, "z_w1")]
         z_s = [kept([P, M], U8, "z_s%d" % b) for b in range(2)]
+        x_of[7] = rows("d0", "x7")
+        for ms in quarters[:2]:
+            fetch(7, x_of[7], ms.start, QUARTER)
         quantise(z_w[0][:], z_s[0][:], z_bf[0][:].rearrange("p m t -> p (m t)"))
         y_banks = {}
 
@@ -357,35 +385,44 @@ def tile_list_deflated_slots_kernel(
         y_rows = out_0.rearrange("(p t) m -> p t m", t=4)
         words_out = out_1[0].rearrange("p m t -> p (m t)").bitcast(I32)
 
+        y_bf = {}
+
         def finish(q):
-            ms = quarters[q]
             y = at("raw0", [P, 4, QUARTER], F32, "y%d" % q, skip=4 * KB * q)
             for u in range(2):
                 nc.scalar.copy(out=y[:, 2 * u : 2 * u + 2, :], in_=y_banks[(q, u)][:])
-                nc.sync.dma_start(out=y_rows[:, 2 * u : 2 * u + 2, ms], in_=y[:, 2 * u : 2 * u + 2, :])
-            y_bf = at("round0", [P, QUARTER, 4], BF16, "y_bf%d" % q, skip=4 * KB + 2 * KB * (q % 2))
+                nc.sync.dma_start(out=y_rows[:, 2 * u : 2 * u + 2, quarters[q]], in_=y[:, 2 * u : 2 * u + 2, :])
+            y_bf[q] = at("round0", [P, QUARTER, 4], BF16, "y_bf%d" % q, skip=2 * KB * q)
             nc.vector.tensor_copy(
-                out=y_bf[:].rearrange("p (c i) t -> p c t i", i=4),
+                out=y_bf[q][:].rearrange("p (c i) t -> p c t i", i=4),
                 in_=y[:].rearrange("p t (c i) -> p c t i", i=4),
             )
-            quantise(y_w[:, ms], y_s[:, ms], y_bf[:].rearrange("p m t -> p (m t)"))
+
+        def planes(q):
+            ms = quarters[q]
+            quantise(y_w[:, ms], y_s[:, ms], y_bf[q][:].rearrange("p m t -> p (m t)"))
             if q >= 2:
                 done = slice(0, 3 * QUARTER) if q == 2 else ms
                 nc.sync.dma_start(out=words_out[:, done], in_=y_w[:, done])
 
-        x_of[7] = rows("h0", "x7")
-        for ms in quarters:
+        for ms in quarters[2:]:
             fetch(7, x_of[7], ms.start, QUARTER)
-        r_of[7] = x_of[7]
-        u7 = rows("s5", "u7")
+        r_of[7] = rows("w_hi", "r7")
+        u7 = rows("x5", "u7")
         for u in range(2):
-            invert(x_of[7], u7, r_of[7], quarters[2 * u : 2 * u + 2])
-            for ms in quarters[2 * u : 2 * u + 2]:
-                damp(7, ms)
-        for q in range(4):
-            quantise(z_w[1][:, quarters[q]], z_s[1][:, quarters[q]], z_bf[1][:, quarters[q], :].rearrange("p m t -> p (m t)"))
-            last_stage(1, q)
-            finish(q)
+            pair = (2 * u, 2 * u + 1)
+            invert(x_of[7], u7, r_of[7], [quarters[q] for q in pair])
+            for q in pair:
+                damp(7, quarters[q])
+            for q in pair:
+                ms = quarters[q]
+                quantise(z_w[1][:, ms], z_s[1][:, ms], z_bf[1][:, ms, :].rearrange("p m t -> p (m t)"))
+                last_stage(1, q)
+        for q in range(5):
+            if q < 4:
+                finish(q)
+            if q > 0:
+                planes(q - 1)
         for q in range(4):
             nc.scalar.dma_start(
                 out=out_2[0, 4 * q : 4 * q + 4, :].bitcast(I32), in_=y_s[32 * q : 32 * q + 4, :].bitcast(I32)

@@ -139,10 +139,10 @@ def tile_list_deflated_slots_kernel(
         load_wgs(2)
         load_wgs(3)
 
-        v_w = [kept([P, 2, HALF], U32, "v_w%d" % h) for h in range(2)]
+        v_w = [kept([P, S], U32, "v_w%d" % a) for a in range(2)]
 
-        def gather_words(a, h):
-            nc.vector.tensor_copy(v_w[h][:, a, :], tab_w[a][:].bitcast(U32).indirect(idx[:, 32 * h : 32 * (h + 1)]))
+        def gather_words(a, j0=0, w=S):
+            nc.vector.tensor_copy(v_w[a][:, j0 : j0 + w], tab_w[a][:].bitcast(U32).indirect(idx[:, j0 // 16 : (j0 + w) // 16]))
 
         w1_w = {0: kept([P, 2 * HALF], U32, "w1_w0")}
         w1_s = {0: kept([P, 2 * HALF], U8, "w1_s0")}
@@ -184,7 +184,7 @@ def tile_list_deflated_slots_kernel(
                     out=acc_d[:],
                     lhsT=w2_w[b][:, a, 2 * P * t : 2 * P * (t + 1)].bitcast(FP4X4),
                     lhsT_scale=w2_s[b][:, a, cols],
-                    rhs=v_w[h][:, a, :].bitcast(FP8X4), rhs_scale=v_s[a][:, js],
+                    rhs=v_w[a][:, js].bitcast(FP8X4), rhs_scale=v_s[a][:, js],
                     start=(a == passes[0]), stop=(a == passes[1]),
                 )
             for a in passes:
@@ -192,7 +192,7 @@ def tile_list_deflated_slots_kernel(
                     out=acc_a[:],
                     lhsT=w1_w[b][:, HALF * a + P * t : HALF * a + P * (t + 1)].bitcast(FP8X4),
                     lhsT_scale=w1_s[b][:, HALF * a + P * t : HALF * a + P * (t + 1)],
-                    rhs=v_w[h][:, a, :].bitcast(FP8X4), rhs_scale=v_s[a][:, js],
+                    rhs=v_w[a][:, js].bitcast(FP8X4), rhs_scale=v_s[a][:, js],
                     start=(a == passes[0]), stop=(a == passes[1]),
                 )
             nc.scalar.activation(out=d_of[i][:, js], in_=acc_d[:], func=ACT.Copy, scale=beta_t[:, b, t : t + 1])
@@ -227,19 +227,13 @@ def tile_list_deflated_slots_kernel(
             for js in parts:
                 nc.scalar.activation(out=r[:, js], in_=u[:, js], func=ACT.Square, scale=ROOT)
 
-        z_bf = [at("z0", [P, M, 4], BF16, "z_bf0"), kept([P, M, 4], BF16, "z_bf1")]
+        z_bf = {1: kept([P, M, 4], BF16, "z_bf1")}
 
         z_rows = at("z_rows", [P, 4, M], BF16, "z_rows")
 
         def damp(i, ms=slice(0, M)):
             out = z_rows[:, i, ms] if i < 4 else z_bf[1][:, ms, i - 4]
             (nc.gpsimd if i < 7 else nc.vector).tensor_tensor(out, r_of[i][:, ms], given_t[i][:, ms], ALU.mult)
-
-        def weave(t0, t1):
-            nc.scalar.copy(
-                out=z_bf[0][:, :, t0:t1].rearrange("p (c i) t -> p c t i", i=4),
-                in_=z_rows[:, t0:t1, :].rearrange("p t (c i) -> p c t i", i=4),
-            )
 
         def pick(i, place):
             x_of[i] = rows(place, "x%d" % i)
@@ -251,10 +245,9 @@ def tile_list_deflated_slots_kernel(
 
         def invert_back(i, parts):
             r_of[i] = x_of[i]
-            invert(x_of[i], rows("x5", "u%d" % i), r_of[i], parts)
+            invert(x_of[i], rows("z_rows", "u%d" % i, skip=4 * KB), r_of[i], parts)
 
-        gather_words(0, 0)
-        gather_words(0, 1)
+        gather_words(0)
         for a in range(2):
             nc.vector.tensor_copy(v_s[a][:], tab_s[:, a, :].indirect(idx[:]))
         for i in (1, 2):
@@ -270,8 +263,8 @@ def tile_list_deflated_slots_kernel(
         third = slice(HALF, HALF + QUARTER)
         fourth = slice(HALF + QUARTER, 2 * HALF)
         quantise(w1_w[0][:, third], w1_s[0][:, third], rounded[1][:, : 2 * HALF])
-        gather_words(1, 0)
-        gather_words(1, 1)
+        gather_words(1, 0, HALF)
+        gather_words(1, HALF, HALF)
         quantise(w1_w[0][:, fourth], w1_s[0][:, fourth], rounded[1][:, 2 * HALF :])
 
         d_of[0], h_of[0] = rows("d0", "d_rows0"), rows("h0", "h_rows0")
@@ -316,33 +309,35 @@ def tile_list_deflated_slots_kernel(
         pick(1, "s5")
 
         a_place = {3: "s4", 4: "s2", 5: "w_lo", 6: "s3", 7: "s6"}
-        d_place = {4: "s1", 5: "d6", 6: "z0", 7: "s7"}
-        h_place = {4: "h1", 5: "raw3", 6: "h0", 7: "z_rows"}
+        d_place = {4: "s1", 5: "d6", 6: "s7", 7: "z0"}
+        h_place = {4: "h1", 5: "raw3", 6: "h0"}
         for i in range(4):
             multiply(i + 4, rows(a_place[i + 4], "a_rows%d" % (i + 4)), rows(d_place[i + 4], "d_rows%d" % (i + 4)))
             invert_into(i, a_place[i + 3])
             damp(i)
-            if i == 3:
-                weave(2, 4)
             scatter(i + 3)
             if i == 2:
                 pick(5, "raw3")
             deflate(i + 4, rows("d0", "t_rows%d" % (i + 4)))
-            weigh(i + 4, rows(h_place[i + 4], "h_rows%d" % (i + 4)))
-            if i == 2:
-                weave(0, 2)
+            if i < 3:
+                weigh(i + 4, rows(h_place[i + 4], "h_rows%d" % (i + 4)))
             if i == 0:
                 pick(2, "s1")
             if i == 1:
                 pick(3, "x4")
                 pick(4, "x5")
             if i == 3:
-                x_of[6] = rows("w_hi", "x6")
-                for js in halves:
-                    fetch(6, x_of[6], js.start, HALF)
+                pick(6, "w_hi")
 
-        invert_into(4, "s6")
+        r_of[4] = rows("s6", "r4")
+        invert(x_of[4], rows("z0", "u4"), r_of[4], halves)
+        z_bf[0] = at("z0", [P, M, 4], BF16, "z_bf0")
+        nc.scalar.copy(
+            out=z_bf[0][:].rearrange("p (c i) t -> p c t i", i=4),
+            in_=z_rows[:].rearrange("p t (c i) -> p c t i", i=4),
+        )
         damp(4)
+        weigh(7, rows("z_rows", "h_rows7"))
         invert_back(5, halves)
         w5_w = at("s6", [P, 2, N], I32, "w5_w")
         nc.gpsimd.tensor_copy(
@@ -359,8 +354,7 @@ def tile_list_deflated_slots_kernel(
         z_w = [at("z_rows", [P, M], U32, "z_w0"), kept([P, M], U32, "z_w1")]
         z_s = [kept([P, M], U8, "z_s%d" % b) for b in range(2)]
         x_of[7] = rows("d0", "x7")
-        for ms in quarters[:2]:
-            fetch(7, x_of[7], ms.start, QUARTER)
+        fetch(7, x_of[7], 0, HALF)
         quantise(z_w[0][:], z_s[0][:], z_bf[0][:].rearrange("p m t -> p (m t)"))
         y_banks = {}
 
@@ -405,10 +399,9 @@ def tile_list_deflated_slots_kernel(
                 done = slice(0, 3 * QUARTER) if q == 2 else ms
                 nc.sync.dma_start(out=words_out[:, done], in_=y_w[:, done])
 
-        for ms in quarters[2:]:
-            fetch(7, x_of[7], ms.start, QUARTER)
+        fetch(7, x_of[7], HALF, HALF)
         r_of[7] = rows("w_hi", "r7")
-        u7 = rows("x5", "u7")
+        u7 = rows("z_rows", "u7", skip=4 * KB)
         for u in range(2):
             pair = (2 * u, 2 * u + 1)
             invert(x_of[7], u7, r_of[7], [quarters[q] for q in pair])

@@ -59,10 +59,10 @@ def tile_list_deflated_slots_kernel(
         idx3 = kept([P, M // 16], U16, "idx3")
 
         def load_scale_rows(plane, scales, row=0):
-            for q in range(4):
+            for r in range(4):
                 nc.sync.dma_start(
-                    out=plane[32 * q + row : 32 * q + row + 4, :, :].bitcast(I32),
-                    in_=scales[:, 4 * q : 4 * q + 4, :].rearrange("a r c -> r a c").bitcast(I32),
+                    out=plane[row + r : P : 32, :, :].bitcast(I32),
+                    in_=scales[:, r:16:4, :].rearrange("a q c -> q a c").bitcast(I32),
                 )
 
         tab_s = at("spare", [P, 2, T], U8, "tab_s")
@@ -233,7 +233,7 @@ def tile_list_deflated_slots_kernel(
 
         def damp(i, ms=slice(0, M)):
             out = z_rows[:, i, ms] if i < 4 else z_bf[1][:, ms, i - 4]
-            (nc.gpsimd if i < 7 else nc.vector).tensor_tensor(out, r_of[i][:, ms], given_t[i][:, ms], ALU.mult)
+            nc.gpsimd.tensor_tensor(out, r_of[i][:, ms], given_t[i][:, ms], ALU.mult)
 
         def pick(i, place):
             x_of[i] = rows(place, "x%d" % i)
@@ -400,7 +400,7 @@ def tile_list_deflated_slots_kernel(
                 nc.sync.dma_start(out=words_out[:, done], in_=y_w[:, done])
 
         fetch(7, x_of[7], HALF, HALF)
-        r_of[7] = rows("w_hi", "r7")
+        r_of[7] = x_of[7]
         u7 = rows("z_rows", "u7", skip=4 * KB)
         for u in range(2):
             pair = (2 * u, 2 * u + 1)
@@ -416,7 +416,5 @@ def tile_list_deflated_slots_kernel(
                 finish(q)
             if q > 0:
                 planes(q - 1)
-        for q in range(4):
-            nc.scalar.dma_start(
-                out=out_2[0, 4 * q : 4 * q + 4, :].bitcast(I32), in_=y_s[32 * q : 32 * q + 4, :].bitcast(I32)
-            )
+        for r in range(4):
+            nc.scalar.dma_start(out=out_2[0, r:16:4, :].bitcast(I32), in_=y_s[r:P:32, :].bitcast(I32))

@@ -24,8 +24,8 @@ KB = 1024
 
 PLACES = [
     ("page0", 8), ("page1", 8), ("page2", 8), ("spare", 8), ("raw0", 8), ("raw1", 8), ("raw2", 8), ("raw3", 8),
-    ("round0", 8), ("late_words", 2), ("late_scales", 1), ("d0", 4), ("w_lo", 4), ("w_hi", 4), ("s1", 4), ("s2", 4),
-    ("s3", 4), ("s4", 4), ("s5", 4), ("s6", 4), ("s7", 4), ("x4", 2), ("d6", 2), ("x5", 4), ("h0", 4), ("h1", 4), ("w5_raw", 4), ("z0", 8), ("z_rows", 8), ("tab1", 8),
+    ("round0", 8), ("d0", 4), ("w_lo", 4), ("w_hi", 4), ("s1", 4), ("s2", 4),
+    ("s3", 4), ("s4", 4), ("s5", 4), ("s6", 4), ("s7", 4), ("x4", 2), ("d6", 2), ("x5", 4), ("h0", 4), ("h1", 4), ("w5_raw", 4), ("z0", 8), ("z_rows", 8), ("tab0", 8), ("tab1", 8),
 ]
 
 
@@ -67,15 +67,16 @@ def tile_list_deflated_slots_kernel(
 
         tab_s = at("spare", [P, 2, T], U8, "tab_s")
         v_s = [kept([P, S], U8, "v_s%d" % a) for a in range(2)]
-        w_s_raw = [kept([P, 2, HALF], U8, "w_s_raw0"), at("late_scales", [P, 2, HALF], U8, "w_s_raw1")]
+        w_s_raw = [kept([P, 2, HALF], U8, "w_s_raw0"), kept([P, 2, HALF], U8, "w_s_raw1")]
         nc.vector.memset(tab_s[:].bitcast(I32), 0)
         nc.vector.memset(w_s_raw[0][:].bitcast(I32), 0)
         nc.vector.memset(w_s_raw[1][:].bitcast(I32), 0)
-        pages = [at("page0", [P, T2], F32, "page0")]
-        nc.vector.memset(pages[0][:], 0.0)
+        pages = [at("page%d" % i, [P, T2], F32, "page%d" % i) for i in range(3)]
+        for page in pages:
+            nc.vector.memset(page[:], 0.0)
 
-        tab_w = [at("page1", [P, T], I32, "tab_w0", skip=4 * KB), at("tab1", [P, T], I32, "tab_w1")]
-        w2_w_raw = [kept([P, 2, 2 * HALF], U8, "w2_w_raw0"), at("late_words", [P, 2, 2 * HALF], U8, "w2_w_raw1")]
+        tab_w = [at("tab0", [P, T], I32, "tab_w0"), at("tab1", [P, T], I32, "tab_w1")]
+        w2_w_raw = [kept([P, 2, 2 * HALF], U8, "w2_w_raw0"), kept([P, 2, 2 * HALF], U8, "w2_w_raw1")]
         w1_raw = {}
 
         def load_tab_words(a):
@@ -158,11 +159,13 @@ def tile_list_deflated_slots_kernel(
         def quantise(words, scales, values):
             nc.vector.quantize_mx(out=words.bitcast(FP8X4), scales=scales, in_=values)
 
-        def deal_w2(b):
+        def deal_words(b):
             nc.vector.tensor_copy(
                 out=w2_w[b][:].bitcast(U16).rearrange("p a (t m) -> p a t m", t=4),
                 in_=w2_w_raw[b][:].bitcast(U16).rearrange("p a (m t) -> p a t m", t=4),
             )
+
+        def deal_scales(b):
             nc.vector.tensor_copy(
                 out=w2_s[b][:].rearrange("p a (t m) -> p a t m", t=4),
                 in_=w_s_raw[b][:].rearrange("p a (m t) -> p a t m", t=4),
@@ -170,6 +173,11 @@ def tile_list_deflated_slots_kernel(
 
         halves = [slice(0, HALF), slice(HALF, S)]
         a_of, d_of, t_of, h_of, x_of, r_of = {}, {}, {}, {}, {}, {}
+
+        def w1_scales(b, a, t):
+            if (b, a) == (0, 1) and t >= 2:
+                return last_scales[:, P * (t - 2) : P * (t - 1)]
+            return w1_s[b][:, HALF * a + P * t : HALF * a + P * (t + 1)]
 
         def products(i, h):
             b, t = divmod(i, 4)
@@ -191,7 +199,7 @@ def tile_list_deflated_slots_kernel(
                 nc.tensor.matmul_mx(
                     out=acc_a[:],
                     lhsT=w1_w[b][:, HALF * a + P * t : HALF * a + P * (t + 1)].bitcast(FP8X4),
-                    lhsT_scale=w1_s[b][:, HALF * a + P * t : HALF * a + P * (t + 1)],
+                    lhsT_scale=w1_scales(b, a, t),
                     rhs=v_w[a][:, js].bitcast(FP8X4), rhs_scale=v_s[a][:, js],
                     start=(a == passes[0]), stop=(a == passes[1]),
                 )
@@ -250,22 +258,21 @@ def tile_list_deflated_slots_kernel(
         gather_words(0)
         for a in range(2):
             nc.vector.tensor_copy(v_s[a][:], tab_s[:, a, :].indirect(idx[:]))
-        for i in (1, 2):
-            pages.append(at("page%d" % i, [P, T2], F32, "page%d" % i))
-            nc.gpsimd.memset(pages[i][:], 0.0)
         rounded = [at("round0", [P, 4 * HALF], BF16, "rounded0%d" % a, skip=4 * KB * a) for a in range(2)]
         round_w1(0, 0, rounded[0][:])
         for t in (0, 2):
             round_w1(0, 1, rounded[1][:], t, t + 2)
         load_given(0)
-        deal_w2(0)
+        deal_words(0)
+        deal_scales(0)
         quantise(w1_w[0][:, :HALF], w1_s[0][:, :HALF], rounded[0][:])
         third = slice(HALF, HALF + QUARTER)
         fourth = slice(HALF + QUARTER, 2 * HALF)
         quantise(w1_w[0][:, third], w1_s[0][:, third], rounded[1][:, : 2 * HALF])
         gather_words(1, 0, HALF)
         gather_words(1, HALF, HALF)
-        quantise(w1_w[0][:, fourth], w1_s[0][:, fourth], rounded[1][:, 2 * HALF :])
+        last_scales = at("tab1", [P, QUARTER], U8, "last_scales")
+        quantise(w1_w[0][:, fourth], last_scales[:], rounded[1][:, 2 * HALF :])
 
         d_of[0], h_of[0] = rows("d0", "d_rows0"), rows("h0", "h_rows0")
         first, second = halves
@@ -296,10 +303,11 @@ def tile_list_deflated_slots_kernel(
             scatter(1, js.start, HALF)
         pick(0, "s3")
         w2_w[1] = at("raw3", [P, 2, 2 * HALF], U8, "w2_w1", skip=4 * KB)
-        w2_s[1] = at("raw3", [P, 2, HALF], U8, "w2_s1", skip=6 * KB)
-        deal_w2(1)
+        w2_s[1] = at("raw3", [P, 2, HALF], U8, "w2_s1", skip=7 * KB)
+        deal_words(1)
+        deal_scales(1)
         w1_w[1] = at("raw2", [P, 2 * HALF], U32, "w1_w1")
-        w1_s[1] = at("late_words", [P, 2 * HALF], U8, "w1_s1", skip=3 * HALF)
+        w1_s[1] = at("raw3", [P, 2 * HALF], U8, "w1_s1", skip=6 * KB)
         for a in range(2):
             quantise(w1_w[1][:, halves[a]], w1_s[1][:, halves[a]], late[a][:])
         scatter(2)
@@ -327,7 +335,9 @@ def tile_list_deflated_slots_kernel(
                 pick(3, "x4")
                 pick(4, "x5")
             if i == 3:
-                pick(6, "w_hi")
+                x_of[6] = rows("w_hi", "x6")
+                for js in halves:
+                    fetch(6, x_of[6], js.start, HALF)
 
         r_of[4] = rows("s6", "r4")
         invert(x_of[4], rows("z0", "u4"), r_of[4], halves)
@@ -354,7 +364,8 @@ def tile_list_deflated_slots_kernel(
         z_w = [at("z_rows", [P, M], U32, "z_w0"), kept([P, M], U32, "z_w1")]
         z_s = [kept([P, M], U8, "z_s%d" % b) for b in range(2)]
         x_of[7] = rows("d0", "x7")
-        fetch(7, x_of[7], 0, HALF)
+        for ms in quarters[:2]:
+            fetch(7, x_of[7], ms.start, QUARTER)
         quantise(z_w[0][:], z_s[0][:], z_bf[0][:].rearrange("p m t -> p (m t)"))
         y_banks = {}
 

@@ -25,7 +25,7 @@ KB = 1024
 PLACES = [
     ("page0", 8), ("page1", 8), ("page2", 8), ("spare", 8), ("raw0", 8), ("raw1", 8), ("raw2", 8), ("raw3", 8),
     ("round0", 8), ("d0", 4), ("w_lo", 4), ("w_hi", 4), ("s1", 4), ("s2", 4),
-    ("s3", 4), ("s4", 4), ("s5", 4), ("s6", 4), ("s7", 4), ("x4", 2), ("d6", 2), ("x5", 4), ("h0", 4), ("h1", 4), ("w5_raw", 4), ("z0", 8), ("z_rows", 8), ("tab0", 8), ("tab1", 8),
+    ("s3", 4), ("s4", 4), ("s5", 4), ("s7", 4), ("x4", 2), ("d6", 2), ("x5", 4), ("h0", 4), ("h1", 4), ("w5_raw", 4), ("z0", 8), ("z_rows", 8), ("tab0", 8), ("tab1", 8), ("d_first", 2),
 ]
 
 
@@ -96,23 +96,30 @@ def tile_list_deflated_slots_kernel(
             )
             w1_raw[(b, a)] = raw
 
-        beta_t = kept([P, 2, 4], F32, "beta_t")
+        def load_w1_columns(a, g):
+            raw = at("raw%d" % g, [P, 4, QUARTER], F32, "w1_raw0%d%d" % (a, g), skip=4 * KB * a)
+            nc.sync.dma_start(
+                out=raw[:],
+                in_=w1[512 * a : 512 * (a + 1), QUARTER * g : QUARTER * (g + 1)].rearrange("(p i) c -> p i c", i=4),
+            )
+            w1_raw[(0, a, g)] = raw
+
+        beta_t = [kept([P, 4], F32, "beta%d" % b) for b in range(2)]
+        wgs_plain = kept([P, S], F32, "wgs_plain")[:]
         wgs_t = [kept([P, S], F32, "wgs%d" % t)[:] for t in range(4)]
         wgs_rows = wgs.rearrange("(p t) j -> p t j", t=4)
 
-        def load_wgs(t):
+        def load_wgs(t, js=slice(0, S)):
             for q in (0, 2, 1, 3):
-                nc.sync.dma_start(out=wgs_t[t][32 * q : 32 * (q + 1), :], in_=wgs_rows[:, t, :])
+                nc.sync.dma_start(out=wgs_t[t][32 * q : 32 * (q + 1), js], in_=wgs_rows[:, t, js])
 
         given_t = {}
 
         def load_given(b):
             for u in range(2):
-                g = at((("raw0", "raw1"), ("spare", "tab1"))[b][u], [P, 2, M], F32, "given%d%d" % (b, u))
-                nc.sync.dma_start(
-                    out=g[:],
-                    in_=given[512 * b : 512 * (b + 1), :].rearrange("(p t) m -> p t m", t=4)[:, 2 * u : 2 * u + 2, :],
-                )
+                g = at((("spare", "tab0"), ("raw1", "tab1"))[b][u], [P, 2, M], F32, "given%d%d" % (b, u))
+                block = given[512 * b : 512 * (b + 1), :].rearrange(("(t p) m -> p t m", "(p t) m -> p t m")[b], t=4)
+                nc.sync.dma_start(out=g[:], in_=block[:, 2 * u : 2 * u + 2, :])
                 for e in range(2):
                     given_t[4 * b + 2 * u + e] = g[:, e, :]
 
@@ -121,39 +128,42 @@ def tile_list_deflated_slots_kernel(
         load_tab_words(0)
         nc.sync.dma_start(idx[:], offs)
         load_scale_rows(tab_s, tab_scales)
-        load_w1(0, 0)
+        load_w1_columns(0, 0)
         load_w2_words(0)
         load_scale_rows(w_s_raw[0], w2_scales[:, :, :HALF])
-        load_w1(0, 1)
+        load_w1_columns(1, 0)
+        load_w1_columns(0, 1)
         load_tab_words(1)
-        nc.sync.dma_start(out=beta_t[:], in_=beta.rearrange("(b p t) -> p b t", b=2, t=4))
+        nc.sync.dma_start(out=beta_t[0][:], in_=beta[:HALF].rearrange("(t p) -> p t", t=4))
+        load_w1_columns(1, 1)
+        nc.sync.dma_start(out=wgs_plain, in_=wgs)
         nc.sync.dma_start(idx2[:], offs2)
-        load_wgs(0)
         nc.sync.dma_start(idx3[:], offs3)
-        load_wgs(1)
         load_w1(1, 0)
         load_w2_words(1)
         load_scale_rows(w_s_raw[1], w2_scales[:, :, HALF:])
         load_scale_rows(w_s_raw[1], w5_scales, row=4)
         load_w1(1, 1)
-        nc.sync.dma_start(out=w5_w_raw[:], in_=w5_words.rearrange("a p c i -> p a (c i)").bitcast(I32))
-        load_wgs(2)
-        load_wgs(3)
+        nc.sync.dma_start(out=beta_t[1][:], in_=beta[HALF:].rearrange("(p t) -> p t", t=4))
 
         v_w = [kept([P, S], U32, "v_w%d" % a) for a in range(2)]
 
         def gather_words(a, j0=0, w=S):
             nc.vector.tensor_copy(v_w[a][:, j0 : j0 + w], tab_w[a][:].bitcast(U32).indirect(idx[:, j0 // 16 : (j0 + w) // 16]))
 
-        w1_w = {0: kept([P, 2 * HALF], U32, "w1_w0")}
-        w1_s = {0: kept([P, 2 * HALF], U8, "w1_s0")}
-        w2_w = {0: kept([P, 2, 2 * HALF], U8, "w2_w0")}
-        w2_s = {0: kept([P, 2, HALF], U8, "w2_s0")}
+        w1_w, w1_s = {}, {}
+        w2_w, w2_s = {0: w2_w_raw[0]}, {0: w_s_raw[0]}
 
-        def round_w1(b, a, out, t0=0, t1=4):
+        def round_columns(a, g, out):
             nc.scalar.copy(
-                out=out.rearrange("p (t m i) -> p m t i", t=4, i=4)[:, :, t0:t1, :],
-                in_=w1_raw[(b, a)][:].rearrange("p i (m t) -> p m t i", t=4)[:, :, t0:t1, :],
+                out=out.rearrange("p (c j i) -> p c i j", j=4, i=4),
+                in_=w1_raw[(0, a, g)][:].rearrange("p i (c j) -> p c i j", j=4),
+            )
+
+        def round_w1(b, a, out):
+            nc.scalar.copy(
+                out=out.rearrange("p (t m i) -> p m t i", t=4, i=4),
+                in_=w1_raw[(b, a)][:].rearrange("p i (m t) -> p m t i", t=4),
             )
 
         def quantise(words, scales, values):
@@ -174,14 +184,11 @@ def tile_list_deflated_slots_kernel(
         halves = [slice(0, HALF), slice(HALF, S)]
         a_of, d_of, t_of, h_of, x_of, r_of = {}, {}, {}, {}, {}, {}
 
-        def w1_scales(b, a, t):
-            if (b, a) == (0, 1) and t >= 2:
-                return last_scales[:, P * (t - 2) : P * (t - 1)]
-            return w1_s[b][:, HALF * a + P * t : HALF * a + P * (t + 1)]
-
-        def products(i, h):
+        def products(i, h, d_rows):
             b, t = divmod(i, 4)
             cols = slice(P * t, P * (t + 1))
+            group = min(i // 2, 2)
+            w1_cols = cols if b else slice(P * (t % 2), P * (t % 2 + 1))
             js = halves[h]
             bank = 4 * (i % 2) + 2 * h
             passes = (0, 1) if i == 0 else (1, 0)
@@ -198,18 +205,18 @@ def tile_list_deflated_slots_kernel(
             for a in passes:
                 nc.tensor.matmul_mx(
                     out=acc_a[:],
-                    lhsT=w1_w[b][:, HALF * a + P * t : HALF * a + P * (t + 1)].bitcast(FP8X4),
-                    lhsT_scale=w1_scales(b, a, t),
+                    lhsT=w1_w[group][:, a, w1_cols].bitcast(FP8X4),
+                    lhsT_scale=last_scales[:, w1_cols] if (group, a) == (1, 1) else w1_s[group][:, a, w1_cols],
                     rhs=v_w[a][:, js].bitcast(FP8X4), rhs_scale=v_s[a][:, js],
                     start=(a == passes[0]), stop=(a == passes[1]),
                 )
-            nc.scalar.activation(out=d_of[i][:, js], in_=acc_d[:], func=ACT.Copy, scale=beta_t[:, b, t : t + 1])
+            nc.scalar.activation(out=d_rows, in_=acc_d[:], func=ACT.Copy, scale=beta_t[b][:, t : t + 1])
             return acc_a
 
         def multiply(i, a_rows, d_rows):
             a_of[i], d_of[i] = a_rows, d_rows
             for h in range(2):
-                nc.scalar.copy(out=a_of[i][:, halves[h]], in_=products(i, h)[:])
+                nc.scalar.copy(out=a_of[i][:, halves[h]], in_=products(i, h, d_rows[:, halves[h]])[:])
 
         def deflate(i, t_rows, js=slice(0, S)):
             t_of[i] = t_rows
@@ -217,7 +224,7 @@ def tile_list_deflated_slots_kernel(
 
         def weigh(i, h_rows, js=slice(0, S)):
             h_of[i] = h_rows
-            nc.gpsimd.tensor_tensor(h_of[i][:, js], t_of[i][:, js], wgs_t[i % 4][:, js], ALU.mult)
+            nc.gpsimd.tensor_tensor(h_of[i][:, js], t_of[i][:, js], (wgs_plain if i < 4 else wgs_t[i - 4])[:, js], ALU.mult)
 
         def scatter(i, j0=0, w=S):
             nc.vector.tensor_copy(pages[i % 3][:].indirect(idx2[:, j0 // 16 : (j0 + w) // 16]), h_of[i][:, j0 : j0 + w])
@@ -240,8 +247,13 @@ def tile_list_deflated_slots_kernel(
         z_rows = at("z_rows", [P, 4, M], BF16, "z_rows")
 
         def damp(i, ms=slice(0, M)):
-            out = z_rows[:, i, ms] if i < 4 else z_bf[1][:, ms, i - 4]
-            nc.gpsimd.tensor_tensor(out, r_of[i][:, ms], given_t[i][:, ms], ALU.mult)
+            if i < 4:
+                plain = at("raw0", [P, M], BF16, "z_plain%d" % i, skip=2 * KB * i)
+                nc.gpsimd.tensor_tensor(plain[:], r_of[i], given_t[i], ALU.mult)
+                for t in range(4):
+                    nc.sync.dma_start(out=z_rows[32 * i : 32 * (i + 1), t, :], in_=plain[t:P:4, :])
+            else:
+                nc.gpsimd.tensor_tensor(z_bf[1][:, ms, i - 4], r_of[i][:, ms], given_t[i][:, ms], ALU.mult)
 
         def pick(i, place):
             x_of[i] = rows(place, "x%d" % i)
@@ -258,31 +270,37 @@ def tile_list_deflated_slots_kernel(
         gather_words(0)
         for a in range(2):
             nc.vector.tensor_copy(v_s[a][:], tab_s[:, a, :].indirect(idx[:]))
-        rounded = [at("round0", [P, 4 * HALF], BF16, "rounded0%d" % a, skip=4 * KB * a) for a in range(2)]
-        round_w1(0, 0, rounded[0][:])
-        for t in (0, 2):
-            round_w1(0, 1, rounded[1][:], t, t + 2)
-        load_given(0)
-        deal_words(0)
-        deal_scales(0)
-        quantise(w1_w[0][:, :HALF], w1_s[0][:, :HALF], rounded[0][:])
-        third = slice(HALF, HALF + QUARTER)
-        fourth = slice(HALF + QUARTER, 2 * HALF)
-        quantise(w1_w[0][:, third], w1_s[0][:, third], rounded[1][:, : 2 * HALF])
+        for g in range(2):
+            w1_w[g] = kept([P, 2, QUARTER], U32, "w1_w%d" % g)
+            w1_s[g] = kept([P, 2, QUARTER], U8, "w1_s%d" % g)
+        for n, (a, g) in enumerate(((0, 0), (1, 0), (0, 1))):
+            rounded = at("round0", [P, 4 * QUARTER], BF16, "rounded%d" % n, skip=2 * KB * n)
+            round_columns(a, g, rounded[:])
+            quantise(w1_w[g][:, a, :], w1_s[g][:, a, :], rounded[:])
         gather_words(1, 0, HALF)
         gather_words(1, HALF, HALF)
-        last_scales = at("tab1", [P, QUARTER], U8, "last_scales")
-        quantise(w1_w[0][:, fourth], last_scales[:], rounded[1][:, 2 * HALF :])
+        load_given(0)
+        for t in range(4):
+            load_wgs(t)
+        nc.sync.dma_start(out=w5_w_raw[:], in_=w5_words.rearrange("a p c i -> p a (c i)").bitcast(I32))
 
-        d_of[0], h_of[0] = rows("d0", "d_rows0"), rows("h0", "h_rows0")
+        rounded = at("round0", [P, QUARTER, 4], BF16, "rounded3", skip=6 * KB)
+        nc.gpsimd.tensor_scalar(
+            rounded[:], w1_raw[(0, 1, 1)][:].rearrange("p i c -> p c i"), 1.0, 0.0, ALU.mult, ALU.add
+        )
         first, second = halves
-        nc.vector.tensor_tensor(h_of[0][:, first], products(0, 0)[:], d_of[0][:, first], ALU.subtract)
-        nc.vector.tensor_tensor(h_of[0][:, first], h_of[0][:, first], wgs_t[0][:, first], ALU.mult)
+        h_of[0] = rows("h0", "h_rows0")
+        d_first = at("d_first", [P, HALF], F32, "d_first")
+        nc.vector.tensor_tensor(h_of[0][:, first], products(0, 0, d_first[:])[:], d_first[:], ALU.subtract)
+        last_scales = at("d_first", [P, QUARTER], U8, "last_scales")
+        quantise(w1_w[1][:, 1, :], last_scales[:], rounded[:].rearrange("p c i -> p (c i)"))
+        nc.vector.tensor_tensor(h_of[0][:, first], h_of[0][:, first], wgs_plain[:, first], ALU.mult)
         scatter(0, 0, HALF)
         a_half = at("w_hi", [P, HALF], F32, "a_half")
-        nc.scalar.copy(out=a_half[:], in_=products(0, 1)[:])
-        nc.gpsimd.tensor_tensor(d_of[0][:, second], a_half[:], d_of[0][:, second], ALU.subtract)
-        nc.gpsimd.tensor_tensor(h_of[0][:, second], d_of[0][:, second], wgs_t[0][:, second], ALU.mult)
+        d_half = at("d0", [P, HALF], F32, "d_half", skip=2 * KB)
+        nc.scalar.copy(out=a_half[:], in_=products(0, 1, d_half[:])[:])
+        nc.gpsimd.tensor_tensor(d_half[:], a_half[:], d_half[:], ALU.subtract)
+        nc.gpsimd.tensor_tensor(h_of[0][:, second], d_half[:], wgs_plain[:, second], ALU.mult)
         scatter(0, HALF, HALF)
 
         multiply(1, rows("w_lo", "a_rows1"), rows("s2", "d_rows1"))
@@ -291,7 +309,7 @@ def tile_list_deflated_slots_kernel(
         t_rows1, h_rows1 = at("d0", [P, HALF], F32, "t_rows1", skip=2 * KB), rows("h1", "h_rows1")
         for js in halves:
             nc.gpsimd.tensor_tensor(t_rows1[:], a_of[1][:, js], d_of[1][:, js], ALU.subtract)
-            nc.gpsimd.tensor_tensor(h_rows1[:, js], t_rows1[:], wgs_t[1][:, js], ALU.mult)
+            nc.gpsimd.tensor_tensor(h_rows1[:, js], t_rows1[:], wgs_plain[:, js], ALU.mult)
         h_of[1] = h_rows1
         multiply(2, rows("s1", "a_rows2"), rows("s3", "d_rows2"))
         late.append(at("w_lo", [P, 4 * HALF], BF16, "rounded11"))
@@ -299,47 +317,47 @@ def tile_list_deflated_slots_kernel(
         deflate(2, rows("d0", "t_rows2"))
         weigh(2, rows("raw3", "h_rows2"))
         multiply(3, rows("s4", "a_rows3"), rows("s5", "d_rows3"))
-        for js in halves:
-            scatter(1, js.start, HALF)
-        pick(0, "s3")
+        scatter(1, 0, HALF)
+        pick(0, "s2")
+        scatter(1, HALF, HALF)
         w2_w[1] = at("raw3", [P, 2, 2 * HALF], U8, "w2_w1", skip=4 * KB)
         w2_s[1] = at("raw3", [P, 2, HALF], U8, "w2_s1", skip=7 * KB)
         deal_words(1)
         deal_scales(1)
-        w1_w[1] = at("raw2", [P, 2 * HALF], U32, "w1_w1")
-        w1_s[1] = at("raw3", [P, 2 * HALF], U8, "w1_s1", skip=6 * KB)
+        w1_w[2] = at("raw2", [P, 2, HALF], U32, "w1_w2")
+        w1_s[2] = at("raw3", [P, 2, HALF], U8, "w1_s2", skip=6 * KB)
         for a in range(2):
-            quantise(w1_w[1][:, halves[a]], w1_s[1][:, halves[a]], late[a][:])
+            quantise(w1_w[2][:, a, :], w1_s[2][:, a, :], late[a][:])
         scatter(2)
         load_given(1)
         deflate(3, rows("d0", "t_rows3", skip=2 * KB))
         weigh(3, rows("h0", "h_rows3"))
         pick(1, "s5")
 
-        a_place = {3: "s4", 4: "s2", 5: "w_lo", 6: "s3", 7: "s6"}
-        d_place = {4: "s1", 5: "d6", 6: "s7", 7: "z0"}
+        a_place = {3: "s4", 4: "s3", 5: "s4", 6: "s3", 7: "s4"}
+        d_place = {4: "d6", 5: "s1", 6: "s7", 7: "z0"}
         h_place = {4: "h1", 5: "raw3", 6: "h0"}
+        multiply(4, rows(a_place[4], "a_rows4"), rows(d_place[4], "d_rows4"))
         for i in range(4):
-            multiply(i + 4, rows(a_place[i + 4], "a_rows%d" % (i + 4)), rows(d_place[i + 4], "d_rows%d" % (i + 4)))
             invert_into(i, a_place[i + 3])
             damp(i)
+            if i < 3:
+                multiply(i + 5, rows(a_place[i + 5], "a_rows%d" % (i + 5)), rows(d_place[i + 5], "d_rows%d" % (i + 5)))
             scatter(i + 3)
-            if i == 2:
-                pick(5, "raw3")
+            if i in (1, 2):
+                pick(i + 3, h_place[i + 3])
             deflate(i + 4, rows("d0", "t_rows%d" % (i + 4)))
             if i < 3:
                 weigh(i + 4, rows(h_place[i + 4], "h_rows%d" % (i + 4)))
             if i == 0:
-                pick(2, "s1")
-            if i == 1:
-                pick(3, "x4")
-                pick(4, "x5")
+                pick(2, "x4")
+                pick(3, "x5")
             if i == 3:
                 x_of[6] = rows("w_hi", "x6")
                 for js in halves:
                     fetch(6, x_of[6], js.start, HALF)
 
-        r_of[4] = rows("s6", "r4")
+        r_of[4] = rows("s4", "r4")
         invert(x_of[4], rows("z0", "u4"), r_of[4], halves)
         z_bf[0] = at("z0", [P, M, 4], BF16, "z_bf0")
         nc.scalar.copy(
@@ -349,7 +367,7 @@ def tile_list_deflated_slots_kernel(
         damp(4)
         weigh(7, rows("z_rows", "h_rows7"))
         invert_back(5, halves)
-        w5_w = at("s6", [P, 2, N], I32, "w5_w")
+        w5_w = at("s4", [P, 2, N], I32, "w5_w")
         nc.gpsimd.tensor_copy(
             out=w5_w[:].rearrange("p a (t m) -> p a t m", t=4),
             in_=w5_w_raw[:].rearrange("p a (m t) -> p a t m", t=4),

@@ -25,7 +25,7 @@ KB = 1024
 PLACES = [
     ("page0", 8), ("page1", 8), ("page2", 8), ("spare", 8), ("raw0", 8), ("raw1", 8), ("raw2", 8), ("raw3", 8),
     ("round0", 8), ("d0", 4), ("w_lo", 4), ("w_hi", 4), ("s1", 4), ("s2", 4),
-    ("s3", 4), ("s4", 4), ("s5", 4), ("s7", 4), ("x4", 2), ("d6", 2), ("x5", 4), ("h0", 4), ("h1", 4), ("w5_raw", 4), ("z0", 8), ("z_rows", 8), ("tab0", 8), ("tab1", 8), ("d_first", 2),
+    ("s3", 4), ("s4", 4), ("s5", 4), ("s7", 4), ("x4", 2), ("d6", 2), ("x5", 4), ("h0", 4), ("h1", 4), ("w5_raw", 4), ("z0", 8), ("z_rows", 8), ("tab0", 8), ("tab1", 8),
 ]
 
 
@@ -253,7 +253,8 @@ def tile_list_deflated_slots_kernel(
                 for t in range(4):
                     nc.sync.dma_start(out=z_rows[32 * i : 32 * (i + 1), t, :], in_=plain[t:P:4, :])
             else:
-                nc.gpsimd.tensor_tensor(z_bf[1][:, ms, i - 4], r_of[i][:, ms], given_t[i][:, ms], ALU.mult)
+                engine = nc.gpsimd if i < 7 else nc.vector
+                engine.tensor_tensor(z_late[:, i - 4, ms], r_of[i][:, ms], given_t[i][:, ms], ALU.mult)
 
         def pick(i, place):
             x_of[i] = rows(place, "x%d" % i)
@@ -284,29 +285,30 @@ def tile_list_deflated_slots_kernel(
             load_wgs(t)
         nc.sync.dma_start(out=w5_w_raw[:], in_=w5_words.rearrange("a p c i -> p a (c i)").bitcast(I32))
 
-        rounded = at("round0", [P, QUARTER, 4], BF16, "rounded3", skip=6 * KB)
+        rounded = at("h0", [P, QUARTER, 4], BF16, "rounded3")
         nc.gpsimd.tensor_scalar(
             rounded[:], w1_raw[(0, 1, 1)][:].rearrange("p i c -> p c i"), 1.0, 0.0, ALU.mult, ALU.add
         )
-        first, second = halves
-        h_of[0] = rows("h0", "h_rows0")
-        d_first = at("d_first", [P, HALF], F32, "d_first")
-        nc.vector.tensor_tensor(h_of[0][:, first], products(0, 0, d_first[:])[:], d_first[:], ALU.subtract)
-        last_scales = at("d_first", [P, QUARTER], U8, "last_scales")
+        last_scales = at("tab1", [P, QUARTER], U8, "last_scales")
         quantise(w1_w[1][:, 1, :], last_scales[:], rounded[:].rearrange("p c i -> p (c i)"))
-        nc.vector.tensor_tensor(h_of[0][:, first], h_of[0][:, first], wgs_plain[:, first], ALU.mult)
+        first, second = halves
+        d_first = at("d0", [P, HALF], F32, "d_first")
+        nc.vector.tensor_tensor(d_first[:], products(0, 0, d_first[:])[:], d_first[:], ALU.subtract)
+        h_of[0] = rows("h0", "h_rows0")
+        nc.vector.tensor_tensor(h_of[0][:, first], d_first[:], wgs_plain[:, first], ALU.mult)
         scatter(0, 0, HALF)
         a_half = at("w_hi", [P, HALF], F32, "a_half")
         d_half = at("d0", [P, HALF], F32, "d_half", skip=2 * KB)
         nc.scalar.copy(out=a_half[:], in_=products(0, 1, d_half[:])[:])
-        nc.gpsimd.tensor_tensor(d_half[:], a_half[:], d_half[:], ALU.subtract)
-        nc.gpsimd.tensor_tensor(h_of[0][:, second], d_half[:], wgs_plain[:, second], ALU.mult)
+        t_half = at("d0", [P, HALF], F32, "t_half")
+        nc.gpsimd.tensor_tensor(t_half[:], a_half[:], d_half[:], ALU.subtract)
+        nc.gpsimd.tensor_tensor(h_of[0][:, second], t_half[:], wgs_plain[:, second], ALU.mult)
         scatter(0, HALF, HALF)
 
         multiply(1, rows("w_lo", "a_rows1"), rows("s2", "d_rows1"))
         late = [at("w_hi", [P, 4 * HALF], BF16, "rounded10")]
         round_w1(1, 0, late[0][:])
-        t_rows1, h_rows1 = at("d0", [P, HALF], F32, "t_rows1", skip=2 * KB), rows("h1", "h_rows1")
+        t_rows1, h_rows1 = at("d0", [P, HALF], F32, "t_rows1"), rows("h1", "h_rows1")
         for js in halves:
             nc.gpsimd.tensor_tensor(t_rows1[:], a_of[1][:, js], d_of[1][:, js], ALU.subtract)
             nc.gpsimd.tensor_tensor(h_rows1[:, js], t_rows1[:], wgs_plain[:, js], ALU.mult)
@@ -353,9 +355,7 @@ def tile_list_deflated_slots_kernel(
                 pick(2, "x4")
                 pick(3, "x5")
             if i == 3:
-                x_of[6] = rows("w_hi", "x6")
-                for js in halves:
-                    fetch(6, x_of[6], js.start, HALF)
+                pick(6, "w_hi")
 
         r_of[4] = rows("s4", "r4")
         invert(x_of[4], rows("z0", "u4"), r_of[4], halves)
@@ -364,6 +364,7 @@ def tile_list_deflated_slots_kernel(
             out=z_bf[0][:].rearrange("p (c i) t -> p c t i", i=4),
             in_=z_rows[:].rearrange("p t (c i) -> p c t i", i=4),
         )
+        z_late = at("s1", [P, 4, M], BF16, "z_late")
         damp(4)
         weigh(7, rows("z_rows", "h_rows7"))
         invert_back(5, halves)
@@ -374,8 +375,7 @@ def tile_list_deflated_slots_kernel(
         )
         damp(5)
         invert_back(6, halves)
-        for js in halves:
-            damp(6, js)
+        damp(6)
         scatter(7)
 
         quarters = [slice(QUARTER * q, QUARTER * (q + 1)) for q in range(4)]
@@ -436,6 +436,11 @@ def tile_list_deflated_slots_kernel(
             invert(x_of[7], u7, r_of[7], [quarters[q] for q in pair])
             for q in pair:
                 damp(7, quarters[q])
+            for q in pair:
+                nc.vector.tensor_copy(
+                    out=z_bf[1][:, quarters[q], :].rearrange("p (c i) t -> p c t i", i=4),
+                    in_=z_late[:, :, quarters[q]].rearrange("p t (c i) -> p c t i", i=4),
+                )
             for q in pair:
                 ms = quarters[q]
                 quantise(z_w[1][:, ms], z_s[1][:, ms], z_bf[1][:, ms, :].rearrange("p m t -> p (m t)"))

@@ -176,7 +176,7 @@ def tile_list_deflated_slots_kernel(
             )
 
         def deal_scales(b):
-            nc.vector.tensor_copy(
+            nc.gpsimd.tensor_copy(
                 out=w2_s[b][:].rearrange("p a (t m) -> p a t m", t=4),
                 in_=w_s_raw[b][:].rearrange("p a (m t) -> p a t m", t=4),
             )
@@ -256,8 +256,8 @@ def tile_list_deflated_slots_kernel(
                 engine = nc.gpsimd if i < 7 else nc.vector
                 engine.tensor_tensor(z_late[:, i - 4, ms], r_of[i][:, ms], given_t[i][:, ms], ALU.mult)
 
-        def pick(i, place):
-            x_of[i] = rows(place, "x%d" % i)
+        def pick(i, place, skip=0):
+            x_of[i] = rows(place, "x%d" % i, skip)
             fetch(i, x_of[i])
 
         def invert_into(i, place):
@@ -323,47 +323,52 @@ def tile_list_deflated_slots_kernel(
         pick(0, "s2")
         scatter(1, HALF, HALF)
         w2_w[1] = at("raw3", [P, 2, 2 * HALF], U8, "w2_w1", skip=4 * KB)
-        w2_s[1] = at("raw3", [P, 2, HALF], U8, "w2_s1", skip=7 * KB)
         deal_words(1)
-        deal_scales(1)
         w1_w[2] = at("raw2", [P, 2, HALF], U32, "w1_w2")
         w1_s[2] = at("raw3", [P, 2, HALF], U8, "w1_s2", skip=6 * KB)
         for a in range(2):
             quantise(w1_w[2][:, a, :], w1_s[2][:, a, :], late[a][:])
         scatter(2)
         load_given(1)
+        w2_s[1] = at("w_lo", [P, 2, HALF], U8, "w2_s1", skip=3 * KB)
+        deal_scales(1)
         deflate(3, rows("d0", "t_rows3", skip=2 * KB))
         weigh(3, rows("h0", "h_rows3"))
         pick(1, "s5")
 
         a_place = {3: "s4", 4: "s3", 5: "s4", 6: "s3", 7: "s4"}
-        d_place = {4: "d6", 5: "s1", 6: "s7", 7: "z0"}
+        d_place = {4: "d6", 5: "s1", 6: "s7", 7: "s2"}
         h_place = {4: "h1", 5: "raw3", 6: "h0"}
-        multiply(4, rows(a_place[4], "a_rows4"), rows(d_place[4], "d_rows4"))
+        invert_into(0, a_place[3])
+        damp(0)
         for i in range(4):
-            invert_into(i, a_place[i + 3])
-            damp(i)
-            if i < 3:
-                multiply(i + 5, rows(a_place[i + 5], "a_rows%d" % (i + 5)), rows(d_place[i + 5], "d_rows%d" % (i + 5)))
+            if i == 2:
+                for done in (2, 3):
+                    invert_into(done, a_place[done + 1])
+                    damp(done)
+            multiply(i + 4, rows(a_place[i + 4], "a_rows%d" % (i + 4)), rows(d_place[i + 4], "d_rows%d" % (i + 4)))
             scatter(i + 3)
-            if i in (1, 2):
-                pick(i + 3, h_place[i + 3])
             deflate(i + 4, rows("d0", "t_rows%d" % (i + 4)))
             if i < 3:
                 weigh(i + 4, rows(h_place[i + 4], "h_rows%d" % (i + 4)))
             if i == 0:
+                invert_into(1, a_place[4])
+                damp(1)
                 pick(2, "x4")
                 pick(3, "x5")
+            if i == 2:
+                pick(4, "tab0")
+                pick(5, "tab0", 4 * KB)
             if i == 3:
                 pick(6, "w_hi")
 
-        r_of[4] = rows("s4", "r4")
-        invert(x_of[4], rows("z0", "u4"), r_of[4], halves)
         z_bf[0] = at("z0", [P, M, 4], BF16, "z_bf0")
         nc.scalar.copy(
             out=z_bf[0][:].rearrange("p (c i) t -> p c t i", i=4),
             in_=z_rows[:].rearrange("p t (c i) -> p c t i", i=4),
         )
+        r_of[4] = rows("s4", "r4")
+        invert(x_of[4], rows("z_rows", "u4", skip=4 * KB), r_of[4], halves)
         z_late = at("s1", [P, 4, M], BF16, "z_late")
         damp(4)
         weigh(7, rows("z_rows", "h_rows7"))

@@ -23,9 +23,10 @@ ROOT = 75.0 / 64.0
 KB = 1024
 
 PLACES = [
-    ("page0", 8), ("page1", 8), ("page2", 8), ("spare", 8), ("raw0", 8), ("raw1", 8), ("raw2", 8), ("raw3", 8),
-    ("round0", 8), ("d0", 4), ("w_lo", 4), ("w_hi", 4), ("s1", 4), ("s2", 4),
-    ("s3", 4), ("s4", 4), ("s5", 4), ("s7", 4), ("x4", 2), ("d6", 2), ("x5", 4), ("h0", 4), ("h1", 4), ("w5_raw", 4), ("z0", 8), ("z_rows", 8), ("tab0", 8), ("tab1", 8),
+    ("page0", 8), ("page1", 8), ("tab0", 8), ("tab1", 8), ("raw0", 8), ("raw1", 8), ("rawb0", 8), ("rawb1", 8),
+    ("round0", 4), ("round1", 4), ("roundb", 8), ("a0", 4), ("a1", 4), ("d0", 4), ("d1", 4),
+    ("e2", 2), ("xb", 4), ("w1b", 4), ("w2b", 2), ("s2b", 1), ("xc", 4), ("e6", 6), ("xa", 4), ("w1g", 2), ("xd", 4), ("z0a", 3),
+    ("h0", 4), ("h1", 4), ("h2", 4), ("given0", 8), ("given1", 8),
 ]
 
 
@@ -54,9 +55,21 @@ def tile_list_deflated_slots_kernel(
         def rows(place, name, skip=0):
             return at(place, [P, S], F32, name, skip)[:]
 
+        halves = [slice(0, HALF), slice(HALF, S)]
+        quarters = [slice(QUARTER * q, QUARTER * (q + 1)) for q in range(4)]
+
         idx = kept([P, S // 16], U16, "idx")
         idx2 = kept([P, S // 16], U16, "idx2")
         idx3 = kept([P, M // 16], U16, "idx3")
+
+        tab_s = kept([P, T], U8, "tab_s")
+        v_s = [kept([P, S], U8, "v_s%d" % a) for a in range(2)]
+        w_s_raw = [kept([P, 2, HALF], U8, "w_s_raw%d" % b) for b in range(2)]
+        pages = [at("page%d" % i, [P, T2], F32, "page%d" % i) for i in range(2)]
+        for cleared in (tab_s, w_s_raw[0], v_s[1], w_s_raw[1]):
+            nc.vector.memset(cleared[:].bitcast(I32), 0)
+        for page in pages:
+            nc.vector.memset(page[:], 0.0)
 
         def load_scale_rows(plane, scales, row=0):
             for r in range(4):
@@ -65,22 +78,9 @@ def tile_list_deflated_slots_kernel(
                     in_=scales[:, r:16:4, :].rearrange("a q c -> q a c").bitcast(I32),
                 )
 
-        tab_s = at("spare", [P, 2, T], U8, "tab_s")
-        v_s = [kept([P, S], U8, "v_s%d" % a) for a in range(2)]
-        w_s_raw = [kept([P, 2, HALF], U8, "w_s_raw0"), kept([P, 2, HALF], U8, "w_s_raw1")]
-        nc.vector.memset(tab_s[:].bitcast(I32), 0)
-        nc.vector.memset(w_s_raw[0][:].bitcast(I32), 0)
-        nc.vector.memset(w_s_raw[1][:].bitcast(I32), 0)
-        pages = [at("page%d" % i, [P, T2], F32, "page%d" % i) for i in range(3)]
-        for page in pages:
-            nc.vector.memset(page[:], 0.0)
-
-        tab_w = [at("tab0", [P, T], I32, "tab_w0"), at("tab1", [P, T], I32, "tab_w1")]
-        w2_w_raw = [kept([P, 2, 2 * HALF], U8, "w2_w_raw0"), kept([P, 2, 2 * HALF], U8, "w2_w_raw1")]
+        tab_w = [at("tab%d" % a, [P, T], I32, "tab_w%d" % a) for a in range(2)]
+        w2_w_raw = [kept([P, 2, 2 * HALF], U8, "w2_w_raw%d" % b) for b in range(2)]
         w1_raw = {}
-
-        def load_tab_words(a):
-            nc.sync.dma_start(out=tab_w[a][:], in_=tab_words[a].rearrange("p t i -> p (t i)").bitcast(I32))
 
         def load_w2_words(b):
             nc.sync.dma_start(
@@ -88,101 +88,81 @@ def tile_list_deflated_slots_kernel(
                 in_=w2_words[:, :, 1024 * b : 1024 * (b + 1)].rearrange("a p c -> p a c").bitcast(I32),
             )
 
-        def load_w1(b, a):
-            raw = at("raw%d" % (2 * b + a), [P, 4, HALF], F32, "w1_raw%d%d" % (b, a))
+        def load_w1(group, a):
+            c0, width = ((0, QUARTER), (QUARTER, QUARTER), (HALF, HALF))[group]
+            place, skip = (("raw0", 4 * KB * a), ("raw1", 4 * KB * a), ("rawb%d" % a, 0))[group]
+            raw = at(place, [P, 4, width], F32, "w1_raw%d%d" % (group, a), skip)
             nc.sync.dma_start(
-                out=raw[:],
-                in_=w1[512 * a : 512 * (a + 1), 512 * b : 512 * (b + 1)].rearrange("(p i) c -> p i c", i=4),
+                out=raw[:], in_=w1[512 * a : 512 * (a + 1), c0 : c0 + width].rearrange("(p i) c -> p i c", i=4)
             )
-            w1_raw[(b, a)] = raw
-
-        def load_w1_columns(a, g):
-            raw = at("raw%d" % g, [P, 4, QUARTER], F32, "w1_raw0%d%d" % (a, g), skip=4 * KB * a)
-            nc.sync.dma_start(
-                out=raw[:],
-                in_=w1[512 * a : 512 * (a + 1), QUARTER * g : QUARTER * (g + 1)].rearrange("(p i) c -> p i c", i=4),
-            )
-            w1_raw[(0, a, g)] = raw
+            w1_raw[(group, a)] = raw
 
         beta_t = [kept([P, 4], F32, "beta%d" % b) for b in range(2)]
         wgs_plain = kept([P, S], F32, "wgs_plain")[:]
         wgs_t = [kept([P, S], F32, "wgs%d" % t)[:] for t in range(4)]
         wgs_rows = wgs.rearrange("(p t) j -> p t j", t=4)
-
-        def load_wgs(t, js=slice(0, S)):
-            for q in (0, 2, 1, 3):
-                nc.sync.dma_start(out=wgs_t[t][32 * q : 32 * (q + 1), js], in_=wgs_rows[:, t, js])
-
         given_t = {}
 
         def load_given(b):
             for u in range(2):
-                g = at((("spare", "tab0"), ("raw1", "tab1"))[b][u], [P, 2, M], F32, "given%d%d" % (b, u))
+                g = at(("given%d", "tab%d")[b] % u, [P, 2, M], F32, "given%d%d" % (b, u))
                 block = given[512 * b : 512 * (b + 1), :].rearrange(("(t p) m -> p t m", "(p t) m -> p t m")[b], t=4)
                 nc.sync.dma_start(out=g[:], in_=block[:, 2 * u : 2 * u + 2, :])
                 for e in range(2):
                     given_t[4 * b + 2 * u + e] = g[:, e, :]
 
-        w5_w_raw = at("w5_raw", [P, 2, N], I32, "w5_w_raw")
-
-        load_tab_words(0)
         nc.sync.dma_start(idx[:], offs)
-        load_scale_rows(tab_s, tab_scales)
-        load_w1_columns(0, 0)
-        load_w2_words(0)
-        load_scale_rows(w_s_raw[0], w2_scales[:, :, :HALF])
-        load_w1_columns(1, 0)
-        load_w1_columns(0, 1)
-        load_tab_words(1)
-        nc.sync.dma_start(out=beta_t[0][:], in_=beta[:HALF].rearrange("(t p) -> p t", t=4))
-        load_w1_columns(1, 1)
-        nc.sync.dma_start(out=wgs_plain, in_=wgs)
         nc.sync.dma_start(idx2[:], offs2)
-        nc.sync.dma_start(idx3[:], offs3)
+        for r in range(4):
+            nc.sync.dma_start(out=tab_s[r:P:32, :].bitcast(I32), in_=tab_scales[0, r:16:4, :].bitcast(I32))
+        nc.sync.dma_start(out=tab_s[4:P:8, :].bitcast(I32), in_=tab_scales[1].bitcast(I32))
+        for a in range(2):
+            nc.sync.dma_start(out=tab_w[a][:], in_=tab_words[a].rearrange("p t i -> p (t i)").bitcast(I32))
+        load_scale_rows(w_s_raw[0], w2_scales[:, :, :HALF])
+        load_w2_words(0)
+        load_w1(0, 0)
+        load_w1(0, 1)
+        nc.sync.dma_start(out=beta_t[0][:], in_=beta[:HALF].rearrange("(t p) -> p t", t=4))
+        nc.sync.dma_start(out=wgs_plain, in_=wgs)
         load_w1(1, 0)
+        load_w1(1, 1)
+        nc.sync.dma_start(idx3[:], offs3)
+        load_w1(2, 0)
+        load_w1(2, 1)
         load_w2_words(1)
         load_scale_rows(w_s_raw[1], w2_scales[:, :, HALF:])
         load_scale_rows(w_s_raw[1], w5_scales, row=4)
-        load_w1(1, 1)
         nc.sync.dma_start(out=beta_t[1][:], in_=beta[HALF:].rearrange("(p t) -> p t", t=4))
+        load_given(0)
+        for t in range(4):
+            for q in (0, 2, 1, 3):
+                nc.sync.dma_start(out=wgs_t[t][32 * q : 32 * (q + 1), :], in_=wgs_rows[:, t, :])
+        w5_w_raw = kept([P, 2, N], I32, "w5_w_raw")
+        nc.sync.dma_start(out=w5_w_raw[:], in_=w5_words.rearrange("a p c i -> p a (c i)").bitcast(I32))
 
         v_w = [kept([P, S], U32, "v_w%d" % a) for a in range(2)]
 
-        def gather_words(a, j0=0, w=S):
-            nc.vector.tensor_copy(v_w[a][:, j0 : j0 + w], tab_w[a][:].bitcast(U32).indirect(idx[:, j0 // 16 : (j0 + w) // 16]))
-
-        w1_w, w1_s = {}, {}
-        w2_w, w2_s = {0: w2_w_raw[0]}, {0: w_s_raw[0]}
-
-        def round_columns(a, g, out):
-            nc.scalar.copy(
-                out=out.rearrange("p (c j i) -> p c i j", j=4, i=4),
-                in_=w1_raw[(0, a, g)][:].rearrange("p i (c j) -> p c i j", j=4),
-            )
-
-        def round_w1(b, a, out):
-            nc.scalar.copy(
-                out=out.rearrange("p (t m i) -> p m t i", t=4, i=4),
-                in_=w1_raw[(b, a)][:].rearrange("p i (m t) -> p m t i", t=4),
-            )
+        def gather_words(a, js):
+            nc.vector.tensor_copy(v_w[a][:, js], tab_w[a][:].bitcast(U32).indirect(idx[:, js.start // 16 : js.stop // 16]))
 
         def quantise(words, scales, values):
             nc.vector.quantize_mx(out=words.bitcast(FP8X4), scales=scales, in_=values)
 
-        def deal_words(b):
-            nc.vector.tensor_copy(
-                out=w2_w[b][:].bitcast(U16).rearrange("p a (t m) -> p a t m", t=4),
-                in_=w2_w_raw[b][:].bitcast(U16).rearrange("p a (m t) -> p a t m", t=4),
+        def round_plain(group, a, cs, out):
+            nc.scalar.copy(
+                out=out.rearrange("p (c j i) -> p c i j", j=4, i=4),
+                in_=w1_raw[(group, a)][:, :, cs].rearrange("p i (c j) -> p c i j", j=4),
             )
 
-        def deal_scales(b):
-            nc.gpsimd.tensor_copy(
-                out=w2_s[b][:].rearrange("p a (t m) -> p a t m", t=4),
-                in_=w_s_raw[b][:].rearrange("p a (m t) -> p a t m", t=4),
+        def round_dealt(a, out):
+            nc.scalar.copy(
+                out=out.rearrange("p (t m i) -> p m t i", t=4, i=4),
+                in_=w1_raw[(2, a)][:].rearrange("p i (m t) -> p m t i", t=4),
             )
 
-        halves = [slice(0, HALF), slice(HALF, S)]
-        a_of, d_of, t_of, h_of, x_of, r_of = {}, {}, {}, {}, {}, {}
+        w1_w, w1_s = {}, {}
+        w2_w, w2_s = {0: w2_w_raw[0]}, {0: w_s_raw[0]}
+        a_of, d_of, t_of, h_of, x_of = {}, {}, {}, {}, {}
 
         def products(i, h, d_rows):
             b, t = divmod(i, 4)
@@ -191,7 +171,7 @@ def tile_list_deflated_slots_kernel(
             w1_cols = cols if b else slice(P * (t % 2), P * (t % 2 + 1))
             js = halves[h]
             bank = 4 * (i % 2) + 2 * h
-            passes = (0, 1) if i == 0 else (1, 0)
+            passes = (0, 1) if (i, h) == (0, 0) else (1, 0)
             acc_d = psum.tile([P, HALF], F32, name="bank%d" % bank)
             acc_a = psum.tile([P, HALF], F32, name="bank%d" % (bank + 1))
             for a in passes:
@@ -206,193 +186,207 @@ def tile_list_deflated_slots_kernel(
                 nc.tensor.matmul_mx(
                     out=acc_a[:],
                     lhsT=w1_w[group][:, a, w1_cols].bitcast(FP8X4),
-                    lhsT_scale=last_scales[:, w1_cols] if (group, a) == (1, 1) else w1_s[group][:, a, w1_cols],
+                    lhsT_scale=w1_s[group][:, a, w1_cols],
                     rhs=v_w[a][:, js].bitcast(FP8X4), rhs_scale=v_s[a][:, js],
                     start=(a == passes[0]), stop=(a == passes[1]),
                 )
             nc.scalar.activation(out=d_rows, in_=acc_d[:], func=ACT.Copy, scale=beta_t[b][:, t : t + 1])
             return acc_a
 
-        def multiply(i, a_rows, d_rows):
-            a_of[i], d_of[i] = a_rows, d_rows
+        def multiply(i, d_place, skip=0):
+            a_of[i] = rows("a%d" % (i % 2), "a_rows%d" % i)
+            d_of[i] = rows(d_place, "d_rows%d" % i, skip)
             for h in range(2):
-                nc.scalar.copy(out=a_of[i][:, halves[h]], in_=products(i, h, d_rows[:, halves[h]])[:])
+                nc.scalar.copy(out=a_of[i][:, halves[h]], in_=products(i, h, d_of[i][:, halves[h]])[:])
 
-        def deflate(i, t_rows, js=slice(0, S)):
+        def deflate(i, t_rows, parts=(slice(0, S),)):
             t_of[i] = t_rows
-            nc.gpsimd.tensor_tensor(t_of[i][:, js], a_of[i][:, js], d_of[i][:, js], ALU.subtract)
+            for js in parts:
+                nc.gpsimd.tensor_tensor(t_rows[:, js], a_of[i][:, js], d_of[i][:, js], ALU.subtract)
 
-        def weigh(i, h_rows, js=slice(0, S)):
+        def weigh(i, h_rows, parts=(slice(0, S),)):
             h_of[i] = h_rows
-            nc.gpsimd.tensor_tensor(h_of[i][:, js], t_of[i][:, js], (wgs_plain if i < 4 else wgs_t[i - 4])[:, js], ALU.mult)
-
-        def scatter(i, j0=0, w=S):
-            nc.vector.tensor_copy(pages[i % 3][:].indirect(idx2[:, j0 // 16 : (j0 + w) // 16]), h_of[i][:, j0 : j0 + w])
-
-        def fetch(i, x, m0=0, w=M):
-            nc.vector.tensor_copy(x[:, m0 : m0 + w], pages[i % 3][:].indirect(idx3[:, m0 // 16 : (m0 + w) // 16]))
-
-        def invert(x, u, r, parts):
+            weights = wgs_plain if i < 4 else wgs_t[i - 4]
             for js in parts:
-                nc.scalar.activation(out=u[:, js], in_=x[:, js], func=ACT.Square)
-            for js in parts:
+                nc.gpsimd.tensor_tensor(h_rows[:, js], t_of[i][:, js], weights[:, js], ALU.mult)
+
+        def put(i, js, values):
+            nc.vector.tensor_copy(pages[i % 2][:].indirect(idx2[:, js.start // 16 : js.stop // 16]), values)
+
+        def scatter(i, js):
+            put(i, js, h_of[i][:, js])
+
+        def fetch(i, ms):
+            nc.vector.tensor_copy(x_of[i][:, ms], pages[i % 2][:].indirect(idx3[:, ms.start // 16 : ms.stop // 16]))
+
+        def invert(i, u, parts):
+            x = x_of[i]
+            for ms in parts:
+                nc.scalar.activation(out=u[:, ms], in_=x[:, ms], func=ACT.Square)
+            for ms in parts:
                 nc.scalar.activation(
-                    out=u[:, js], in_=u[:, js], func=ACT.Abs_reciprocal_sqrt, scale=ROOT * ROOT, bias=ROOT * ROOT
+                    out=u[:, ms], in_=u[:, ms], func=ACT.Abs_reciprocal_sqrt, scale=ROOT * ROOT, bias=ROOT * ROOT
                 )
-            for js in parts:
-                nc.scalar.activation(out=r[:, js], in_=u[:, js], func=ACT.Square, scale=ROOT)
+            for ms in parts:
+                nc.scalar.activation(out=x[:, ms], in_=u[:, ms], func=ACT.Square, scale=ROOT)
 
-        z_bf = {1: kept([P, M, 4], BF16, "z_bf1")}
+        def damp(i, out, ms=slice(0, M)):
+            engine = nc.gpsimd if i < 7 else nc.vector
+            engine.tensor_tensor(out[:, ms], x_of[i][:, ms], given_t[i][:, ms], ALU.mult)
 
-        z_rows = at("z_rows", [P, 4, M], BF16, "z_rows")
+        def damp_plain(i, place, skip):
+            plain = at(place, [P, M], BF16, "z_plain%d" % i, skip)
+            damp(i, plain[:])
+            for t in range(4):
+                nc.sync.dma_start(out=z_rows[32 * i : 32 * (i + 1), t, :], in_=plain[t:P:4, :])
 
-        def damp(i, ms=slice(0, M)):
-            if i < 4:
-                plain = at("raw0", [P, M], BF16, "z_plain%d" % i, skip=2 * KB * i)
-                nc.gpsimd.tensor_tensor(plain[:], r_of[i], given_t[i], ALU.mult)
-                for t in range(4):
-                    nc.sync.dma_start(out=z_rows[32 * i : 32 * (i + 1), t, :], in_=plain[t:P:4, :])
-            else:
-                engine = nc.gpsimd if i < 7 else nc.vector
-                engine.tensor_tensor(z_late[:, i - 4, ms], r_of[i][:, ms], given_t[i][:, ms], ALU.mult)
+        def place_and_pick(i, place):
+            scatter(i, halves[0])
+            x_of[i - 1] = rows(place, "x%d" % (i - 1))
+            fetch(i - 1, slice(0, M))
+            scatter(i, halves[1])
 
-        def pick(i, place, skip=0):
-            x_of[i] = rows(place, "x%d" % i, skip)
-            fetch(i, x_of[i])
-
-        def invert_into(i, place):
-            r_of[i] = rows(place, "r%d" % i)
-            invert(x_of[i], r_of[i], r_of[i], halves)
-
-        def invert_back(i, parts):
-            r_of[i] = x_of[i]
-            invert(x_of[i], rows("z_rows", "u%d" % i, skip=4 * KB), r_of[i], parts)
-
-        gather_words(0)
-        for a in range(2):
-            nc.vector.tensor_copy(v_s[a][:], tab_s[:, a, :].indirect(idx[:]))
-        for g in range(2):
-            w1_w[g] = kept([P, 2, QUARTER], U32, "w1_w%d" % g)
-            w1_s[g] = kept([P, 2, QUARTER], U8, "w1_s%d" % g)
-        for n, (a, g) in enumerate(((0, 0), (1, 0), (0, 1))):
-            rounded = at("round0", [P, 4 * QUARTER], BF16, "rounded%d" % n, skip=2 * KB * n)
-            round_columns(a, g, rounded[:])
-            quantise(w1_w[g][:, a, :], w1_s[g][:, a, :], rounded[:])
-        gather_words(1, 0, HALF)
-        gather_words(1, HALF, HALF)
-        load_given(0)
-        for t in range(4):
-            load_wgs(t)
-        nc.sync.dma_start(out=w5_w_raw[:], in_=w5_words.rearrange("a p c i -> p a (c i)").bitcast(I32))
-
-        rounded = at("h0", [P, QUARTER, 4], BF16, "rounded3")
-        nc.gpsimd.tensor_scalar(
-            rounded[:], w1_raw[(0, 1, 1)][:].rearrange("p i c -> p c i"), 1.0, 0.0, ALU.mult, ALU.add
-        )
-        last_scales = at("tab1", [P, QUARTER], U8, "last_scales")
-        quantise(w1_w[1][:, 1, :], last_scales[:], rounded[:].rearrange("p c i -> p (c i)"))
+        nc.vector.tensor_copy(v_s[0][:], tab_s[:].indirect(idx[:]))
+        for r in range(4):
+            nc.gpsimd.dma_start(out=v_s[1][r:P:32, :].bitcast(I32), in_=v_s[0][4 + 8 * r : P : 32, :].bitcast(I32))
+        gather_words(0, slice(0, S))
+        gather_words(1, halves[0])
+        gather_words(1, halves[1])
+        load_given(1)
+        w1_w[0] = kept([P, 2, QUARTER], U32, "w1_w0")
+        w1_s[0] = kept([P, 2, QUARTER], U8, "w1_s0")
+        rounded = at("round0", [P, 4 * QUARTER], BF16, "rounded00")
+        round_plain(0, 0, slice(0, QUARTER), rounded[:])
+        quantise(w1_w[0][:, 0, :], w1_s[0][:, 0, :], rounded[:])
+        rounded = at("round0", [P, 4 * P], BF16, "rounded010", skip=2 * KB)
+        round_plain(0, 1, slice(0, P), rounded[:])
+        quantise(w1_w[0][:, 1, :P], w1_s[0][:, 1, :P], rounded[:])
         first, second = halves
-        d_first = at("d0", [P, HALF], F32, "d_first")
-        nc.vector.tensor_tensor(d_first[:], products(0, 0, d_first[:])[:], d_first[:], ALU.subtract)
+        d_first = at("xa", [P, HALF], F32, "d_first", skip=3 * KB)
+        acc_first = products(0, 0, d_first[:])
+        rounded = at("h0", [P, 4 * P], BF16, "rounded011")
+        round_plain(0, 1, slice(P, QUARTER), rounded[:])
+        nc.vector.tensor_tensor(d_first[:], acc_first[:], d_first[:], ALU.subtract)
+        quantise(w1_w[0][:, 1, P:], w1_s[0][:, 1, P:], rounded[:])
         h_of[0] = rows("h0", "h_rows0")
         nc.vector.tensor_tensor(h_of[0][:, first], d_first[:], wgs_plain[:, first], ALU.mult)
-        scatter(0, 0, HALF)
-        a_half = at("w_hi", [P, HALF], F32, "a_half")
-        d_half = at("d0", [P, HALF], F32, "d_half", skip=2 * KB)
+        scatter(0, first)
+        a_half = at("round1", [P, HALF], F32, "a_half")
+        d_half = at("d0", [P, HALF], F32, "d_half")
         nc.scalar.copy(out=a_half[:], in_=products(0, 1, d_half[:])[:])
-        t_half = at("d0", [P, HALF], F32, "t_half")
+        t_half = at("xa", [P, HALF], F32, "t_half0", skip=3 * KB)
         nc.gpsimd.tensor_tensor(t_half[:], a_half[:], d_half[:], ALU.subtract)
         nc.gpsimd.tensor_tensor(h_of[0][:, second], t_half[:], wgs_plain[:, second], ALU.mult)
-        scatter(0, HALF, HALF)
+        scatter(0, second)
 
-        multiply(1, rows("w_lo", "a_rows1"), rows("s2", "d_rows1"))
-        late = [at("w_hi", [P, 4 * HALF], BF16, "rounded10")]
-        round_w1(1, 0, late[0][:])
-        t_rows1, h_rows1 = at("d0", [P, HALF], F32, "t_rows1"), rows("h1", "h_rows1")
-        for js in halves:
-            nc.gpsimd.tensor_tensor(t_rows1[:], a_of[1][:, js], d_of[1][:, js], ALU.subtract)
-            nc.gpsimd.tensor_tensor(h_rows1[:, js], t_rows1[:], wgs_plain[:, js], ALU.mult)
-        h_of[1] = h_rows1
-        multiply(2, rows("s1", "a_rows2"), rows("s3", "d_rows2"))
-        late.append(at("w_lo", [P, 4 * HALF], BF16, "rounded11"))
-        round_w1(1, 1, late[1][:])
-        deflate(2, rows("d0", "t_rows2"))
-        weigh(2, rows("raw3", "h_rows2"))
-        multiply(3, rows("s4", "a_rows3"), rows("s5", "d_rows3"))
-        scatter(1, 0, HALF)
-        pick(0, "s2")
-        scatter(1, HALF, HALF)
-        w2_w[1] = at("raw3", [P, 2, 2 * HALF], U8, "w2_w1", skip=4 * KB)
-        deal_words(1)
-        w1_w[2] = at("raw2", [P, 2, HALF], U32, "w1_w2")
-        w1_s[2] = at("raw3", [P, 2, HALF], U8, "w1_s2", skip=6 * KB)
+        multiply(1, "d1")
+        rounded = at("round1", [P, 2, 4 * QUARTER], BF16, "rounded1")
         for a in range(2):
-            quantise(w1_w[2][:, a, :], w1_s[2][:, a, :], late[a][:])
-        scatter(2)
-        load_given(1)
-        w2_s[1] = at("w_lo", [P, 2, HALF], U8, "w2_s1", skip=3 * KB)
-        deal_scales(1)
-        deflate(3, rows("d0", "t_rows3", skip=2 * KB))
-        weigh(3, rows("h0", "h_rows3"))
-        pick(1, "s5")
-
-        a_place = {3: "s4", 4: "s3", 5: "s4", 6: "s3", 7: "s4"}
-        d_place = {4: "d6", 5: "s1", 6: "s7", 7: "s2"}
-        h_place = {4: "h1", 5: "raw3", 6: "h0"}
-        invert_into(0, a_place[3])
-        damp(0)
-        for i in range(4):
-            if i == 2:
-                for done in (2, 3):
-                    invert_into(done, a_place[done + 1])
-                    damp(done)
-            multiply(i + 4, rows(a_place[i + 4], "a_rows%d" % (i + 4)), rows(d_place[i + 4], "d_rows%d" % (i + 4)))
-            scatter(i + 3)
-            deflate(i + 4, rows("d0", "t_rows%d" % (i + 4)))
-            if i < 3:
-                weigh(i + 4, rows(h_place[i + 4], "h_rows%d" % (i + 4)))
-            if i == 0:
-                invert_into(1, a_place[4])
-                damp(1)
-                pick(2, "x4")
-                pick(3, "x5")
-            if i == 2:
-                pick(4, "tab0")
-                pick(5, "tab0", 4 * KB)
-            if i == 3:
-                pick(6, "w_hi")
-
-        z_bf[0] = at("z0", [P, M, 4], BF16, "z_bf0")
-        nc.scalar.copy(
-            out=z_bf[0][:].rearrange("p (c i) t -> p c t i", i=4),
-            in_=z_rows[:].rearrange("p t (c i) -> p c t i", i=4),
+            round_plain(1, a, slice(0, QUARTER), rounded[:, a, :])
+        h_of[1] = rows("raw1", "h_rows1", skip=2 * KB)
+        t_half = at("xa", [P, HALF], F32, "t_half1", skip=3 * KB)
+        nc.gpsimd.tensor_tensor(t_half[:], a_of[1][:, first], d_of[1][:, first], ALU.subtract)
+        nc.gpsimd.tensor_tensor(h_of[1][:, first], t_half[:], wgs_plain[:, first], ALU.mult)
+        w1_w[1] = at("w1g", [P, 2, QUARTER], U32, "w1_w1")
+        w1_s[1] = kept([P, 2, QUARTER], U8, "w1_s1")
+        quantise(
+            w1_w[1][:].rearrange("p a c -> p (a c)"), w1_s[1][:].rearrange("p a c -> p (a c)"),
+            rounded[:].rearrange("p a c -> p (a c)"),
         )
-        r_of[4] = rows("s4", "r4")
-        invert(x_of[4], rows("z_rows", "u4", skip=4 * KB), r_of[4], halves)
-        z_late = at("s1", [P, 4, M], BF16, "z_late")
-        damp(4)
-        weigh(7, rows("z_rows", "h_rows7"))
-        invert_back(5, halves)
-        w5_w = at("s4", [P, 2, N], I32, "w5_w")
+        t_half = at("round1", [P, HALF], F32, "t_half2")
+        nc.gpsimd.tensor_tensor(t_half[:], a_of[1][:, second], d_of[1][:, second], ALU.subtract)
+        nc.gpsimd.tensor_tensor(h_of[1][:, second], t_half[:], wgs_plain[:, second], ALU.mult)
+        place_and_pick(1, "xa")
+        multiply(2, "roundb")
+        multiply(3, "d1")
+        rounded = at("roundb", [P, 2, 4 * HALF], BF16, "rounded2")
+        for a in range(2):
+            round_dealt(a, rounded[:, a, :])
+        deflate(2, rows("xb", "t_rows2", skip=4 * KB - KB // 4))
+        weigh(2, rows("h2", "h_rows2"))
+        invert(0, rows("a0", "u0"), halves)
+        place_and_pick(2, "xb")
+        deflate(3, rows("w1b", "t_rows3", skip=3 * KB + KB // 2))
+        weigh(3, rows("rawb0", "h_rows3", skip=6 * KB))
+        invert(1, rows("a1", "u1"), halves)
+        w2_s[1] = at("s2b", [P, 2, HALF], U8, "w2_s1")
+        nc.gpsimd.tensor_copy(
+            out=w2_s[1][:].rearrange("p a (t m) -> p a t m", t=4),
+            in_=w_s_raw[1][:].rearrange("p a (m t) -> p a t m", t=4),
+        )
+        w2_w[1] = at("w2b", [P, 2, 2 * HALF], U8, "w2_w1")
+        nc.vector.tensor_copy(
+            out=w2_w[1][:].bitcast(U16).rearrange("p a (t m) -> p a t m", t=4),
+            in_=w2_w_raw[1][:].bitcast(U16).rearrange("p a (m t) -> p a t m", t=4),
+        )
+        w1_w[2] = at("w1b", [P, 2, HALF], U32, "w1_w2")
+        w1_s[2] = kept([P, 2, HALF], U8, "w1_s2")
+        quantise(
+            w1_w[2][:].rearrange("p a c -> p (a c)"), w1_s[2][:].rearrange("p a c -> p (a c)"),
+            rounded[:].rearrange("p a c -> p (a c)"),
+        )
+        place_and_pick(3, "xc")
+
+        z_rows = at("rawb0", [P, 4, M], BF16, "z_rows")
+        multiply(4, "d0")
+        damp_plain(0, "roundb", 0)
+        deflate(4, rows("xa", "t_rows4"), halves)
+        weigh(4, rows("h1", "h_rows4"), halves)
+        multiply(5, "d1")
+        invert(2, rows("a0", "u2"), halves)
+        place_and_pick(4, "xa")
+        damp_plain(1, "d0", 0)
+        deflate(5, rows("e2", "t_rows5", skip=KB))
+        weigh(5, rows("h2", "h_rows5"))
+        multiply(6, "d0")
+        invert(3, rows("a1", "u3"), halves)
+        place_and_pick(5, "xb")
+        damp_plain(2, "e2", 0)
+        deflate(6, rows("xc", "t_rows6", skip=3 * KB))
+        weigh(6, rows("h0", "h_rows6"))
+        multiply(7, "e6", 2 * KB)
+        damp_plain(3, "e6", 0)
+        z_bf = [at("rawb1", [P, M, 4], BF16, "z_bf0")]
+        for ms in halves:
+            nc.scalar.copy(
+                out=z_bf[0][:, ms, :].rearrange("p (c i) t -> p c t i", i=4),
+                in_=z_rows[:, :, ms].rearrange("p t (c i) -> p c t i", i=4),
+            )
+        invert(4, rows("a0", "u4"), halves)
+        place_and_pick(6, "xc")
+        cut = (slice(0, QUARTER), slice(QUARTER, S))
+        t_last = (at("xd", [P, QUARTER], F32, "t_head7"), at("z0a", [P, S - QUARTER], F32, "t_rest7"))
+        h_last = (at("h1", [P, QUARTER], F32, "h_head7"), at("rawb0", [P, S - QUARTER], F32, "h_rest7"))
+        for part in range(2):
+            nc.gpsimd.tensor_tensor(t_last[part][:], a_of[7][:, cut[part]], d_of[7][:, cut[part]], ALU.subtract)
+        for part in range(2):
+            nc.gpsimd.tensor_tensor(h_last[part][:], t_last[part][:], wgs_t[3][:, cut[part]], ALU.mult)
+        z_late = at("given0", [P, 4, M], BF16, "z_late")
+        damp(4, z_late[:, 0, :])
+        invert(5, rows("rawb0", "u5", skip=4 * KB), halves)
+        w5_w = at("a1", [P, 2, N], I32, "w5_w")
         nc.gpsimd.tensor_copy(
             out=w5_w[:].rearrange("p a (t m) -> p a t m", t=4),
             in_=w5_w_raw[:].rearrange("p a (m t) -> p a t m", t=4),
         )
-        damp(5)
-        invert_back(6, halves)
-        damp(6)
-        scatter(7)
+        damp(5, z_late[:, 1, :])
+        put(7, cut[0], h_last[0][:])
+        x_of[6] = rows("xd", "x6")
+        for ms in halves:
+            fetch(6, ms)
+        put(7, cut[1], h_last[1][:])
+        u6 = rows("rawb0", "u6", skip=4 * KB)
+        for ms in halves:
+            invert(6, u6, [slice(ms.start, ms.start + QUARTER), slice(ms.start + QUARTER, ms.stop)])
+            damp(6, z_late[:, 2, :], ms)
 
-        quarters = [slice(QUARTER * q, QUARTER * (q + 1)) for q in range(4)]
-        z_w = [at("z_rows", [P, M], U32, "z_w0"), kept([P, M], U32, "z_w1")]
+        z_w = [[at("z0a", [P, HALF], U32, "z_w00"), at("rawb0", [P, HALF], U32, "z_w01")]]
+        z_w.append([kept([P, HALF], U32, "z_w1%d" % u) for u in range(2)])
         z_s = [kept([P, M], U8, "z_s%d" % b) for b in range(2)]
-        x_of[7] = rows("d0", "x7")
-        for ms in quarters[:2]:
-            fetch(7, x_of[7], ms.start, QUARTER)
-        quantise(z_w[0][:], z_s[0][:], z_bf[0][:].rearrange("p m t -> p (m t)"))
         y_banks = {}
 
         def last_stage(b, q):
+            part = quarters[q % 2]
             for u in range(2):
                 if b == 0:
                     y_banks[(q, u)] = psum.tile([P, 2, QUARTER], F32, name="bank%d" % (2 * q + u))
@@ -401,18 +395,25 @@ def tile_list_deflated_slots_kernel(
                     nc.tensor.matmul_mx(
                         out=y_banks[(q, u)][:, e, :],
                         lhsT=w5_w[:, b, cols].bitcast(FP8X4), lhsT_scale=w2_s[1][4:, b, cols],
-                        rhs=z_w[b][:, quarters[q]].bitcast(FP8X4), rhs_scale=z_s[b][:, quarters[q]],
+                        rhs=z_w[b][q // 2][:, part].bitcast(FP8X4), rhs_scale=z_s[b][:, quarters[q]],
                         start=(b == 0 and e == 0), stop=(b == 1 and e == 1),
                     )
 
-        for q in range(4):
-            last_stage(0, q)
+        def first_half_of_y(u):
+            quantise(z_w[0][u][:], z_s[0][:, halves[u]], z_bf[0][:, halves[u], :].rearrange("p m t -> p (m t)"))
+            for q in (2 * u, 2 * u + 1):
+                last_stage(0, q)
+
+        first_half_of_y(0)
+        x_of[7] = rows("xa", "x7")
+        for ms in quarters:
+            fetch(7, ms)
+        first_half_of_y(1)
 
         y_w = kept([P, M], I32, "y_w")
         y_s = kept([P, M], U8, "y_s")
         y_rows = out_0.rearrange("(p t) m -> p t m", t=4)
         words_out = out_1[0].rearrange("p m t -> p (m t)").bitcast(I32)
-
         y_bf = {}
 
         def finish(q):
@@ -420,7 +421,7 @@ def tile_list_deflated_slots_kernel(
             for u in range(2):
                 nc.scalar.copy(out=y[:, 2 * u : 2 * u + 2, :], in_=y_banks[(q, u)][:])
                 nc.sync.dma_start(out=y_rows[:, 2 * u : 2 * u + 2, quarters[q]], in_=y[:, 2 * u : 2 * u + 2, :])
-            y_bf[q] = at("round0", [P, QUARTER, 4], BF16, "y_bf%d" % q, skip=2 * KB * q)
+            y_bf[q] = at("roundb", [P, QUARTER, 4], BF16, "y_bf%d" % q, skip=2 * KB * q)
             nc.vector.tensor_copy(
                 out=y_bf[q][:].rearrange("p (c i) t -> p c t i", i=4),
                 in_=y[:].rearrange("p t (c i) -> p c t i", i=4),
@@ -433,22 +434,23 @@ def tile_list_deflated_slots_kernel(
                 done = slice(0, 3 * QUARTER) if q == 2 else ms
                 nc.sync.dma_start(out=words_out[:, done], in_=y_w[:, done])
 
-        fetch(7, x_of[7], HALF, HALF)
-        r_of[7] = x_of[7]
-        u7 = rows("z_rows", "u7", skip=4 * KB)
+        z_bf.append(at("given1", [P, M, 4], BF16, "z_bf1"))
+        u7 = rows("rawb0", "u7", skip=4 * KB)
         for u in range(2):
             pair = (2 * u, 2 * u + 1)
-            invert(x_of[7], u7, r_of[7], [quarters[q] for q in pair])
+            invert(7, u7, [quarters[q] for q in pair])
             for q in pair:
-                damp(7, quarters[q])
+                damp(7, z_late[:, 3, :], quarters[q])
             for q in pair:
                 nc.vector.tensor_copy(
                     out=z_bf[1][:, quarters[q], :].rearrange("p (c i) t -> p c t i", i=4),
                     in_=z_late[:, :, quarters[q]].rearrange("p t (c i) -> p c t i", i=4),
                 )
             for q in pair:
-                ms = quarters[q]
-                quantise(z_w[1][:, ms], z_s[1][:, ms], z_bf[1][:, ms, :].rearrange("p m t -> p (m t)"))
+                quantise(
+                    z_w[1][u][:, quarters[q % 2]], z_s[1][:, quarters[q]],
+                    z_bf[1][:, quarters[q], :].rearrange("p m t -> p (m t)"),
+                )
                 last_stage(1, q)
         for q in range(5):
             if q < 4:

@@ -24,7 +24,7 @@ KB = 1024
 
 PLACES = [
     ("page0", 8), ("page1", 8), ("tab0", 8), ("tab1", 8), ("raw0", 8), ("raw1", 8), ("rawb0", 8), ("rawb1", 8),
-    ("round0", 4), ("round1", 4), ("roundb", 8), ("a0", 4), ("a1", 4), ("d0", 4), ("d1", 4),
+    ("v_last", 2), ("round0", 1), ("round1", 4), ("roundb", 8), ("a0", 4), ("a1", 4), ("d0", 4), ("d1", 4),
     ("e2", 2), ("xb", 4), ("w1b", 4), ("w2b", 2), ("s2b", 1), ("xc", 4), ("e6", 6), ("xa", 4), ("w1g", 2), ("xd", 4), ("z0a", 3),
     ("h0", 4), ("h1", 4), ("h2", 4), ("given0", 8), ("given1", 8),
 ]
@@ -62,11 +62,11 @@ def tile_list_deflated_slots_kernel(
         idx2 = kept([P, S // 16], U16, "idx2")
         idx3 = kept([P, M // 16], U16, "idx3")
 
-        tab_s = kept([P, T], U8, "tab_s")
+        tab_s = [kept([P, T], U8, "tab_s%d" % a) for a in range(2)]
         v_s = [kept([P, S], U8, "v_s%d" % a) for a in range(2)]
         w_s_raw = [kept([P, 2, HALF], U8, "w_s_raw%d" % b) for b in range(2)]
         pages = [at("page%d" % i, [P, T2], F32, "page%d" % i) for i in range(2)]
-        for cleared in (tab_s, w_s_raw[0], v_s[1], w_s_raw[1]):
+        for cleared in (tab_s[0], tab_s[1], w_s_raw[0], w_s_raw[1]):
             nc.vector.memset(cleared[:].bitcast(I32), 0)
         for page in pages:
             nc.vector.memset(page[:], 0.0)
@@ -113,16 +113,20 @@ def tile_list_deflated_slots_kernel(
 
         nc.sync.dma_start(idx[:], offs)
         nc.sync.dma_start(idx2[:], offs2)
-        for r in range(4):
-            nc.sync.dma_start(out=tab_s[r:P:32, :].bitcast(I32), in_=tab_scales[0, r:16:4, :].bitcast(I32))
-        nc.sync.dma_start(out=tab_s[4:P:8, :].bitcast(I32), in_=tab_scales[1].bitcast(I32))
         for a in range(2):
+            for r in range(4):
+                nc.sync.dma_start(out=tab_s[a][r:P:32, :].bitcast(I32), in_=tab_scales[a, r:16:4, :].bitcast(I32))
             nc.sync.dma_start(out=tab_w[a][:], in_=tab_words[a].rearrange("p t i -> p (t i)").bitcast(I32))
         load_scale_rows(w_s_raw[0], w2_scales[:, :, :HALF])
         load_w2_words(0)
         load_w1(0, 0)
-        load_w1(0, 1)
-        nc.sync.dma_start(out=beta_t[0][:], in_=beta[:HALF].rearrange("(t p) -> p t", t=4))
+        w1_last = [at("raw0", [P, 4, P], F32, "w1_raw01%d" % t, skip=(4 + 2 * t) * KB) for t in range(2)]
+        for t in range(2):
+            nc.sync.dma_start(
+                out=w1_last[t][:], in_=w1[512:, P * t : P * (t + 1)].rearrange("(p i) c -> p i c", i=4)
+            )
+            if t == 0:
+                nc.sync.dma_start(out=beta_t[0][:], in_=beta[:HALF].rearrange("(t p) -> p t", t=4))
         nc.sync.dma_start(out=wgs_plain, in_=wgs)
         load_w1(1, 0)
         load_w1(1, 1)
@@ -140,18 +144,17 @@ def tile_list_deflated_slots_kernel(
         w5_w_raw = kept([P, 2, N], I32, "w5_w_raw")
         nc.sync.dma_start(out=w5_w_raw[:], in_=w5_words.rearrange("a p c i -> p a (c i)").bitcast(I32))
 
-        v_w = [kept([P, S], U32, "v_w%d" % a) for a in range(2)]
+        v_w = {}
 
-        def gather_words(a, js):
-            nc.vector.tensor_copy(v_w[a][:, js], tab_w[a][:].bitcast(U32).indirect(idx[:, js.start // 16 : js.stop // 16]))
+        def gather_words(a, js, out):
+            nc.vector.tensor_copy(out, tab_w[a][:].bitcast(U32).indirect(idx[:, js.start // 16 : js.stop // 16]))
 
         def quantise(words, scales, values):
             nc.vector.quantize_mx(out=words.bitcast(FP8X4), scales=scales, in_=values)
 
-        def round_plain(group, a, cs, out):
+        def round_plain(raw, out):
             nc.scalar.copy(
-                out=out.rearrange("p (c j i) -> p c i j", j=4, i=4),
-                in_=w1_raw[(group, a)][:, :, cs].rearrange("p i (c j) -> p c i j", j=4),
+                out=out.rearrange("p (c j i) -> p c i j", j=4, i=4), in_=raw.rearrange("p i (c j) -> p c i j", j=4)
             )
 
         def round_dealt(a, out):
@@ -172,14 +175,14 @@ def tile_list_deflated_slots_kernel(
             js = halves[h]
             bank = 4 * (i % 2) + 2 * h
             passes = (0, 1) if (i, h) == (0, 0) else (1, 0)
-            acc_d = psum.tile([P, HALF], F32, name="bank%d" % bank)
-            acc_a = psum.tile([P, HALF], F32, name="bank%d" % (bank + 1))
+            acc_d = psum.tile([P, HALF], F32, name="bank%d" % (bank if i > 1 else 0))
+            acc_a = psum.tile([P, HALF], F32, name="bank%d" % (bank + 1 if i > 1 or bank == 0 else bank))
             for a in passes:
                 nc.tensor.matmul_mx(
                     out=acc_d[:],
                     lhsT=w2_w[b][:, a, 2 * P * t : 2 * P * (t + 1)].bitcast(FP4X4),
                     lhsT_scale=w2_s[b][:, a, cols],
-                    rhs=v_w[a][:, js].bitcast(FP8X4), rhs_scale=v_s[a][:, js],
+                    rhs=v_w[(a, h)].bitcast(FP8X4), rhs_scale=v_s[a][:, js],
                     start=(a == passes[0]), stop=(a == passes[1]),
                 )
             for a in passes:
@@ -187,7 +190,7 @@ def tile_list_deflated_slots_kernel(
                     out=acc_a[:],
                     lhsT=w1_w[group][:, a, w1_cols].bitcast(FP8X4),
                     lhsT_scale=w1_s[group][:, a, w1_cols],
-                    rhs=v_w[a][:, js].bitcast(FP8X4), rhs_scale=v_s[a][:, js],
+                    rhs=v_w[(a, h)].bitcast(FP8X4), rhs_scale=v_s[a][:, js],
                     start=(a == passes[0]), stop=(a == passes[1]),
                 )
             nc.scalar.activation(out=d_rows, in_=acc_d[:], func=ACT.Copy, scale=beta_t[b][:, t : t + 1])
@@ -246,26 +249,33 @@ def tile_list_deflated_slots_kernel(
             fetch(i - 1, slice(0, M))
             scatter(i, halves[1])
 
-        nc.vector.tensor_copy(v_s[0][:], tab_s[:].indirect(idx[:]))
-        for r in range(4):
-            nc.gpsimd.dma_start(out=v_s[1][r:P:32, :].bitcast(I32), in_=v_s[0][4 + 8 * r : P : 32, :].bitcast(I32))
-        gather_words(0, slice(0, S))
-        gather_words(1, halves[0])
-        gather_words(1, halves[1])
-        load_given(1)
+        nc.vector.tensor_copy(v_s[0][:], tab_s[0][:].indirect(idx[:]))
+        v_first = kept([P, S], U32, "v_w0")
+        gather_words(0, slice(0, S), v_first[:])
+        for h in range(2):
+            v_w[(0, h)] = v_first[:, halves[h]]
+        nc.vector.tensor_copy(v_s[1][:], tab_s[1][:].indirect(idx[:]))
+        v_w[(1, 0)] = kept([P, HALF], U32, "v_w10")[:]
+        gather_words(1, halves[0], v_w[(1, 0)])
         w1_w[0] = kept([P, 2, QUARTER], U32, "w1_w0")
         w1_s[0] = kept([P, 2, QUARTER], U8, "w1_s0")
-        rounded = at("round0", [P, 4 * QUARTER], BF16, "rounded00")
-        round_plain(0, 0, slice(0, QUARTER), rounded[:])
-        quantise(w1_w[0][:, 0, :], w1_s[0][:, 0, :], rounded[:])
-        rounded = at("round0", [P, 4 * P], BF16, "rounded010", skip=2 * KB)
-        round_plain(0, 1, slice(0, P), rounded[:])
+        rounded = at("round0", [P, 4 * P], BF16, "rounded000")
+        round_plain(w1_raw[(0, 0)][:, :, :P], rounded[:])
+        quantise(w1_w[0][:, 0, :P], w1_s[0][:, 0, :P], rounded[:])
+        rounded = at("v_last", [P, 4 * P], BF16, "rounded010")
+        round_plain(w1_last[0][:], rounded[:])
         quantise(w1_w[0][:, 1, :P], w1_s[0][:, 1, :P], rounded[:])
+        v_w[(1, 1)] = at("v_last", [P, HALF], U32, "v_w11")[:]
+        gather_words(1, halves[1], v_w[(1, 1)])
+        load_given(1)
+        rounded = at("round0", [P, 4 * P], BF16, "rounded001")
+        round_plain(w1_raw[(0, 0)][:, :, P:], rounded[:])
+        quantise(w1_w[0][:, 0, P:], w1_s[0][:, 0, P:], rounded[:])
         first, second = halves
         d_first = at("xa", [P, HALF], F32, "d_first", skip=3 * KB)
         acc_first = products(0, 0, d_first[:])
         rounded = at("h0", [P, 4 * P], BF16, "rounded011")
-        round_plain(0, 1, slice(P, QUARTER), rounded[:])
+        round_plain(w1_last[1][:], rounded[:])
         nc.vector.tensor_tensor(d_first[:], acc_first[:], d_first[:], ALU.subtract)
         quantise(w1_w[0][:, 1, P:], w1_s[0][:, 1, P:], rounded[:])
         h_of[0] = rows("h0", "h_rows0")
@@ -282,7 +292,7 @@ def tile_list_deflated_slots_kernel(
         multiply(1, "d1")
         rounded = at("round1", [P, 2, 4 * QUARTER], BF16, "rounded1")
         for a in range(2):
-            round_plain(1, a, slice(0, QUARTER), rounded[:, a, :])
+            round_plain(w1_raw[(1, a)][:], rounded[:, a, :])
         h_of[1] = rows("raw1", "h_rows1", skip=2 * KB)
         t_half = at("xa", [P, HALF], F32, "t_half1", skip=3 * KB)
         nc.gpsimd.tensor_tensor(t_half[:], a_of[1][:, first], d_of[1][:, first], ALU.subtract)
@@ -338,7 +348,7 @@ def tile_list_deflated_slots_kernel(
         damp_plain(1, "d0", 0)
         deflate(5, rows("e2", "t_rows5", skip=KB))
         weigh(5, rows("h2", "h_rows5"))
-        multiply(6, "d0")
+        multiply(6, "roundb", 2 * KB)
         invert(3, rows("a1", "u3"), halves)
         place_and_pick(5, "xb")
         damp_plain(2, "e2", 0)

@@ -23,9 +23,9 @@ ROOT = 75.0 / 64.0
 KB = 1024
 
 PLACES = [
-    ("page0", 8), ("page1", 8), ("tab0", 8), ("tab1", 8), ("raw0", 8), ("raw1", 8), ("rawb0", 8), ("rawb1", 8),
+    ("page0", 8), ("page1", 8), ("page2", 8), ("tab0", 8), ("tab1", 8), ("raw0", 8), ("raw1", 8), ("rawb0", 8), ("rawb1", 8),
     ("v_last", 2), ("round0", 1), ("round1", 4), ("roundb", 8), ("a0", 4), ("a1", 4), ("d0", 4), ("d1", 4),
-    ("e2", 2), ("xb", 4), ("w1b", 4), ("w2b", 2), ("s2b", 1), ("xc", 4), ("e6", 6), ("xa", 4), ("w1g", 2), ("xd", 4), ("z0a", 3),
+    ("e2", 4), ("xb", 4), ("w1b", 4), ("w2b", 2), ("s2b", 1), ("xc", 4), ("xa", 4), ("w1g", 2), ("xd", 4), ("xe", 4),
     ("h0", 4), ("h1", 4), ("h2", 4), ("given0", 8), ("given1", 8),
 ]
 
@@ -62,7 +62,7 @@ def tile_list_deflated_slots_kernel(
         idx2 = kept([P, S // 16], U16, "idx2")
         idx3 = kept([P, M // 16], U16, "idx3")
 
-        tab_s = [kept([P, T], U8, "tab_s%d" % a) for a in range(2)]
+        tab_s = [at("page2", [P, T], U8, "tab_s0"), kept([P, T], U8, "tab_s1")]
         v_s = [kept([P, S], U8, "v_s%d" % a) for a in range(2)]
         w_s_raw = [kept([P, 2, HALF], U8, "w_s_raw%d" % b) for b in range(2)]
         pages = [at("page%d" % i, [P, T2], F32, "page%d" % i) for i in range(2)]
@@ -213,14 +213,11 @@ def tile_list_deflated_slots_kernel(
             for js in parts:
                 nc.gpsimd.tensor_tensor(h_rows[:, js], t_of[i][:, js], weights[:, js], ALU.mult)
 
-        def put(i, js, values):
-            nc.vector.tensor_copy(pages[i % 2][:].indirect(idx2[:, js.start // 16 : js.stop // 16]), values)
-
         def scatter(i, js):
-            put(i, js, h_of[i][:, js])
+            nc.vector.tensor_copy(pages[i % 3][:].indirect(idx2[:, js.start // 16 : js.stop // 16]), h_of[i][:, js])
 
         def fetch(i, ms):
-            nc.vector.tensor_copy(x_of[i][:, ms], pages[i % 2][:].indirect(idx3[:, ms.start // 16 : ms.stop // 16]))
+            nc.vector.tensor_copy(x_of[i][:, ms], pages[i % 3][:].indirect(idx3[:, ms.start // 16 : ms.stop // 16]))
 
         def invert(i, u, parts):
             x = x_of[i]
@@ -243,13 +240,17 @@ def tile_list_deflated_slots_kernel(
             for t in range(4):
                 nc.sync.dma_start(out=z_rows[32 * i : 32 * (i + 1), t, :], in_=plain[t:P:4, :])
 
+        def pick(i, place):
+            x_of[i] = rows(place, "x%d" % i)
+            fetch(i, slice(0, M))
+
         def place_and_pick(i, place):
-            scatter(i, halves[0])
-            x_of[i - 1] = rows(place, "x%d" % (i - 1))
-            fetch(i - 1, slice(0, M))
-            scatter(i, halves[1])
+            scatter(i, slice(0, S))
+            pick(i - 1, place)
 
         nc.vector.tensor_copy(v_s[0][:], tab_s[0][:].indirect(idx[:]))
+        pages.append(at("page2", [P, T2], F32, "page2"))
+        nc.gpsimd.memset(pages[2][:], 0.0)
         v_first = kept([P, S], U32, "v_w0")
         gather_words(0, slice(0, S), v_first[:])
         for h in range(2):
@@ -306,7 +307,9 @@ def tile_list_deflated_slots_kernel(
         t_half = at("round1", [P, HALF], F32, "t_half2")
         nc.gpsimd.tensor_tensor(t_half[:], a_of[1][:, second], d_of[1][:, second], ALU.subtract)
         nc.gpsimd.tensor_tensor(h_of[1][:, second], t_half[:], wgs_plain[:, second], ALU.mult)
-        place_and_pick(1, "xa")
+        scatter(1, first)
+        pick(0, "xa")
+        scatter(1, second)
         multiply(2, "roundb")
         multiply(3, "d1")
         rounded = at("roundb", [P, 2, 4 * HALF], BF16, "rounded2")
@@ -340,37 +343,35 @@ def tile_list_deflated_slots_kernel(
         z_rows = at("rawb0", [P, 4, M], BF16, "z_rows")
         multiply(4, "d0")
         damp_plain(0, "roundb", 0)
-        deflate(4, rows("xa", "t_rows4"), halves)
+        pick(3, "xa")
+        deflate(4, rows("xd", "t_rows4"), halves)
         weigh(4, rows("h1", "h_rows4"), halves)
         multiply(5, "d1")
         invert(2, rows("a0", "u2"), halves)
-        place_and_pick(4, "xa")
+        scatter(4, slice(0, S))
         damp_plain(1, "d0", 0)
         deflate(5, rows("e2", "t_rows5", skip=KB))
         weigh(5, rows("h2", "h_rows5"))
         multiply(6, "roundb", 2 * KB)
         invert(3, rows("a1", "u3"), halves)
         place_and_pick(5, "xb")
-        damp_plain(2, "e2", 0)
-        deflate(6, rows("xc", "t_rows6", skip=3 * KB))
+        pick(5, "xd")
+        damp_plain(2, "e2", 2 * KB)
+        damp_plain(3, "e2", 0)
+        deflate(6, rows("xc", "t_rows6", skip=2 * KB))
         weigh(6, rows("h0", "h_rows6"))
-        multiply(7, "e6", 2 * KB)
-        damp_plain(3, "e6", 0)
+        multiply(7, "d1")
         z_bf = [at("rawb1", [P, M, 4], BF16, "z_bf0")]
         for ms in halves:
             nc.scalar.copy(
                 out=z_bf[0][:, ms, :].rearrange("p (c i) t -> p c t i", i=4),
                 in_=z_rows[:, :, ms].rearrange("p t (c i) -> p c t i", i=4),
             )
-        invert(4, rows("a0", "u4"), halves)
-        place_and_pick(6, "xc")
-        cut = (slice(0, QUARTER), slice(QUARTER, S))
-        t_last = (at("xd", [P, QUARTER], F32, "t_head7"), at("z0a", [P, S - QUARTER], F32, "t_rest7"))
-        h_last = (at("h1", [P, QUARTER], F32, "h_head7"), at("rawb0", [P, S - QUARTER], F32, "h_rest7"))
-        for part in range(2):
-            nc.gpsimd.tensor_tensor(t_last[part][:], a_of[7][:, cut[part]], d_of[7][:, cut[part]], ALU.subtract)
-        for part in range(2):
-            nc.gpsimd.tensor_tensor(h_last[part][:], t_last[part][:], wgs_t[3][:, cut[part]], ALU.mult)
+        scatter(6, slice(0, S))
+        pick(6, "xe")
+        deflate(7, rows("xc", "t_rows7", skip=2 * KB))
+        weigh(7, rows("rawb0", "h_rows7"))
+        invert(4, rows("rawb0", "u4", skip=4 * KB), halves)
         z_late = at("given0", [P, 4, M], BF16, "z_late")
         damp(4, z_late[:, 0, :])
         invert(5, rows("rawb0", "u5", skip=4 * KB), halves)
@@ -380,17 +381,13 @@ def tile_list_deflated_slots_kernel(
             in_=w5_w_raw[:].rearrange("p a (m t) -> p a t m", t=4),
         )
         damp(5, z_late[:, 1, :])
-        put(7, cut[0], h_last[0][:])
-        x_of[6] = rows("xd", "x6")
-        for ms in halves:
-            fetch(6, ms)
-        put(7, cut[1], h_last[1][:])
+        scatter(7, slice(0, S))
         u6 = rows("rawb0", "u6", skip=4 * KB)
         for ms in halves:
             invert(6, u6, [slice(ms.start, ms.start + QUARTER), slice(ms.start + QUARTER, ms.stop)])
             damp(6, z_late[:, 2, :], ms)
 
-        z_w = [[at("z0a", [P, HALF], U32, "z_w00"), at("rawb0", [P, HALF], U32, "z_w01")]]
+        z_w = [[at("xc", [P, HALF], U32, "z_w00", skip=2 * KB), at("rawb0", [P, HALF], U32, "z_w01")]]
         z_w.append([kept([P, HALF], U32, "z_w1%d" % u) for u in range(2)])
         z_s = [kept([P, M], U8, "z_s%d" % b) for b in range(2)]
         y_banks = {}
@@ -416,7 +413,7 @@ def tile_list_deflated_slots_kernel(
 
         first_half_of_y(0)
         x_of[7] = rows("xa", "x7")
-        for ms in quarters:
+        for ms in halves:
             fetch(7, ms)
         first_half_of_y(1)
 

@@ -24,7 +24,7 @@ KB = 1024
 
 PLACES = [
     ("page0", 8), ("page1", 8), ("page2", 8), ("tab0", 8), ("tab1", 8), ("raw0", 8), ("raw1", 8), ("rawb0", 8), ("rawb1", 8),
-    ("v_last", 2), ("round0", 1), ("round1", 4), ("roundb", 8), ("a0", 4), ("a1", 4), ("d0", 4), ("d1", 4),
+    ("round0", 3), ("round1", 4), ("roundb", 8), ("a0", 4), ("a1", 4), ("d0", 4), ("d1", 4),
     ("e2", 4), ("xb", 4), ("w1b", 4), ("w2b", 2), ("s2b", 1), ("xc", 4), ("xa", 4), ("w1g", 2), ("xd", 4), ("xe", 4),
     ("h0", 4), ("h1", 4), ("h2", 4), ("given0", 8), ("given1", 8),
 ]
@@ -62,14 +62,13 @@ def tile_list_deflated_slots_kernel(
         idx2 = kept([P, S // 16], U16, "idx2")
         idx3 = kept([P, M // 16], U16, "idx3")
 
-        tab_s = [at("page2", [P, T], U8, "tab_s0"), kept([P, T], U8, "tab_s1")]
+        tab_s = [at("page1", [P, T], U8, "tab_s0", skip=7 * KB), kept([P, T], U8, "tab_s1")]
         v_s = [kept([P, S], U8, "v_s%d" % a) for a in range(2)]
         w_s_raw = [kept([P, 2, HALF], U8, "w_s_raw%d" % b) for b in range(2)]
-        pages = [at("page%d" % i, [P, T2], F32, "page%d" % i) for i in range(2)]
+        pages = [at("page0", [P, T2], F32, "page0")]
         for cleared in (tab_s[0], tab_s[1], w_s_raw[0], w_s_raw[1]):
             nc.vector.memset(cleared[:].bitcast(I32), 0)
-        for page in pages:
-            nc.vector.memset(page[:], 0.0)
+        nc.vector.memset(pages[0][:], 0.0)
 
         def load_scale_rows(plane, scales, row=0):
             for r in range(4):
@@ -120,7 +119,7 @@ def tile_list_deflated_slots_kernel(
         load_scale_rows(w_s_raw[0], w2_scales[:, :, :HALF])
         load_w2_words(0)
         load_w1(0, 0)
-        w1_last = [at("raw0", [P, 4, P], F32, "w1_raw01%d" % t, skip=(4 + 2 * t) * KB) for t in range(2)]
+        w1_last = [at("raw0", [P, 4, P], F32, "w1_raw010", skip=4 * KB), at("h0", [P, 4, P], F32, "w1_raw011")]
         for t in range(2):
             nc.sync.dma_start(
                 out=w1_last[t][:], in_=w1[512:, P * t : P * (t + 1)].rearrange("(p i) c -> p i c", i=4)
@@ -152,6 +151,12 @@ def tile_list_deflated_slots_kernel(
         def quantise(words, scales, values):
             nc.vector.quantize_mx(out=words.bitcast(FP8X4), scales=scales, in_=values)
 
+        def quantise_group(group, values):
+            quantise(
+                w1_w[group][:].rearrange("p a c -> p (a c)"), w1_s[group][:].rearrange("p a c -> p (a c)"),
+                values[:].rearrange("p a c -> p (a c)"),
+            )
+
         def round_plain(raw, out):
             nc.scalar.copy(
                 out=out.rearrange("p (c j i) -> p c i j", j=4, i=4), in_=raw.rearrange("p i (c j) -> p c i j", j=4)
@@ -170,8 +175,8 @@ def tile_list_deflated_slots_kernel(
         def products(i, h, d_rows):
             b, t = divmod(i, 4)
             cols = slice(P * t, P * (t + 1))
-            group = min(i // 2, 2)
-            w1_cols = cols if b else slice(P * (t % 2), P * (t % 2 + 1))
+            group = (0, 1, 2, 2, 3, 3, 3, 3)[i]
+            w1_cols = cols if b else slice(P * max(t - 2, 0), P * (max(t - 2, 0) + 1))
             js = halves[h]
             bank = 4 * (i % 2) + 2 * h
             passes = (0, 1) if (i, h) == (0, 0) else (1, 0)
@@ -249,8 +254,9 @@ def tile_list_deflated_slots_kernel(
             pick(i - 1, place)
 
         nc.vector.tensor_copy(v_s[0][:], tab_s[0][:].indirect(idx[:]))
-        pages.append(at("page2", [P, T2], F32, "page2"))
-        nc.gpsimd.memset(pages[2][:], 0.0)
+        for i in (1, 2):
+            pages.append(at("page%d" % i, [P, T2], F32, "page%d" % i))
+            nc.gpsimd.memset(pages[i][:], 0.0)
         v_first = kept([P, S], U32, "v_w0")
         gather_words(0, slice(0, S), v_first[:])
         for h in range(2):
@@ -258,27 +264,26 @@ def tile_list_deflated_slots_kernel(
         nc.vector.tensor_copy(v_s[1][:], tab_s[1][:].indirect(idx[:]))
         v_w[(1, 0)] = kept([P, HALF], U32, "v_w10")[:]
         gather_words(1, halves[0], v_w[(1, 0)])
-        w1_w[0] = kept([P, 2, QUARTER], U32, "w1_w0")
-        w1_s[0] = kept([P, 2, QUARTER], U8, "w1_s0")
+        for group in range(2):
+            w1_w[group] = kept([P, 2, P], U32, "w1_w%d" % group)
+            w1_s[group] = kept([P, 2, P], U8, "w1_s%d" % group)
         rounded = at("round0", [P, 4 * P], BF16, "rounded000")
         round_plain(w1_raw[(0, 0)][:, :, :P], rounded[:])
-        quantise(w1_w[0][:, 0, :P], w1_s[0][:, 0, :P], rounded[:])
-        rounded = at("v_last", [P, 4 * P], BF16, "rounded010")
+        quantise(w1_w[0][:, 0, :], w1_s[0][:, 0, :], rounded[:])
+        rounded = at("round0", [P, 4 * P], BF16, "rounded010", skip=KB)
         round_plain(w1_last[0][:], rounded[:])
-        quantise(w1_w[0][:, 1, :P], w1_s[0][:, 1, :P], rounded[:])
-        v_w[(1, 1)] = at("v_last", [P, HALF], U32, "v_w11")[:]
+        quantise(w1_w[0][:, 1, :], w1_s[0][:, 1, :], rounded[:])
+        v_w[(1, 1)] = at("raw0", [P, HALF], U32, "v_w11", skip=4 * KB)[:]
         gather_words(1, halves[1], v_w[(1, 1)])
         load_given(1)
-        rounded = at("round0", [P, 4 * P], BF16, "rounded001")
-        round_plain(w1_raw[(0, 0)][:, :, P:], rounded[:])
-        quantise(w1_w[0][:, 0, P:], w1_s[0][:, 0, P:], rounded[:])
+        rounded = at("round0", [P, 2, 4 * P], BF16, "rounded01", skip=KB)
+        round_plain(w1_raw[(0, 0)][:, :, P:], rounded[:, 0, :])
         first, second = halves
         d_first = at("xa", [P, HALF], F32, "d_first", skip=3 * KB)
         acc_first = products(0, 0, d_first[:])
-        rounded = at("h0", [P, 4 * P], BF16, "rounded011")
-        round_plain(w1_last[1][:], rounded[:])
+        round_plain(w1_last[1][:], rounded[:, 1, :])
         nc.vector.tensor_tensor(d_first[:], acc_first[:], d_first[:], ALU.subtract)
-        quantise(w1_w[0][:, 1, P:], w1_s[0][:, 1, P:], rounded[:])
+        quantise_group(1, rounded)
         h_of[0] = rows("h0", "h_rows0")
         nc.vector.tensor_tensor(h_of[0][:, first], d_first[:], wgs_plain[:, first], ALU.mult)
         scatter(0, first)
@@ -298,12 +303,9 @@ def tile_list_deflated_slots_kernel(
         t_half = at("xa", [P, HALF], F32, "t_half1", skip=3 * KB)
         nc.gpsimd.tensor_tensor(t_half[:], a_of[1][:, first], d_of[1][:, first], ALU.subtract)
         nc.gpsimd.tensor_tensor(h_of[1][:, first], t_half[:], wgs_plain[:, first], ALU.mult)
-        w1_w[1] = at("w1g", [P, 2, QUARTER], U32, "w1_w1")
-        w1_s[1] = kept([P, 2, QUARTER], U8, "w1_s1")
-        quantise(
-            w1_w[1][:].rearrange("p a c -> p (a c)"), w1_s[1][:].rearrange("p a c -> p (a c)"),
-            rounded[:].rearrange("p a c -> p (a c)"),
-        )
+        w1_w[2] = at("w1g", [P, 2, QUARTER], U32, "w1_w2")
+        w1_s[2] = kept([P, 2, QUARTER], U8, "w1_s2")
+        quantise_group(2, rounded)
         t_half = at("round1", [P, HALF], F32, "t_half2")
         nc.gpsimd.tensor_tensor(t_half[:], a_of[1][:, second], d_of[1][:, second], ALU.subtract)
         nc.gpsimd.tensor_tensor(h_of[1][:, second], t_half[:], wgs_plain[:, second], ALU.mult)
@@ -332,12 +334,9 @@ def tile_list_deflated_slots_kernel(
             out=w2_w[1][:].bitcast(U16).rearrange("p a (t m) -> p a t m", t=4),
             in_=w2_w_raw[1][:].bitcast(U16).rearrange("p a (m t) -> p a t m", t=4),
         )
-        w1_w[2] = at("w1b", [P, 2, HALF], U32, "w1_w2")
-        w1_s[2] = kept([P, 2, HALF], U8, "w1_s2")
-        quantise(
-            w1_w[2][:].rearrange("p a c -> p (a c)"), w1_s[2][:].rearrange("p a c -> p (a c)"),
-            rounded[:].rearrange("p a c -> p (a c)"),
-        )
+        w1_w[3] = at("w1b", [P, 2, HALF], U32, "w1_w3")
+        w1_s[3] = kept([P, 2, HALF], U8, "w1_s3")
+        quantise_group(3, rounded)
         place_and_pick(3, "xc")
 
         z_rows = at("rawb0", [P, 4, M], BF16, "z_rows")

@@ -224,16 +224,16 @@ def tile_list_deflated_slots_kernel(
         def fetch(i, ms):
             nc.vector.tensor_copy(x_of[i][:, ms], pages[i % 3][:].indirect(idx3[:, ms.start // 16 : ms.stop // 16]))
 
+        def invert_parts(parts):
+            for x, u in parts:
+                nc.scalar.activation(out=u, in_=x, func=ACT.Square)
+            for x, u in parts:
+                nc.scalar.activation(out=u, in_=u, func=ACT.Abs_reciprocal_sqrt, scale=ROOT * ROOT, bias=ROOT * ROOT)
+            for x, u in parts:
+                nc.scalar.activation(out=x, in_=u, func=ACT.Square, scale=ROOT)
+
         def invert(i, u, parts):
-            x = x_of[i]
-            for ms in parts:
-                nc.scalar.activation(out=u[:, ms], in_=x[:, ms], func=ACT.Square)
-            for ms in parts:
-                nc.scalar.activation(
-                    out=u[:, ms], in_=u[:, ms], func=ACT.Abs_reciprocal_sqrt, scale=ROOT * ROOT, bias=ROOT * ROOT
-                )
-            for ms in parts:
-                nc.scalar.activation(out=x[:, ms], in_=u[:, ms], func=ACT.Square, scale=ROOT)
+            invert_parts([(x_of[i][:, ms], u[:, ms]) for ms in parts])
 
         def damp(i, out, ms=slice(0, M)):
             engine = nc.gpsimd if i < 7 else nc.vector
@@ -386,13 +386,11 @@ def tile_list_deflated_slots_kernel(
             invert(6, u6, [slice(ms.start, ms.start + QUARTER), slice(ms.start + QUARTER, ms.stop)])
             damp(6, z_late[:, 2, :], ms)
 
-        z_w = [[at("xc", [P, HALF], U32, "z_w00", skip=2 * KB), at("rawb0", [P, HALF], U32, "z_w01")]]
-        z_w.append([kept([P, HALF], U32, "z_w1%d" % u) for u in range(2)])
+        z_w = {}
         z_s = [kept([P, M], U8, "z_s%d" % b) for b in range(2)]
         y_banks = {}
 
         def last_stage(b, q):
-            part = quarters[q % 2]
             for u in range(2):
                 if b == 0:
                     y_banks[(q, u)] = psum.tile([P, 2, QUARTER], F32, name="bank%d" % (2 * q + u))
@@ -401,20 +399,24 @@ def tile_list_deflated_slots_kernel(
                     nc.tensor.matmul_mx(
                         out=y_banks[(q, u)][:, e, :],
                         lhsT=w5_w[:, b, cols].bitcast(FP8X4), lhsT_scale=w2_s[1][4:, b, cols],
-                        rhs=z_w[b][q // 2][:, part].bitcast(FP8X4), rhs_scale=z_s[b][:, quarters[q]],
+                        rhs=z_w[(b, q)].bitcast(FP8X4), rhs_scale=z_s[b][:, quarters[q]],
                         start=(b == 0 and e == 0), stop=(b == 1 and e == 1),
                     )
 
-        def first_half_of_y(u):
-            quantise(z_w[0][u][:], z_s[0][:, halves[u]], z_bf[0][:, halves[u], :].rearrange("p m t -> p (m t)"))
-            for q in (2 * u, 2 * u + 1):
-                last_stage(0, q)
+        def contract(b, q, words):
+            z_w[(b, q)] = words
+            quantise(words, z_s[b][:, quarters[q]], z_bf[b][:, quarters[q], :].rearrange("p m t -> p (m t)"))
+            last_stage(b, q)
 
-        first_half_of_y(0)
-        x_of[7] = rows("xa", "x7")
-        for ms in halves:
-            fetch(7, ms)
-        first_half_of_y(1)
+        def early_words(q, place, skip):
+            return at(place, [P, QUARTER], U32, "z_w0%d" % q, skip)[:]
+
+        contract(0, 0, early_words(0, "xc", 2 * KB))
+        x_last = [at("xa", [P, HALF], F32, "x7%d" % u, skip=2 * KB * u)[:] for u in range(2)]
+        for u in range(2):
+            nc.vector.tensor_copy(x_last[u], pages[7 % 3][:].indirect(idx3[:, 32 * u : 32 * (u + 1)]))
+        for q in (1, 3):
+            contract(0, q, early_words(q, "rawb0", KB * q))
 
         y_w = kept([P, M], I32, "y_w")
         y_s = kept([P, M], U8, "y_s")
@@ -427,7 +429,7 @@ def tile_list_deflated_slots_kernel(
             for u in range(2):
                 nc.scalar.copy(out=y[:, 2 * u : 2 * u + 2, :], in_=y_banks[(q, u)][:])
                 nc.sync.dma_start(out=y_rows[:, 2 * u : 2 * u + 2, quarters[q]], in_=y[:, 2 * u : 2 * u + 2, :])
-            y_bf[q] = at("roundb", [P, QUARTER, 4], BF16, "y_bf%d" % q, skip=2 * KB * q)
+            y_bf[q] = at("given0", [P, QUARTER, 4], BF16, "y_bf%d" % q, skip=2 * KB * q)
             nc.vector.tensor_copy(
                 out=y_bf[q][:].rearrange("p (c i) t -> p c t i", i=4),
                 in_=y[:].rearrange("p t (c i) -> p c t i", i=4),
@@ -436,28 +438,40 @@ def tile_list_deflated_slots_kernel(
         def planes(q):
             ms = quarters[q]
             quantise(y_w[:, ms], y_s[:, ms], y_bf[q][:].rearrange("p m t -> p (m t)"))
-            if q >= 2:
-                done = slice(0, 3 * QUARTER) if q == 2 else ms
-                nc.sync.dma_start(out=words_out[:, done], in_=y_w[:, done])
+            if q % 2:
+                nc.sync.dma_start(out=words_out[:, halves[q // 2]], in_=y_w[:, halves[q // 2]])
 
         z_bf.append(at("given1", [P, M, 4], BF16, "z_bf1"))
-        u7 = rows("rawb0", "u7", skip=4 * KB)
+        late_words = [kept([P, HALF], U32, "z_w1%d" % u) for u in range(2)]
+        u_last = [at("rawb0", [P, QUARTER], F32, "u7%d" % q, skip=4 * KB + KB * q)[:] for q in range(4)]
         for u in range(2):
-            pair = (2 * u, 2 * u + 1)
-            invert(7, u7, [quarters[q] for q in pair])
-            for q in pair:
-                damp(7, z_late[:, 3, :], quarters[q])
-            for q in pair:
-                nc.vector.tensor_copy(
-                    out=z_bf[1][:, quarters[q], :].rearrange("p (c i) t -> p c t i", i=4),
-                    in_=z_late[:, :, quarters[q]].rearrange("p t (c i) -> p c t i", i=4),
-                )
-            for q in pair:
-                quantise(
-                    z_w[1][u][:, quarters[q % 2]], z_s[1][:, quarters[q]],
-                    z_bf[1][:, quarters[q], :].rearrange("p m t -> p (m t)"),
-                )
-                last_stage(1, q)
+            invert_parts([(x_last[u][:, quarters[e]], u_last[2 * u + e]) for e in range(2)])
+
+        def damp_last(q):
+            nc.vector.tensor_tensor(
+                z_late[:, 3, quarters[q]], x_last[q // 2][:, quarters[q % 2]], given_t[7][:, quarters[q]], ALU.mult
+            )
+
+        def weave(q):
+            nc.vector.tensor_copy(
+                out=z_bf[1][:, quarters[q], :].rearrange("p (c i) t -> p c t i", i=4),
+                in_=z_late[:, :, quarters[q]].rearrange("p t (c i) -> p c t i", i=4),
+            )
+
+        def close(q):
+            contract(1, q, late_words[q // 2][:, quarters[q % 2]])
+
+        damp_last(0)
+        contract(0, 2, early_words(2, "rawb0", 4 * KB))
+        weave(0)
+        damp_last(1)
+        close(0)
+        for q in (1, 2):
+            weave(q)
+            damp_last(q + 1)
+            close(q)
+        weave(3)
+        close(3)
         for q in range(5):
             if q < 4:
                 finish(q)

@@ -413,10 +413,9 @@ def tile_list_deflated_slots_kernel(
 
         contract(0, 0, early_words(0, "xc", 2 * KB))
         x_last = [at("xa", [P, HALF], F32, "x7%d" % u, skip=2 * KB * u)[:] for u in range(2)]
-        for u in range(2):
-            nc.vector.tensor_copy(x_last[u], pages[7 % 3][:].indirect(idx3[:, 32 * u : 32 * (u + 1)]))
-        for q in (1, 3):
-            contract(0, q, early_words(q, "rawb0", KB * q))
+        for u, part in ((0, quarters[0]), (0, quarters[1]), (1, first)):
+            columns = slice((HALF * u + part.start) // 16, (HALF * u + part.stop) // 16)
+            nc.vector.tensor_copy(x_last[u][:, part], pages[7 % 3][:].indirect(idx3[:, columns]))
 
         y_w = kept([P, M], I32, "y_w")
         y_s = kept([P, M], U8, "y_s")
@@ -426,9 +425,9 @@ def tile_list_deflated_slots_kernel(
 
         def finish(q):
             y = at("raw0", [P, 4, QUARTER], F32, "y%d" % q, skip=4 * KB * q)
-            for u in range(2):
-                nc.scalar.copy(out=y[:, 2 * u : 2 * u + 2, :], in_=y_banks[(q, u)][:])
-                nc.sync.dma_start(out=y_rows[:, 2 * u : 2 * u + 2, quarters[q]], in_=y[:, 2 * u : 2 * u + 2, :])
+            for ts in ((slice(0, 1), slice(1, 2)) if q == 0 else (slice(0, 2),)) + (slice(2, 4),):
+                nc.scalar.copy(out=y[:, ts, :], in_=y_banks[(q, ts.start // 2)][:, ts.start % 2 : (ts.stop - 1) % 2 + 1, :])
+                nc.sync.dma_start(out=y_rows[:, ts, quarters[q]], in_=y[:, ts, :])
             y_bf[q] = at("given0", [P, QUARTER, 4], BF16, "y_bf%d" % q, skip=2 * KB * q)
             nc.vector.tensor_copy(
                 out=y_bf[q][:].rearrange("p (c i) t -> p c t i", i=4),
@@ -443,9 +442,15 @@ def tile_list_deflated_slots_kernel(
 
         z_bf.append(at("given1", [P, M, 4], BF16, "z_bf1"))
         late_words = [kept([P, HALF], U32, "z_w1%d" % u) for u in range(2)]
-        u_last = [at("rawb0", [P, QUARTER], F32, "u7%d" % q, skip=4 * KB + KB * q)[:] for q in range(4)]
-        for u in range(2):
-            invert_parts([(x_last[u][:, quarters[e]], u_last[2 * u + e]) for e in range(2)])
+        for q in range(2):
+            x = x_last[0][:, quarters[q]]
+            squares = at("rawb0", [P, QUARTER], F32, "squares%d" % q, skip=7 * KB)[:]
+            roots = at("rawb0", [P, QUARTER], F32, "roots%d" % q, skip=(4 * KB, 2 * KB)[q])[:]
+            nc.scalar.activation(out=squares, in_=x, func=ACT.Square)
+            nc.scalar.activation(out=roots, in_=squares, func=ACT.Abs_reciprocal_sqrt, scale=ROOT * ROOT, bias=ROOT * ROOT)
+            nc.scalar.activation(out=x, in_=roots, func=ACT.Square, scale=ROOT)
+        u_last = at("rawb0", [P, HALF], F32, "u7", skip=5 * KB + 64)
+        invert_parts([(x_last[1][:, ms], u_last[:, ms]) for ms in quarters[:2]])
 
         def damp_last(q):
             nc.vector.tensor_tensor(
@@ -462,15 +467,19 @@ def tile_list_deflated_slots_kernel(
             contract(1, q, late_words[q // 2][:, quarters[q % 2]])
 
         damp_last(0)
-        contract(0, 2, early_words(2, "rawb0", 4 * KB))
+        contract(0, 1, early_words(1, "rawb0", 4 * KB))
         weave(0)
         damp_last(1)
         close(0)
-        for q in (1, 2):
-            weave(q)
-            damp_last(q + 1)
-            close(q)
+        weave(1)
+        damp_last(2)
+        close(1)
+        contract(0, 2, early_words(2, "rawb0", 2 * KB))
+        weave(2)
+        damp_last(3)
+        close(2)
         weave(3)
+        contract(0, 3, early_words(3, "rawb0", 6 * KB))
         close(3)
         for q in range(5):
             if q < 4:

@@ -24,7 +24,7 @@ KB = 1024
 
 PLACES = [
     ("page0", 8), ("page1", 8), ("page2", 8), ("tab0", 8), ("tab1", 8), ("raw0", 8), ("raw1", 8), ("rawb0", 8), ("rawb1", 8),
-    ("round0", 3), ("round1", 4), ("roundb", 8), ("a0", 4), ("a1", 4), ("d0", 4), ("d1", 4),
+    ("round0", 4), ("round1", 4), ("roundb", 8), ("a0", 4), ("a1", 4), ("d0", 4), ("d1", 4),
     ("e2", 4), ("xb", 4), ("w1b", 4), ("w2b", 2), ("s2b", 1), ("xc", 4), ("xa", 4), ("w1g", 2), ("xd", 4), ("xe", 4),
     ("h0", 4), ("h1", 4), ("h2", 4), ("given0", 8), ("given1", 8),
 ]
@@ -78,14 +78,15 @@ def tile_list_deflated_slots_kernel(
                 )
 
         tab_w = [at("tab%d" % a, [P, T], I32, "tab_w%d" % a) for a in range(2)]
-        w2_w_raw = [kept([P, 2, 2 * HALF], U8, "w2_w_raw%d" % b) for b in range(2)]
         w1_raw = {}
 
-        def load_w2_words(b):
+        def load_w2_words(first, last):
+            words = kept([P, 2, 2 * P * (last - first)], U8, "w2_raw%d" % first)
             nc.sync.dma_start(
-                out=w2_w_raw[b][:].bitcast(I32),
-                in_=w2_words[:, :, 1024 * b : 1024 * (b + 1)].rearrange("a p c -> p a c").bitcast(I32),
+                out=words[:].bitcast(I32),
+                in_=w2_words[:, :, 2 * P * first : 2 * P * last].rearrange("a p c -> p a c").bitcast(I32),
             )
+            return words
 
         def load_w1(group, a):
             c0, width = ((0, QUARTER), (QUARTER, QUARTER), (HALF, HALF))[group]
@@ -117,7 +118,7 @@ def tile_list_deflated_slots_kernel(
                 nc.sync.dma_start(out=tab_s[a][r:P:32, :].bitcast(I32), in_=tab_scales[a, r:16:4, :].bitcast(I32))
             nc.sync.dma_start(out=tab_w[a][:], in_=tab_words[a].rearrange("p t i -> p (t i)").bitcast(I32))
         load_scale_rows(w_s_raw[0], w2_scales[:, :, :HALF])
-        load_w2_words(0)
+        w2_first = load_w2_words(0, 1)
         load_w1(0, 0)
         w1_last = [at("raw0", [P, 4, P], F32, "w1_raw010", skip=4 * KB), at("h0", [P, 4, P], F32, "w1_raw011")]
         for t in range(2):
@@ -126,13 +127,14 @@ def tile_list_deflated_slots_kernel(
             )
             if t == 0:
                 nc.sync.dma_start(out=beta_t[0][:], in_=beta[:HALF].rearrange("(t p) -> p t", t=4))
+        w2_rest = load_w2_words(1, 4)
         nc.sync.dma_start(out=wgs_plain, in_=wgs)
         load_w1(1, 0)
         load_w1(1, 1)
         nc.sync.dma_start(idx3[:], offs3)
         load_w1(2, 0)
         load_w1(2, 1)
-        load_w2_words(1)
+        w2_late = load_w2_words(4, 8)
         load_scale_rows(w_s_raw[1], w2_scales[:, :, HALF:])
         load_scale_rows(w_s_raw[1], w5_scales, row=4)
         nc.sync.dma_start(out=beta_t[1][:], in_=beta[HALF:].rearrange("(p t) -> p t", t=4))
@@ -169,7 +171,9 @@ def tile_list_deflated_slots_kernel(
             )
 
         w1_w, w1_s = {}, {}
-        w2_w, w2_s = {0: w2_w_raw[0]}, {0: w_s_raw[0]}
+        w2_w, w2_s = {0: w2_first[:]}, {0: w_s_raw[0]}
+        for t in range(1, 4):
+            w2_w[t] = w2_rest[:, :, 2 * P * (t - 1) : 2 * P * t]
         a_of, d_of, t_of, h_of, x_of = {}, {}, {}, {}, {}
 
         def products(i, h, d_rows):
@@ -185,7 +189,7 @@ def tile_list_deflated_slots_kernel(
             for a in passes:
                 nc.tensor.matmul_mx(
                     out=acc_d[:],
-                    lhsT=w2_w[b][:, a, 2 * P * t : 2 * P * (t + 1)].bitcast(FP4X4),
+                    lhsT=w2_w[i][:, a, :].bitcast(FP4X4),
                     lhsT_scale=w2_s[b][:, a, cols],
                     rhs=v_w[(a, h)].bitcast(FP8X4), rhs_scale=v_s[a][:, js],
                     start=(a == passes[0]), stop=(a == passes[1]),
@@ -276,14 +280,14 @@ def tile_list_deflated_slots_kernel(
         v_w[(1, 1)] = at("raw0", [P, HALF], U32, "v_w11", skip=4 * KB)[:]
         gather_words(1, halves[1], v_w[(1, 1)])
         load_given(1)
-        rounded = at("round0", [P, 2, 4 * P], BF16, "rounded01", skip=KB)
+        rounded = at("round0", [P, 2, 4 * P], BF16, "rounded01", skip=2 * KB)
         round_plain(w1_raw[(0, 0)][:, :, P:], rounded[:, 0, :])
+        round_plain(w1_last[1][:], rounded[:, 1, :])
+        quantise_group(1, rounded)
         first, second = halves
         d_first = at("xa", [P, HALF], F32, "d_first", skip=3 * KB)
         acc_first = products(0, 0, d_first[:])
-        round_plain(w1_last[1][:], rounded[:, 1, :])
         nc.vector.tensor_tensor(d_first[:], acc_first[:], d_first[:], ALU.subtract)
-        quantise_group(1, rounded)
         h_of[0] = rows("h0", "h_rows0")
         nc.vector.tensor_tensor(h_of[0][:, first], d_first[:], wgs_plain[:, first], ALU.mult)
         scatter(0, first)
@@ -329,11 +333,13 @@ def tile_list_deflated_slots_kernel(
             out=w2_s[1][:].rearrange("p a (t m) -> p a t m", t=4),
             in_=w_s_raw[1][:].rearrange("p a (m t) -> p a t m", t=4),
         )
-        w2_w[1] = at("w2b", [P, 2, 2 * HALF], U8, "w2_w1")
+        w2_dealt = at("w2b", [P, 2, 2 * HALF], U8, "w2_dealt")
         nc.vector.tensor_copy(
-            out=w2_w[1][:].bitcast(U16).rearrange("p a (t m) -> p a t m", t=4),
-            in_=w2_w_raw[1][:].bitcast(U16).rearrange("p a (m t) -> p a t m", t=4),
+            out=w2_dealt[:].bitcast(U16).rearrange("p a (t m) -> p a t m", t=4),
+            in_=w2_late[:].bitcast(U16).rearrange("p a (m t) -> p a t m", t=4),
         )
+        for t in range(4):
+            w2_w[4 + t] = w2_dealt[:, :, 2 * P * t : 2 * P * (t + 1)]
         w1_w[3] = at("w1b", [P, 2, HALF], U32, "w1_w3")
         w1_s[3] = kept([P, 2, HALF], U8, "w1_s3")
         quantise_group(3, rounded)

@@ -21,12 +21,13 @@ HALF = 512
 QUARTER = 256
 ROOT = 75.0 / 64.0
 KB = 1024
+LIVE = 100
 
 PLACES = [
     ("page0", 8), ("page1", 8), ("page2", 8), ("tab0", 8), ("tab1", 8), ("raw0", 8), ("raw1", 8), ("rawb0", 8), ("rawb1", 8),
     ("round0", 4), ("round1", 4), ("roundb", 8), ("a0", 4), ("a1", 4), ("d0", 4), ("d1", 4),
     ("e2", 4), ("xb", 4), ("w1b", 4), ("w2b", 2), ("s2b", 1), ("xc", 4), ("xa", 4), ("w1g", 2), ("xd", 4), ("xe", 4),
-    ("h0", 4), ("h1", 4), ("h2", 4), ("given0", 8), ("given1", 8),
+    ("h0", 4), ("h1", 4), ("h2", 4), ("given0", 8), ("given1", 8), ("lead", 2), ("hold", 2),
 ]
 
 
@@ -62,11 +63,11 @@ def tile_list_deflated_slots_kernel(
         idx2 = kept([P, S // 16], U16, "idx2")
         idx3 = kept([P, M // 16], U16, "idx3")
 
-        tab_s = [at("page1", [P, T], U8, "tab_s0", skip=7 * KB), kept([P, T], U8, "tab_s1")]
+        tab_s = at("page1", [P, T], U8, "tab_s", skip=7 * KB)
         v_s = [kept([P, S], U8, "v_s%d" % a) for a in range(2)]
         w_s_raw = [kept([P, 2, HALF], U8, "w_s_raw%d" % b) for b in range(2)]
         pages = [at("page0", [P, T2], F32, "page0")]
-        for cleared in (tab_s[0], tab_s[1], w_s_raw[0], w_s_raw[1]):
+        for cleared in (tab_s, w_s_raw[0], v_s[1], w_s_raw[1]):
             nc.vector.memset(cleared[:].bitcast(I32), 0)
         nc.vector.memset(pages[0][:], 0.0)
 
@@ -89,8 +90,8 @@ def tile_list_deflated_slots_kernel(
             return words
 
         def load_w1(group, a):
-            c0, width = ((0, QUARTER), (QUARTER, QUARTER), (HALF, HALF))[group]
-            place, skip = (("raw0", 4 * KB * a), ("raw1", 4 * KB * a), ("rawb%d" % a, 0))[group]
+            c0, width = ((QUARTER, QUARTER), (HALF, HALF))[group - 1]
+            place, skip = (("raw1", 4 * KB * a), ("rawb%d" % a, 0))[group - 1]
             raw = at(place, [P, 4, width], F32, "w1_raw%d%d" % (group, a), skip)
             nc.sync.dma_start(
                 out=raw[:], in_=w1[512 * a : 512 * (a + 1), c0 : c0 + width].rearrange("(p i) c -> p i c", i=4)
@@ -113,22 +114,32 @@ def tile_list_deflated_slots_kernel(
 
         nc.sync.dma_start(idx[:], offs)
         nc.sync.dma_start(idx2[:], offs2)
-        for a in range(2):
-            for r in range(4):
-                nc.sync.dma_start(out=tab_s[a][r:P:32, :].bitcast(I32), in_=tab_scales[a, r:16:4, :].bitcast(I32))
-            nc.sync.dma_start(out=tab_w[a][:], in_=tab_words[a].rearrange("p t i -> p (t i)").bitcast(I32))
-        load_scale_rows(w_s_raw[0], w2_scales[:, :, :HALF])
-        w2_first = load_w2_words(0, 1)
-        load_w1(0, 0)
-        w1_last = [at("raw0", [P, 4, P], F32, "w1_raw010", skip=4 * KB), at("h0", [P, 4, P], F32, "w1_raw011")]
-        for t in range(2):
+        for r in range(4):
             nc.sync.dma_start(
-                out=w1_last[t][:], in_=w1[512:, P * t : P * (t + 1)].rearrange("(p i) c -> p i c", i=4)
+                out=tab_s[r:P:16, :].bitcast(I32),
+                in_=tab_scales[:, r:16:4, :].rearrange("a q c -> q a c").bitcast(I32),
             )
-            if t == 0:
-                nc.sync.dma_start(out=beta_t[0][:], in_=beta[:HALF].rearrange("(t p) -> p t", t=4))
-        w2_rest = load_w2_words(1, 4)
+        for a in range(2):
+            nc.sync.dma_start(out=tab_w[a][:], in_=tab_words[a].rearrange("p t i -> p (t i)").bitcast(I32))
+        w2_first = load_w2_words(0, 1)
+        load_scale_rows(w_s_raw[0], w2_scales[:, :, :HALF])
+        early = {}
+
+        def load_early(t):
+            for a in range(2):
+                early[(t, a)] = at("raw0", [P, 4, P], F32, "w1_early%d%d" % (t, a), skip=4 * KB * t + 2 * KB * a)
+                nc.sync.dma_start(
+                    out=early[(t, a)][:],
+                    in_=w1[512 * a : 512 * (a + 1), P * t : P * (t + 1)].rearrange("(p i) c -> p i c", i=4),
+                )
+
+        load_early(0)
+        nc.sync.dma_start(out=beta_t[0][:], in_=beta[:HALF].rearrange("(t p) -> p t", t=4))
+        load_early(1)
+        wgs_lead = kept([P, QUARTER], F32, "wgs_lead")
+        nc.sync.dma_start(out=wgs_lead[:], in_=wgs[:, quarters[0]])
         nc.sync.dma_start(out=wgs_plain, in_=wgs)
+        w2_rest = load_w2_words(1, 4)
         load_w1(1, 0)
         load_w1(1, 1)
         nc.sync.dma_start(idx3[:], offs3)
@@ -145,10 +156,7 @@ def tile_list_deflated_slots_kernel(
         w5_w_raw = kept([P, 2, N], I32, "w5_w_raw")
         nc.sync.dma_start(out=w5_w_raw[:], in_=w5_words.rearrange("a p c i -> p a (c i)").bitcast(I32))
 
-        v_w = {}
-
-        def gather_words(a, js, out):
-            nc.vector.tensor_copy(out, tab_w[a][:].bitcast(U32).indirect(idx[:, js.start // 16 : js.stop // 16]))
+        v_w = [kept([P, S], U32, "v_w%d" % a) for a in range(2)]
 
         def quantise(words, scales, values):
             nc.vector.quantize_mx(out=words.bitcast(FP8X4), scales=scales, in_=values)
@@ -176,22 +184,19 @@ def tile_list_deflated_slots_kernel(
             w2_w[t] = w2_rest[:, :, 2 * P * (t - 1) : 2 * P * t]
         a_of, d_of, t_of, h_of, x_of = {}, {}, {}, {}, {}
 
-        def products(i, h, d_rows):
+        def products(i, js, banks, d_rows):
             b, t = divmod(i, 4)
             cols = slice(P * t, P * (t + 1))
             group = (0, 1, 2, 2, 3, 3, 3, 3)[i]
             w1_cols = cols if b else slice(P * max(t - 2, 0), P * (max(t - 2, 0) + 1))
-            js = halves[h]
-            bank = 4 * (i % 2) + 2 * h
-            passes = (0, 1) if (i, h) == (0, 0) else (1, 0)
-            acc_d = psum.tile([P, HALF], F32, name="bank%d" % (bank if i > 1 else 0))
-            acc_a = psum.tile([P, HALF], F32, name="bank%d" % (bank + 1 if i > 1 or bank == 0 else bank))
+            passes = (0, 1) if i == 0 else (1, 0)
+            acc_d, acc_a = [psum.tile([P, js.stop - js.start], F32, name="bank%d" % bank) for bank in banks]
             for a in passes:
                 nc.tensor.matmul_mx(
                     out=acc_d[:],
                     lhsT=w2_w[i][:, a, :].bitcast(FP4X4),
                     lhsT_scale=w2_s[b][:, a, cols],
-                    rhs=v_w[(a, h)].bitcast(FP8X4), rhs_scale=v_s[a][:, js],
+                    rhs=v_w[a][:, js].bitcast(FP8X4), rhs_scale=v_s[a][:, js],
                     start=(a == passes[0]), stop=(a == passes[1]),
                 )
             for a in passes:
@@ -199,7 +204,7 @@ def tile_list_deflated_slots_kernel(
                     out=acc_a[:],
                     lhsT=w1_w[group][:, a, w1_cols].bitcast(FP8X4),
                     lhsT_scale=w1_s[group][:, a, w1_cols],
-                    rhs=v_w[(a, h)].bitcast(FP8X4), rhs_scale=v_s[a][:, js],
+                    rhs=v_w[a][:, js].bitcast(FP8X4), rhs_scale=v_s[a][:, js],
                     start=(a == passes[0]), stop=(a == passes[1]),
                 )
             nc.scalar.activation(out=d_rows, in_=acc_d[:], func=ACT.Copy, scale=beta_t[b][:, t : t + 1])
@@ -208,8 +213,9 @@ def tile_list_deflated_slots_kernel(
         def multiply(i, d_place, skip=0):
             a_of[i] = rows("a%d" % (i % 2), "a_rows%d" % i)
             d_of[i] = rows(d_place, "d_rows%d" % i, skip)
-            for h in range(2):
-                nc.scalar.copy(out=a_of[i][:, halves[h]], in_=products(i, h, d_of[i][:, halves[h]])[:])
+            for h, js in enumerate(halves):
+                bank = 4 * (i % 2) + 2 * h
+                nc.scalar.copy(out=a_of[i][:, js], in_=products(i, js, (bank, bank + 1), d_of[i][:, js])[:])
 
         def deflate(i, t_rows, parts=(slice(0, S),)):
             t_of[i] = t_rows
@@ -257,65 +263,61 @@ def tile_list_deflated_slots_kernel(
             scatter(i, slice(0, S))
             pick(i - 1, place)
 
-        nc.vector.tensor_copy(v_s[0][:], tab_s[0][:].indirect(idx[:]))
+        nc.vector.tensor_copy(v_s[0][:], tab_s[:].indirect(idx[:]))
+        nc.scalar.dma_start(out=v_s[1][:LIVE, :].bitcast(I32), in_=v_s[0][16 : 16 + LIVE, :].bitcast(I32))
         for i in (1, 2):
             pages.append(at("page%d" % i, [P, T2], F32, "page%d" % i))
             nc.gpsimd.memset(pages[i][:], 0.0)
-        v_first = kept([P, S], U32, "v_w0")
-        gather_words(0, slice(0, S), v_first[:])
-        for h in range(2):
-            v_w[(0, h)] = v_first[:, halves[h]]
-        nc.vector.tensor_copy(v_s[1][:], tab_s[1][:].indirect(idx[:]))
-        v_w[(1, 0)] = kept([P, HALF], U32, "v_w10")[:]
-        gather_words(1, halves[0], v_w[(1, 0)])
-        for group in range(2):
-            w1_w[group] = kept([P, 2, P], U32, "w1_w%d" % group)
-            w1_s[group] = kept([P, 2, P], U8, "w1_s%d" % group)
-        rounded = at("round0", [P, 4 * P], BF16, "rounded000")
-        round_plain(w1_raw[(0, 0)][:, :, :P], rounded[:])
-        quantise(w1_w[0][:, 0, :], w1_s[0][:, 0, :], rounded[:])
-        rounded = at("round0", [P, 4 * P], BF16, "rounded010", skip=KB)
-        round_plain(w1_last[0][:], rounded[:])
-        quantise(w1_w[0][:, 1, :], w1_s[0][:, 1, :], rounded[:])
-        v_w[(1, 1)] = at("raw0", [P, HALF], U32, "v_w11", skip=4 * KB)[:]
-        gather_words(1, halves[1], v_w[(1, 1)])
+        for a in range(2):
+            nc.vector.tensor_copy(v_w[a][:], tab_w[a][:].bitcast(U32).indirect(idx[:]))
         load_given(1)
-        rounded = at("round0", [P, 2, 4 * P], BF16, "rounded01", skip=2 * KB)
-        round_plain(w1_raw[(0, 0)][:, :, P:], rounded[:, 0, :])
-        round_plain(w1_last[1][:], rounded[:, 1, :])
-        quantise_group(1, rounded)
+
+        def early_weights(t, words):
+            w1_w[t] = words
+            w1_s[t] = kept([P, 2, P], U8, "w1_s%d" % t)
+            rounded = at("round0", [P, 2, 4 * P], BF16, "rounded0%d" % t, skip=2 * KB * t)
+            for a in range(2):
+                round_plain(early[(t, a)][:], rounded[:, a, :])
+            quantise_group(t, rounded)
+
+        early_weights(0, kept([P, 2, P], U32, "w1_w0"))
         first, second = halves
-        d_first = at("xa", [P, HALF], F32, "d_first", skip=3 * KB)
-        acc_first = products(0, 0, d_first[:])
-        nc.vector.tensor_tensor(d_first[:], acc_first[:], d_first[:], ALU.subtract)
         h_of[0] = rows("h0", "h_rows0")
-        nc.vector.tensor_tensor(h_of[0][:, first], d_first[:], wgs_plain[:, first], ALU.mult)
-        scatter(0, first)
-        a_half = at("round1", [P, HALF], F32, "a_half")
-        d_half = at("d0", [P, HALF], F32, "d_half")
-        nc.scalar.copy(out=a_half[:], in_=products(0, 1, d_half[:])[:])
-        t_half = at("xa", [P, HALF], F32, "t_half0", skip=3 * KB)
-        nc.gpsimd.tensor_tensor(t_half[:], a_half[:], d_half[:], ALU.subtract)
-        nc.gpsimd.tensor_tensor(h_of[0][:, second], t_half[:], wgs_plain[:, second], ALU.mult)
-        scatter(0, second)
+        a_of[0] = rows("a0", "a_rows0")
+        d_of[0] = rows("d0", "d_rows0")
+        lead_d = at("lead", [P, QUARTER], F32, "lead_d")
+        lead_a = products(0, quarters[0], (0, 1), lead_d[:])
+        next_a = products(0, quarters[1], (2, 3), d_of[0][:, quarters[1]])
+        lead_t = at("hold", [P, QUARTER], F32, "lead_t")
+        nc.vector.tensor_tensor(lead_t[:], lead_a[:], lead_d[:], ALU.subtract)
+        nc.vector.tensor_tensor(h_of[0][:, quarters[0]], lead_t[:], wgs_lead[:], ALU.mult)
+        early_weights(1, at("lead", [P, 2, P], U32, "w1_w1", skip=3 * KB // 4))
+        nc.scalar.copy(out=a_of[0][:, quarters[1]], in_=next_a[:])
+        nc.scalar.copy(out=a_of[0][:, second], in_=products(0, second, (1, 0), d_of[0][:, second])[:])
+
+        def part_of(i, js, place, skip):
+            t_part = at(place, [P, js.stop - js.start], F32, "t_part%d_%d" % (i, js.start), skip)
+            nc.gpsimd.tensor_tensor(t_part[:], a_of[i][:, js], d_of[i][:, js], ALU.subtract)
+            nc.gpsimd.tensor_tensor(h_of[i][:, js], t_part[:], wgs_plain[:, js], ALU.mult)
+
+        for js, (place, skip) in zip(quarters[1:], (("hold", KB // 2), ("xe", 0), ("xa", 3 * KB))):
+            part_of(0, js, place, skip)
+        for js in (quarters[0], quarters[1], second):
+            scatter(0, js)
 
         multiply(1, "d1")
         rounded = at("round1", [P, 2, 4 * QUARTER], BF16, "rounded1")
         for a in range(2):
             round_plain(w1_raw[(1, a)][:], rounded[:, a, :])
         h_of[1] = rows("raw1", "h_rows1", skip=2 * KB)
-        t_half = at("xa", [P, HALF], F32, "t_half1", skip=3 * KB)
-        nc.gpsimd.tensor_tensor(t_half[:], a_of[1][:, first], d_of[1][:, first], ALU.subtract)
-        nc.gpsimd.tensor_tensor(h_of[1][:, first], t_half[:], wgs_plain[:, first], ALU.mult)
+        part_of(1, first, "xa", 3 * KB)
         w1_w[2] = at("w1g", [P, 2, QUARTER], U32, "w1_w2")
         w1_s[2] = kept([P, 2, QUARTER], U8, "w1_s2")
         quantise_group(2, rounded)
-        t_half = at("round1", [P, HALF], F32, "t_half2")
-        nc.gpsimd.tensor_tensor(t_half[:], a_of[1][:, second], d_of[1][:, second], ALU.subtract)
-        nc.gpsimd.tensor_tensor(h_of[1][:, second], t_half[:], wgs_plain[:, second], ALU.mult)
-        scatter(1, first)
+        for q in (2, 3):
+            part_of(1, quarters[q], "round1", KB * q)
         pick(0, "xa")
-        scatter(1, second)
+        scatter(1, slice(0, S))
         multiply(2, "roundb")
         multiply(3, "d1")
         rounded = at("roundb", [P, 2, 4 * HALF], BF16, "rounded2")

@@ -24,9 +24,9 @@ KB = 1024
 LIVE = 100
 
 PLACES = [
-    ("page0", 8), ("page1", 8), ("page2", 8), ("tab0", 8), ("tab1", 8), ("raw0", 8), ("raw1", 8), ("rawb0", 8), ("rawb1", 8),
-    ("round0", 4), ("round1", 4), ("roundb", 8), ("a0", 4), ("a1", 4), ("d0", 4), ("d1", 4),
-    ("e2", 4), ("xb", 4), ("w1b", 4), ("w2b", 2), ("s2b", 1), ("xc", 4), ("xa", 4), ("w1g", 2), ("xd", 4), ("xe", 4),
+    ("page0", 8), ("page1", 8), ("page2", 8), ("tab0", 8), ("tab1", 8), ("raw0", 8), ("raw1", 8), ("d1x", 4), ("rawb0", 8), ("rawb1", 8),
+    ("round0", 4), ("h1pre", 2), ("round1", 4), ("roundb", 8), ("a0", 4), ("a1", 4), ("d0", 4), ("d1", 4),
+    ("e2", 4), ("xb", 4), ("w1b", 4), ("w2b", 2), ("s2b", 1), ("xc", 4), ("xa", 4), ("w1g", 3), ("xd", 4), ("xe", 4),
     ("h0", 4), ("h1", 4), ("h2", 4), ("given0", 8), ("given1", 8), ("lead", 2), ("hold", 2),
 ]
 
@@ -136,9 +136,8 @@ def tile_list_deflated_slots_kernel(
         load_early(0)
         nc.sync.dma_start(out=beta_t[0][:], in_=beta[:HALF].rearrange("(t p) -> p t", t=4))
         load_early(1)
-        wgs_lead = kept([P, QUARTER], F32, "wgs_lead")
-        nc.sync.dma_start(out=wgs_lead[:], in_=wgs[:, quarters[0]])
-        nc.sync.dma_start(out=wgs_plain, in_=wgs)
+        nc.sync.dma_start(out=wgs_plain[:, halves[0]], in_=wgs[:, halves[0]])
+        nc.sync.dma_start(out=wgs_plain[:, halves[1]], in_=wgs[:, halves[1]])
         w2_rest = load_w2_words(1, 4)
         load_w1(1, 0)
         load_w1(1, 1)
@@ -228,8 +227,11 @@ def tile_list_deflated_slots_kernel(
             for js in parts:
                 nc.gpsimd.tensor_tensor(h_rows[:, js], t_of[i][:, js], weights[:, js], ALU.mult)
 
+        def put(i, js, values):
+            nc.vector.tensor_copy(pages[i % 3][:].indirect(idx2[:, js.start // 16 : js.stop // 16]), values)
+
         def scatter(i, js):
-            nc.vector.tensor_copy(pages[i % 3][:].indirect(idx2[:, js.start // 16 : js.stop // 16]), h_of[i][:, js])
+            put(i, js, h_of[i][:, js])
 
         def fetch(i, ms):
             nc.vector.tensor_copy(x_of[i][:, ms], pages[i % 3][:].indirect(idx3[:, ms.start // 16 : ms.stop // 16]))
@@ -255,8 +257,8 @@ def tile_list_deflated_slots_kernel(
             for t in range(4):
                 nc.sync.dma_start(out=z_rows[32 * i : 32 * (i + 1), t, :], in_=plain[t:P:4, :])
 
-        def pick(i, place):
-            x_of[i] = rows(place, "x%d" % i)
+        def pick(i, place, skip=0):
+            x_of[i] = rows(place, "x%d" % i, skip)
             fetch(i, slice(0, M))
 
         def place_and_pick(i, place):
@@ -272,51 +274,44 @@ def tile_list_deflated_slots_kernel(
             nc.vector.tensor_copy(v_w[a][:], tab_w[a][:].bitcast(U32).indirect(idx[:]))
         load_given(1)
 
-        def early_weights(t, words):
-            w1_w[t] = words
-            w1_s[t] = kept([P, 2, P], U8, "w1_s%d" % t)
-            rounded = at("round0", [P, 2, 4 * P], BF16, "rounded0%d" % t, skip=2 * KB * t)
-            for a in range(2):
-                round_plain(early[(t, a)][:], rounded[:, a, :])
-            quantise_group(t, rounded)
-
-        early_weights(0, kept([P, 2, P], U32, "w1_w0"))
+        w1_s[0] = kept([P, 2, P], U8, "w1_s0")
+        w1_s[1] = at("round1", [P, 2, P], U8, "w1_s1")
+        w1_w[0] = kept([P, 2, P], U32, "w1_w0")
+        for a in range(2):
+            rounded = at("round0", [P, 4 * P], BF16, "rounded00%d" % a, skip=KB * a)
+            round_plain(early[(0, a)][:], rounded[:])
+            quantise(w1_w[0][:, a, :], w1_s[0][:, a, :], rounded[:])
         first, second = halves
-        h_of[0] = rows("h0", "h_rows0")
-        a_of[0] = rows("a0", "a_rows0")
-        d_of[0] = rows("d0", "d_rows0")
-        lead_d = at("lead", [P, QUARTER], F32, "lead_d")
-        lead_a = products(0, quarters[0], (0, 1), lead_d[:])
-        next_a = products(0, quarters[1], (2, 3), d_of[0][:, quarters[1]])
-        lead_t = at("hold", [P, QUARTER], F32, "lead_t")
-        nc.vector.tensor_tensor(lead_t[:], lead_a[:], lead_d[:], ALU.subtract)
-        nc.vector.tensor_tensor(h_of[0][:, quarters[0]], lead_t[:], wgs_lead[:], ALU.mult)
-        early_weights(1, at("lead", [P, 2, P], U32, "w1_w1", skip=3 * KB // 4))
-        nc.scalar.copy(out=a_of[0][:, quarters[1]], in_=next_a[:])
-        nc.scalar.copy(out=a_of[0][:, second], in_=products(0, second, (1, 0), d_of[0][:, second])[:])
+        h_first = at("h0", [P, HALF], F32, "h_first")
+        d_first = at("lead", [P, HALF], F32, "d_first")
+        acc_first = products(0, first, (0, 1), d_first[:])
+        d_second = at("d0", [P, HALF], F32, "d_second")
+        acc_second = products(0, second, (2, 0), d_second[:])
+        t_first = at("hold", [P, HALF], F32, "t_first")
+        nc.vector.tensor_tensor(t_first[:], acc_first[:], d_first[:], ALU.subtract)
+        nc.vector.tensor_tensor(h_first[:], t_first[:], wgs_plain[:, first], ALU.mult)
+        t_second = at("xa", [P, HALF], F32, "t_second", skip=3 * KB)
+        nc.vector.tensor_tensor(t_second[:], acc_second[:], d_second[:], ALU.subtract)
+        w1_w[1] = at("hold", [P, 2, P], U32, "w1_w1")
+        rounded = at("round0", [P, 2, 4 * P], BF16, "rounded01", skip=2 * KB)
+        for a in range(2):
+            round_plain(early[(1, a)][:], rounded[:, a, :])
+        quantise_group(1, rounded)
+        h_second = at("round0", [P, HALF], F32, "h_second", skip=2 * KB)
+        nc.gpsimd.tensor_tensor(h_second[:], t_second[:], wgs_plain[:, second], ALU.mult)
+        put(0, first, h_first[:])
+        put(0, second, h_second[:])
 
-        def part_of(i, js, place, skip):
-            t_part = at(place, [P, js.stop - js.start], F32, "t_part%d_%d" % (i, js.start), skip)
-            nc.gpsimd.tensor_tensor(t_part[:], a_of[i][:, js], d_of[i][:, js], ALU.subtract)
-            nc.gpsimd.tensor_tensor(h_of[i][:, js], t_part[:], wgs_plain[:, js], ALU.mult)
-
-        for js, (place, skip) in zip(quarters[1:], (("hold", KB // 2), ("xe", 0), ("xa", 3 * KB))):
-            part_of(0, js, place, skip)
-        for js in (quarters[0], quarters[1], second):
-            scatter(0, js)
-
-        multiply(1, "d1")
+        multiply(1, "d1x")
         rounded = at("round1", [P, 2, 4 * QUARTER], BF16, "rounded1")
         for a in range(2):
             round_plain(w1_raw[(1, a)][:], rounded[:, a, :])
-        h_of[1] = rows("raw1", "h_rows1", skip=2 * KB)
-        part_of(1, first, "xa", 3 * KB)
-        w1_w[2] = at("w1g", [P, 2, QUARTER], U32, "w1_w2")
-        w1_s[2] = kept([P, 2, QUARTER], U8, "w1_s2")
+        deflate(1, rows("xa", "t_rows1", skip=KB))
+        w1_w[2] = at("w1g", [P, 2, QUARTER], U32, "w1_w2", skip=KB)
+        w1_s[2] = at("d1x", [P, 2, QUARTER], U8, "w1_s2", skip=2 * KB)
         quantise_group(2, rounded)
-        for q in (2, 3):
-            part_of(1, quarters[q], "round1", KB * q)
-        pick(0, "xa")
+        weigh(1, rows("h1pre", "h_rows1"))
+        pick(0, "raw1", 6 * KB)
         scatter(1, slice(0, S))
         multiply(2, "roundb")
         multiply(3, "d1")

@@ -27,7 +27,7 @@ PLACES = [
     ("page0", 8), ("page1", 8), ("page2", 8), ("tab0", 8), ("tab1", 8), ("raw0", 8), ("raw1", 8), ("d1x", 4), ("rawb0", 8), ("rawb1", 8),
     ("round0", 4), ("h1pre", 2), ("round1", 4), ("roundb", 8), ("a0", 4), ("a1", 4), ("d0", 4), ("d1", 4),
     ("e2", 4), ("xb", 4), ("w1b", 4), ("w2b", 2), ("s2b", 1), ("xc", 4), ("xa", 4), ("w1g", 3), ("xd", 4), ("xe", 4),
-    ("h0", 4), ("h1", 4), ("h2", 4), ("given0", 8), ("given1", 8), ("lead", 2), ("hold", 2),
+    ("h0", 4), ("h1", 4), ("h2", 4), ("given0", 8), ("given1", 8), ("lead", 2), ("hold", 2), ("h0a", 1), ("early", 2), ("d0b", 1),
 ]
 
 
@@ -119,15 +119,21 @@ def tile_list_deflated_slots_kernel(
                 out=tab_s[r:P:16, :].bitcast(I32),
                 in_=tab_scales[:, r:16:4, :].rearrange("a q c -> q a c").bitcast(I32),
             )
-        for a in range(2):
+        def load_table(a):
             nc.sync.dma_start(out=tab_w[a][:], in_=tab_words[a].rearrange("p t i -> p (t i)").bitcast(I32))
+
+        load_table(0)
         w2_first = load_w2_words(0, 1)
         load_scale_rows(w_s_raw[0], w2_scales[:, :, :HALF])
+        load_table(1)
+        nc.vector.tensor_copy(v_s[0][:], tab_s[:].indirect(idx[:]))
+        nc.sync.dma_start(out=v_s[1][:LIVE, :].bitcast(I32), in_=v_s[0][16 : 16 + LIVE, :].bitcast(I32))
         early = {}
 
         def load_early(t):
             for a in range(2):
-                early[(t, a)] = at("raw0", [P, 4, P], F32, "w1_early%d%d" % (t, a), skip=4 * KB * t + 2 * KB * a)
+                place, skip = ("early", 0) if (t, a) == (1, 1) else ("raw0", 4 * KB * t + 2 * KB * a)
+                early[(t, a)] = at(place, [P, 4, P], F32, "w1_early%d%d" % (t, a), skip)
                 nc.sync.dma_start(
                     out=early[(t, a)][:],
                     in_=w1[512 * a : 512 * (a + 1), P * t : P * (t + 1)].rearrange("(p i) c -> p i c", i=4),
@@ -265,13 +271,12 @@ def tile_list_deflated_slots_kernel(
             scatter(i, slice(0, S))
             pick(i - 1, place)
 
-        nc.vector.tensor_copy(v_s[0][:], tab_s[:].indirect(idx[:]))
-        nc.scalar.dma_start(out=v_s[1][:LIVE, :].bitcast(I32), in_=v_s[0][16 : 16 + LIVE, :].bitcast(I32))
         for i in (1, 2):
             pages.append(at("page%d" % i, [P, T2], F32, "page%d" % i))
             nc.gpsimd.memset(pages[i][:], 0.0)
-        for a in range(2):
-            nc.vector.tensor_copy(v_w[a][:], tab_w[a][:].bitcast(U32).indirect(idx[:]))
+        nc.vector.tensor_copy(v_w[0][:], tab_w[0][:].bitcast(U32).indirect(idx[:]))
+        for js in halves:
+            nc.vector.tensor_copy(v_w[1][:, js], tab_w[1][:].bitcast(U32).indirect(idx[:, js.start // 16 : js.stop // 16]))
         load_given(1)
 
         w1_s[0] = kept([P, 2, P], U8, "w1_s0")
@@ -282,22 +287,24 @@ def tile_list_deflated_slots_kernel(
             round_plain(early[(0, a)][:], rounded[:])
             quantise(w1_w[0][:, a, :], w1_s[0][:, a, :], rounded[:])
         first, second = halves
-        h_first = at("h0", [P, HALF], F32, "h_first")
         d_first = at("lead", [P, HALF], F32, "d_first")
         acc_first = products(0, first, (0, 1), d_first[:])
-        d_second = at("d0", [P, HALF], F32, "d_second")
-        acc_second = products(0, second, (2, 0), d_second[:])
         t_first = at("hold", [P, HALF], F32, "t_first")
         nc.vector.tensor_tensor(t_first[:], acc_first[:], d_first[:], ALU.subtract)
-        nc.vector.tensor_tensor(h_first[:], t_first[:], wgs_plain[:, first], ALU.mult)
-        t_second = at("xa", [P, HALF], F32, "t_second", skip=3 * KB)
-        nc.vector.tensor_tensor(t_second[:], acc_second[:], d_second[:], ALU.subtract)
-        w1_w[1] = at("hold", [P, 2, P], U32, "w1_w1")
         rounded = at("round0", [P, 2, 4 * P], BF16, "rounded01", skip=2 * KB)
         for a in range(2):
             round_plain(early[(1, a)][:], rounded[:, a, :])
+        d_second = at("early", [P, HALF], F32, "d_second", skip=KB)
+        acc_second = products(0, second, (2, 0), d_second[:])
+        h_first = at("h0a", [P, HALF], F32, "h_first")
+        nc.vector.tensor_tensor(h_first[:], t_first[:], wgs_plain[:, first], ALU.mult)
+        w1_w[1] = kept([P, 2, P], U32, "w1_w1")
         quantise_group(1, rounded)
-        h_second = at("round0", [P, HALF], F32, "h_second", skip=2 * KB)
+        a_second = at("a0", [P, HALF], F32, "a_second")
+        nc.scalar.copy(out=a_second[:], in_=acc_second[:])
+        t_second = at("round0", [P, HALF], F32, "t_second", skip=2 * KB)
+        nc.gpsimd.tensor_tensor(t_second[:], a_second[:], d_second[:], ALU.subtract)
+        h_second = at("h0", [P, HALF], F32, "h_second", skip=2 * KB)
         nc.gpsimd.tensor_tensor(h_second[:], t_second[:], wgs_plain[:, second], ALU.mult)
         put(0, first, h_first[:])
         put(0, second, h_second[:])

@@ -271,9 +271,8 @@ def tile_list_deflated_slots_kernel(
             scatter(i, slice(0, S))
             pick(i - 1, place)
 
-        for i in (1, 2):
-            pages.append(at("page%d" % i, [P, T2], F32, "page%d" % i))
-            nc.gpsimd.memset(pages[i][:], 0.0)
+        pages.append(at("page1", [P, T2], F32, "page1"))
+        nc.gpsimd.memset(pages[1][:], 0.0)
         nc.vector.tensor_copy(v_w[0][:], tab_w[0][:].bitcast(U32).indirect(idx[:]))
         for js in halves:
             nc.vector.tensor_copy(v_w[1][:, js], tab_w[1][:].bitcast(U32).indirect(idx[:, js.start // 16 : js.stop // 16]))
@@ -283,9 +282,11 @@ def tile_list_deflated_slots_kernel(
         w1_s[1] = at("round1", [P, 2, P], U8, "w1_s1")
         w1_w[0] = kept([P, 2, P], U32, "w1_w0")
         for a in range(2):
-            rounded = at("round0", [P, 4 * P], BF16, "rounded00%d" % a, skip=KB * a)
+            rounded = at(("round0", "page2")[a], [P, 4 * P], BF16, "rounded00%d" % a)
             round_plain(early[(0, a)][:], rounded[:])
             quantise(w1_w[0][:, a, :], w1_s[0][:, a, :], rounded[:])
+        pages.append(at("page2", [P, T2], F32, "page2"))
+        nc.vector.memset(pages[2][:], 0.0)
         first, second = halves
         d_first = at("lead", [P, HALF], F32, "d_first")
         acc_first = products(0, first, (0, 1), d_first[:])

@@ -26,7 +26,7 @@ LIVE = 100
 PLACES = [
     ("page0", 8), ("page1", 8), ("page2", 8), ("tab0", 8), ("tab1", 8), ("raw0", 8), ("raw1", 8), ("d1x", 4), ("rawb0", 8), ("rawb1", 8),
     ("round0", 4), ("h1pre", 2), ("round1", 4), ("roundb", 8), ("a0", 4), ("a1", 4), ("d0", 4), ("d1", 4),
-    ("e2", 4), ("xb", 4), ("w1b", 4), ("w2b", 2), ("s2b", 1), ("xc", 4), ("xa", 4), ("w1g", 3), ("xd", 4), ("xe", 4),
+    ("e2", 4), ("xb", 4), ("w1b", 4), ("x1", 4), ("xc", 4), ("xa", 4), ("w1g", 3), ("xd", 4), ("xe", 4),
     ("h0", 4), ("h1", 4), ("h2", 4), ("given0", 8), ("given1", 8), ("lead", 2), ("hold", 2), ("h0a", 1), ("early", 2), ("d0b", 1),
 ]
 
@@ -321,7 +321,7 @@ def tile_list_deflated_slots_kernel(
         weigh(1, rows("h1pre", "h_rows1"))
         pick(0, "raw1", 6 * KB)
         scatter(1, slice(0, S))
-        multiply(2, "roundb")
+        multiply(2, "d0")
         multiply(3, "d1")
         rounded = at("roundb", [P, 2, 4 * HALF], BF16, "rounded2")
         for a in range(2):
@@ -329,17 +329,11 @@ def tile_list_deflated_slots_kernel(
         deflate(2, rows("xb", "t_rows2", skip=4 * KB - KB // 4))
         weigh(2, rows("h2", "h_rows2"))
         invert(0, rows("a0", "u0"), halves)
-        place_and_pick(2, "xb")
+        scatter(2, slice(0, S))
         deflate(3, rows("w1b", "t_rows3", skip=3 * KB + KB // 2))
         weigh(3, rows("rawb0", "h_rows3", skip=6 * KB))
-        invert(1, rows("a1", "u1"), halves)
-        w2_s[1] = at("s2b", [P, 2, HALF], U8, "w2_s1")
-        nc.gpsimd.tensor_copy(
-            out=w2_s[1][:].rearrange("p a (t m) -> p a t m", t=4),
-            in_=w_s_raw[1][:].rearrange("p a (m t) -> p a t m", t=4),
-        )
-        w2_dealt = at("w2b", [P, 2, 2 * HALF], U8, "w2_dealt")
-        nc.vector.tensor_copy(
+        w2_dealt = at("rawb1", [P, 2, 2 * HALF], U8, "w2_dealt", skip=4 * KB)
+        nc.scalar.copy(
             out=w2_dealt[:].bitcast(U16).rearrange("p a (t m) -> p a t m", t=4),
             in_=w2_late[:].bitcast(U16).rearrange("p a (m t) -> p a t m", t=4),
         )
@@ -348,10 +342,18 @@ def tile_list_deflated_slots_kernel(
         w1_w[3] = at("w1b", [P, 2, HALF], U32, "w1_w3")
         w1_s[3] = kept([P, 2, HALF], U8, "w1_s3")
         quantise_group(3, rounded)
-        place_and_pick(3, "xc")
+        w2_s[1] = at("roundb", [P, 2, HALF], U8, "w2_s1", skip=7 * KB)
+        nc.gpsimd.tensor_copy(
+            out=w2_s[1][:].rearrange("p a (t m) -> p a t m", t=4),
+            in_=w_s_raw[1][:].rearrange("p a (m t) -> p a t m", t=4),
+        )
+        pick(1, "x1")
+        scatter(3, slice(0, S))
+        pick(2, "roundb", 2 * KB)
 
         z_rows = at("rawb0", [P, 4, M], BF16, "z_rows")
         multiply(4, "d0")
+        invert(1, rows("a1", "u1"), halves)
         damp_plain(0, "roundb", 0)
         pick(3, "xa")
         deflate(4, rows("xd", "t_rows4"), halves)
@@ -362,7 +364,7 @@ def tile_list_deflated_slots_kernel(
         damp_plain(1, "d0", 0)
         deflate(5, rows("e2", "t_rows5", skip=KB))
         weigh(5, rows("h2", "h_rows5"))
-        multiply(6, "roundb", 2 * KB)
+        multiply(6, "x1")
         invert(3, rows("a1", "u3"), halves)
         place_and_pick(5, "xb")
         pick(5, "xd")

@@ -21,7 +21,6 @@ HALF = 512
 QUARTER = 256
 ROOT = 75.0 / 64.0
 KB = 1024
-LIVE = 100
 
 PLACES = [
     ("page0", 8), ("page1", 8), ("page2", 8), ("tab0", 8), ("tab1", 8), ("raw0", 8), ("raw1", 8), ("d1x", 4), ("rawb0", 8), ("rawb1", 8),
@@ -127,7 +126,8 @@ def tile_list_deflated_slots_kernel(
         load_scale_rows(w_s_raw[0], w2_scales[:, :, :HALF])
         load_table(1)
         nc.vector.tensor_copy(v_s[0][:], tab_s[:].indirect(idx[:]))
-        nc.sync.dma_start(out=v_s[1][:LIVE, :].bitcast(I32), in_=v_s[0][16 : 16 + LIVE, :].bitcast(I32))
+        for r in range(4):
+            nc.sync.dma_start(out=v_s[1][r:P:32, :].bitcast(I32), in_=v_s[0][16 + r : P : 32, :].bitcast(I32))
         early = {}
 
         def load_early(t):

from contextlib import ExitStack

import concourse.mybir as mybir

K, H, N, T, S, T2, M = 1024, 1024, 512, 2048, 1024, 2048, 1024
FLOPS = 2 * (2 * K * H * S + H * N * M)

F32 = mybir.dt.float32
BF16 = mybir.dt.bfloat16
I32 = mybir.dt.int32
U32 = mybir.dt.uint32
U16 = mybir.dt.uint16
U8 = mybir.dt.uint8
FP8X4 = mybir.dt.float8_e4m3fn_x4
FP4X4 = mybir.dt.float4_e2m1fn_x4
ACT = mybir.ActivationFunctionType
ALU = mybir.AluOpType

P = 128
HALF = 512
QUARTER = 256
ROOT = 75.0 / 64.0
KB = 1024

PLACES = [
    ("page0", 8), ("page1", 8), ("page2", 8), ("tab0", 8), ("tab1", 8), ("raw0", 8), ("raw1", 8), ("d1x", 4), ("rawb0", 8), ("rawb1", 8),
    ("round0", 4), ("h1pre", 2), ("round1", 4), ("roundb", 8), ("a0", 4), ("a1", 4), ("d0", 4), ("d1", 4),
    ("e2", 4), ("xb", 4), ("w1b", 4), ("x1", 4), ("xc", 4), ("xa", 4), ("w1g", 3), ("xd", 4), ("xe", 4),
    ("h0", 4), ("h1", 4), ("h2", 4), ("given0", 8), ("given1", 8), ("lead", 2), ("hold", 2), ("h0a", 1), ("early", 2), ("d0b", 1),
]


def tile_list_deflated_slots_kernel(
    tc, tab_words, tab_scales, offs, offs2, offs3, w1, w2_words, w2_scales,
    beta, wgs, given, w5_words, w5_scales, out_0, out_1, out_2,
):
    nc = tc.nc
    with ExitStack() as ctx:
        keep = ctx.enter_context(tc.tile_pool(name="keep", bufs=1))
        arena = ctx.enter_context(tc.tile_pool(name="arena", bufs=1))
        psum = ctx.enter_context(tc.psum_pool(name="psum", bufs=1))

        start = {}
        end = 0
        for place, size in PLACES:
            start[place] = end
            end = end + size * KB

        def kept(shape, dtype, name):
            return keep.tile(shape, dtype, name=name, align_bytes=64)

        def at(place, shape, dtype, name, skip=0):
            return arena.tile(shape, dtype, name=name, offset=start[place] + skip, align_bytes=64)

        def rows(place, name, skip=0):
            return at(place, [P, S], F32, name, skip)[:]

        halves = [slice(0, HALF), slice(HALF, S)]
        quarters = [slice(QUARTER * q, QUARTER * (q + 1)) for q in range(4)]

        idx = kept([P, S // 16], U16, "idx")
        idx2 = kept([P, S // 16], U16, "idx2")
        idx3 = kept([P, M // 16], U16, "idx3")

        tab_s = at("page1", [P, T], U8, "tab_s", skip=7 * KB)
        v_s = [kept([P, S], U8, "v_s%d" % a) for a in range(2)]
        w_s_raw = [kept([P, 2, HALF], U8, "w_s_raw%d" % b) for b in range(2)]
        pages = [at("page0", [P, T2], F32, "page0")]
        for cleared in (tab_s, w_s_raw[0], v_s[1], w_s_raw[1]):
            nc.vector.memset(cleared[:].bitcast(I32), 0)
        nc.vector.memset(pages[0][:], 0.0)

        def load_scale_rows(plane, scales, row=0):
            for r in range(4):
                nc.sync.dma_start(
                    out=plane[row + r : P : 32, :, :].bitcast(I32),
                    in_=scales[:, r:16:4, :].rearrange("a q c -> q a c").bitcast(I32),
                )

        tab_w = [at("tab%d" % a, [P, T], I32, "tab_w%d" % a) for a in range(2)]
        w1_raw = {}

        def load_w2_words(first, last):
            words = kept([P, 2, 2 * P * (last - first)], U8, "w2_raw%d" % first)
            nc.sync.dma_start(
                out=words[:].bitcast(I32),
                in_=w2_words[:, :, 2 * P * first : 2 * P * last].rearrange("a p c -> p a c").bitcast(I32),
            )
            return words

        def load_w1(group, a):
            c0, width = ((QUARTER, QUARTER), (HALF, HALF))[group - 1]
            place, skip = (("raw1", 4 * KB * a), ("rawb%d" % a, 0))[group - 1]
            raw = at(place, [P, 4, width], F32, "w1_raw%d%d" % (group, a), skip)
            nc.sync.dma_start(
                out=raw[:], in_=w1[512 * a : 512 * (a + 1), c0 : c0 + width].rearrange("(p i) c -> p i c", i=4)
            )
            w1_raw[(group, a)] = raw

        beta_t = [kept([P, 4], F32, "beta%d" % b) for b in range(2)]
        wgs_plain = kept([P, S], F32, "wgs_plain")[:]
        wgs_t = [kept([P, S], F32, "wgs%d" % t)[:] for t in range(4)]
        wgs_rows = wgs.rearrange("(p t) j -> p t j", t=4)
        given_t = {}

        def load_given(b):
            for u in range(2):
                g = at(("given%d", "tab%d")[b] % u, [P, 2, M], F32, "given%d%d" % (b, u))
                block = given[512 * b : 512 * (b + 1), :].rearrange(("(t p) m -> p t m", "(p t) m -> p t m")[b], t=4)
                nc.sync.dma_start(out=g[:], in_=block[:, 2 * u : 2 * u + 2, :])
                for e in range(2):
                    given_t[4 * b + 2 * u + e] = g[:, e, :]

        nc.sync.dma_start(idx[:], offs)
        nc.sync.dma_start(idx2[:], offs2)
        for r in range(4):
            nc.sync.dma_start(
                out=tab_s[r:P:16, :].bitcast(I32),
                in_=tab_scales[:, r:16:4, :].rearrange("a q c -> q a c").bitcast(I32),
            )
        def load_table(a):
            nc.sync.dma_start(out=tab_w[a][:], in_=tab_words[a].rearrange("p t i -> p (t i)").bitcast(I32))

        load_table(0)
        w2_first = load_w2_words(0, 1)
        load_scale_rows(w_s_raw[0], w2_scales[:, :, :HALF])
        load_table(1)
        nc.vector.tensor_copy(v_s[0][:], tab_s[:].indirect(idx[:]))
        for r in range(4):
            nc.sync.dma_start(out=v_s[1][r:P:32, :].bitcast(I32), in_=v_s[0][16 + r : P : 32, :].bitcast(I32))
        early = {}

        def load_early(t):
            for a in range(2):
                place, skip = ("early", 0) if (t, a) == (1, 1) else ("raw0", 4 * KB * t + 2 * KB * a)
                early[(t, a)] = at(place, [P, 4, P], F32, "w1_early%d%d" % (t, a), skip)
                nc.sync.dma_start(
                    out=early[(t, a)][:],
                    in_=w1[512 * a : 512 * (a + 1), P * t : P * (t + 1)].rearrange("(p i) c -> p i c", i=4),
                )

        load_early(0)
        nc.sync.dma_start(out=beta_t[0][:], in_=beta[:HALF].rearrange("(t p) -> p t", t=4))
        load_early(1)
        nc.sync.dma_start(out=wgs_plain[:, halves[0]], in_=wgs[:, halves[0]])
        nc.sync.dma_start(out=wgs_plain[:, halves[1]], in_=wgs[:, halves[1]])
        w2_rest = load_w2_words(1, 4)
        load_w1(1, 0)
        load_w1(1, 1)
        nc.sync.dma_start(idx3[:], offs3)
        load_w1(2, 0)
        load_w1(2, 1)
        w2_late = load_w2_words(4, 8)
        load_scale_rows(w_s_raw[1], w2_scales[:, :, HALF:])
        load_scale_rows(w_s_raw[1], w5_scales, row=4)
        nc.sync.dma_start(out=beta_t[1][:], in_=beta[HALF:].rearrange("(p t) -> p t", t=4))
        load_given(0)
        for t in range(4):
            for q in (0, 2, 1, 3):
                nc.sync.dma_start(out=wgs_t[t][32 * q : 32 * (q + 1), :], in_=wgs_rows[:, t, :])
        w5_w_raw = kept([P, 2, N], I32, "w5_w_raw")
        nc.sync.dma_start(out=w5_w_raw[:], in_=w5_words.rearrange("a p c i -> p a (c i)").bitcast(I32))

        v_w = [kept([P, S], U32, "v_w%d" % a) for a in range(2)]

        def quantise(words, scales, values):
            nc.vector.quantize_mx(out=words.bitcast(FP8X4), scales=scales, in_=values)

        def quantise_group(group, values):
            quantise(
                w1_w[group][:].rearrange("p a c -> p (a c)"), w1_s[group][:].rearrange("p a c -> p (a c)"),
                values[:].rearrange("p a c -> p (a c)"),
            )

        def round_plain(raw, out):
            nc.scalar.copy(
                out=out.rearrange("p (c j i) -> p c i j", j=4, i=4), in_=raw.rearrange("p i (c j) -> p c i j", j=4)
            )

        def round_dealt(a, out):
            nc.scalar.copy(
                out=out.rearrange("p (t m i) -> p m t i", t=4, i=4),
                in_=w1_raw[(2, a)][:].rearrange("p i (m t) -> p m t i", t=4),
            )

        w1_w, w1_s = {}, {}
        w2_w, w2_s = {0: w2_first[:]}, {0: w_s_raw[0]}
        for t in range(1, 4):
            w2_w[t] = w2_rest[:, :, 2 * P * (t - 1) : 2 * P * t]
        a_of, d_of, t_of, h_of, x_of = {}, {}, {}, {}, {}

        def products(i, js, banks, d_rows):
            b, t = divmod(i, 4)
            cols = slice(P * t, P * (t + 1))
            group = (0, 1, 2, 2, 3, 3, 3, 3)[i]
            w1_cols = cols if b else slice(P * max(t - 2, 0), P * (max(t - 2, 0) + 1))
            passes = (0, 1) if i == 0 else (1, 0)
            acc_d, acc_a = [psum.tile([P, js.stop - js.start], F32, name="bank%d" % bank) for bank in banks]
            for a in passes:
                nc.tensor.matmul_mx(
                    out=acc_d[:],
                    lhsT=w2_w[i][:, a, :].bitcast(FP4X4),
                    lhsT_scale=w2_s[b][:, a, cols],
                    rhs=v_w[a][:, js].bitcast(FP8X4), rhs_scale=v_s[a][:, js],
                    start=(a == passes[0]), stop=(a == passes[1]),
                )
            for a in passes:
                nc.tensor.matmul_mx(
                    out=acc_a[:],
                    lhsT=w1_w[group][:, a, w1_cols].bitcast(FP8X4),
                    lhsT_scale=w1_s[group][:, a, w1_cols],
                    rhs=v_w[a][:, js].bitcast(FP8X4), rhs_scale=v_s[a][:, js],
                    start=(a == passes[0]), stop=(a == passes[1]),
                )
            nc.scalar.activation(out=d_rows, in_=acc_d[:], func=ACT.Copy, scale=beta_t[b][:, t : t + 1])
            return acc_a

        def multiply(i, d_place, skip=0):
            a_of[i] = rows("a%d" % (i % 2), "a_rows%d" % i)
            d_of[i] = rows(d_place, "d_rows%d" % i, skip)
            for h, js in enumerate(halves):
                bank = 4 * (i % 2) + 2 * h
                nc.scalar.copy(out=a_of[i][:, js], in_=products(i, js, (bank, bank + 1), d_of[i][:, js])[:])

        def deflate(i, t_rows, parts=(slice(0, S),)):
            t_of[i] = t_rows
            for js in parts:
                nc.gpsimd.tensor_tensor(t_rows[:, js], a_of[i][:, js], d_of[i][:, js], ALU.subtract)

        def weigh(i, h_rows, parts=(slice(0, S),)):
            h_of[i] = h_rows
            weights = wgs_plain if i < 4 else wgs_t[i - 4]
            for js in parts:
                nc.gpsimd.tensor_tensor(h_rows[:, js], t_of[i][:, js], weights[:, js], ALU.mult)

        def put(i, js, values):
            nc.vector.tensor_copy(pages[i % 3][:].indirect(idx2[:, js.start // 16 : js.stop // 16]), values)

        def scatter(i, js):
            put(i, js, h_of[i][:, js])

        def fetch(i, ms):
            nc.vector.tensor_copy(x_of[i][:, ms], pages[i % 3][:].indirect(idx3[:, ms.start // 16 : ms.stop // 16]))

        def invert_parts(parts):
            for x, u in parts:
                nc.scalar.activation(out=u, in_=x, func=ACT.Square)
            for x, u in parts:
                nc.scalar.activation(out=u, in_=u, func=ACT.Abs_reciprocal_sqrt, scale=ROOT * ROOT, bias=ROOT * ROOT)
            for x, u in parts:
                nc.scalar.activation(out=x, in_=u, func=ACT.Square, scale=ROOT)

        def invert(i, u, parts):
            invert_parts([(x_of[i][:, ms], u[:, ms]) for ms in parts])

        def damp(i, out, ms=slice(0, M)):
            engine = nc.gpsimd if i < 7 else nc.vector
            engine.tensor_tensor(out[:, ms], x_of[i][:, ms], given_t[i][:, ms], ALU.mult)

        def damp_plain(i, place, skip):
            plain = at(place, [P, M], BF16, "z_plain%d" % i, skip)
            damp(i, plain[:])
            for t in range(4):
                nc.sync.dma_start(out=z_rows[32 * i : 32 * (i + 1), t, :], in_=plain[t:P:4, :])

        def pick(i, place, skip=0):
            x_of[i] = rows(place, "x%d" % i, skip)
            fetch(i, slice(0, M))

        def place_and_pick(i, place):
            scatter(i, slice(0, S))
            pick(i - 1, place)

        pages.append(at("page1", [P, T2], F32, "page1"))
        nc.gpsimd.memset(pages[1][:], 0.0)
        nc.vector.tensor_copy(v_w[0][:], tab_w[0][:].bitcast(U32).indirect(idx[:]))
        for js in halves:
            nc.vector.tensor_copy(v_w[1][:, js], tab_w[1][:].bitcast(U32).indirect(idx[:, js.start // 16 : js.stop // 16]))
        load_given(1)

        w1_s[0] = kept([P, 2, P], U8, "w1_s0")
        w1_s[1] = at("round1", [P, 2, P], U8, "w1_s1")
        w1_w[0] = kept([P, 2, P], U32, "w1_w0")
        for a in range(2):
            rounded = at(("round0", "page2")[a], [P, 4 * P], BF16, "rounded00%d" % a)
            round_plain(early[(0, a)][:], rounded[:])
            quantise(w1_w[0][:, a, :], w1_s[0][:, a, :], rounded[:])
        pages.append(at("page2", [P, T2], F32, "page2"))
        nc.vector.memset(pages[2][:], 0.0)
        first, second = halves
        d_first = at("lead", [P, HALF], F32, "d_first")
        acc_first = products(0, first, (0, 1), d_first[:])
        t_first = at("hold", [P, HALF], F32, "t_first")
        nc.vector.tensor_tensor(t_first[:], acc_first[:], d_first[:], ALU.subtract)
        rounded = at("round0", [P, 2, 4 * P], BF16, "rounded01", skip=2 * KB)
        for a in range(2):
            round_plain(early[(1, a)][:], rounded[:, a, :])
        d_second = at("early", [P, HALF], F32, "d_second", skip=KB)
        acc_second = products(0, second, (2, 0), d_second[:])
        h_first = at("h0a", [P, HALF], F32, "h_first")
        nc.vector.tensor_tensor(h_first[:], t_first[:], wgs_plain[:, first], ALU.mult)
        w1_w[1] = kept([P, 2, P], U32, "w1_w1")
        quantise_group(1, rounded)
        a_second = at("a0", [P, HALF], F32, "a_second")
        nc.scalar.copy(out=a_second[:], in_=acc_second[:])
        t_second = at("round0", [P, HALF], F32, "t_second", skip=2 * KB)
        nc.gpsimd.tensor_tensor(t_second[:], a_second[:], d_second[:], ALU.subtract)
        h_second = at("h0", [P, HALF], F32, "h_second", skip=2 * KB)
        nc.gpsimd.tensor_tensor(h_second[:], t_second[:], wgs_plain[:, second], ALU.mult)
        put(0, first, h_first[:])
        put(0, second, h_second[:])

        multiply(1, "d1x")
        rounded = at("round1", [P, 2, 4 * QUARTER], BF16, "rounded1")
        for a in range(2):
            round_plain(w1_raw[(1, a)][:], rounded[:, a, :])
        deflate(1, rows("xa", "t_rows1", skip=KB))
        w1_w[2] = at("w1g", [P, 2, QUARTER], U32, "w1_w2", skip=KB)
        w1_s[2] = at("d1x", [P, 2, QUARTER], U8, "w1_s2", skip=2 * KB)
        quantise_group(2, rounded)
        weigh(1, rows("h1pre", "h_rows1"))
        pick(0, "raw1", 6 * KB)
        scatter(1, slice(0, S))
        multiply(2, "d0")
        multiply(3, "d1")
        rounded = at("roundb", [P, 2, 4 * HALF], BF16, "rounded2")
        for a in range(2):
            round_dealt(a, rounded[:, a, :])
        deflate(2, rows("xb", "t_rows2", skip=4 * KB - KB // 4))
        weigh(2, rows("h2", "h_rows2"))
        invert(0, rows("a0", "u0"), halves)
        scatter(2, slice(0, S))
        deflate(3, rows("w1b", "t_rows3", skip=3 * KB + KB // 2))
        weigh(3, rows("rawb0", "h_rows3", skip=6 * KB))
        w2_dealt = at("rawb1", [P, 2, 2 * HALF], U8, "w2_dealt", skip=4 * KB)
        nc.scalar.copy(
            out=w2_dealt[:].bitcast(U16).rearrange("p a (t m) -> p a t m", t=4),
            in_=w2_late[:].bitcast(U16).rearrange("p a (m t) -> p a t m", t=4),
        )
        for t in range(4):
            w2_w[4 + t] = w2_dealt[:, :, 2 * P * t : 2 * P * (t + 1)]
        w1_w[3] = at("w1b", [P, 2, HALF], U32, "w1_w3")
        w1_s[3] = kept([P, 2, HALF], U8, "w1_s3")
        quantise_group(3, rounded)
        w2_s[1] = at("roundb", [P, 2, HALF], U8, "w2_s1", skip=7 * KB)
        nc.gpsimd.tensor_copy(
            out=w2_s[1][:].rearrange("p a (t m) -> p a t m", t=4),
            in_=w_s_raw[1][:].rearrange("p a (m t) -> p a t m", t=4),
        )
        pick(1, "x1")
        scatter(3, slice(0, S))
        pick(2, "roundb", 2 * KB)

        z_rows = at("rawb0", [P, 4, M], BF16, "z_rows")
        multiply(4, "d0")
        invert(1, rows("a1", "u1"), halves)
        damp_plain(0, "roundb", 0)
        pick(3, "xa")
        deflate(4, rows("xd", "t_rows4"), halves)
        weigh(4, rows("h1", "h_rows4"), halves)
        multiply(5, "d1")
        invert(2, rows("a0", "u2"), halves)
        scatter(4, slice(0, S))
        damp_plain(1, "d0", 0)
        deflate(5, rows("e2", "t_rows5", skip=KB))
        weigh(5, rows("h2", "h_rows5"))
        multiply(6, "x1")
        invert(3, rows("a1", "u3"), halves)
        place_and_pick(5, "xb")
        pick(5, "xd")
        damp_plain(2, "e2", 2 * KB)
        damp_plain(3, "e2", 0)
        deflate(6, rows("xc", "t_rows6", skip=2 * KB))
        weigh(6, rows("h0", "h_rows6"))
        multiply(7, "d1")
        z_bf = [at("rawb1", [P, M, 4], BF16, "z_bf0")]
        for ms in halves:
            nc.scalar.copy(
                out=z_bf[0][:, ms, :].rearrange("p (c i) t -> p c t i", i=4),
                in_=z_rows[:, :, ms].rearrange("p t (c i) -> p c t i", i=4),
            )
        scatter(6, slice(0, S))
        pick(6, "xe")
        deflate(7, rows("xc", "t_rows7", skip=2 * KB))
        weigh(7, rows("rawb0", "h_rows7"))
        invert(4, rows("rawb0", "u4", skip=4 * KB), halves)
        z_late = at("given0", [P, 4, M], BF16, "z_late")
        damp(4, z_late[:, 0, :])
        invert(5, rows("rawb0", "u5", skip=4 * KB), halves)
        w5_w = at("a1", [P, 2, N], I32, "w5_w")
        nc.gpsimd.tensor_copy(
            out=w5_w[:].rearrange("p a (t m) -> p a t m", t=4),
            in_=w5_w_raw[:].rearrange("p a (m t) -> p a t m", t=4),
        )
        damp(5, z_late[:, 1, :])
        scatter(7, slice(0, S))
        u6 = rows("rawb0", "u6", skip=4 * KB)
        for ms in halves:
            invert(6, u6, [slice(ms.start, ms.start + QUARTER), slice(ms.start + QUARTER, ms.stop)])
            damp(6, z_late[:, 2, :], ms)

        z_w = {}
        z_s = [kept([P, M], U8, "z_s%d" % b) for b in range(2)]
        y_banks = {}

        def last_stage(b, q):
            for u in range(2):
                if b == 0:
                    y_banks[(q, u)] = psum.tile([P, 2, QUARTER], F32, name="bank%d" % (2 * q + u))
                for e in range(2):
                    cols = slice(P * (2 * u + e), P * (2 * u + e + 1))
                    nc.tensor.matmul_mx(
                        out=y_banks[(q, u)][:, e, :],
                        lhsT=w5_w[:, b, cols].bitcast(FP8X4), lhsT_scale=w2_s[1][4:, b, cols],
                        rhs=z_w[(b, q)].bitcast(FP8X4), rhs_scale=z_s[b][:, quarters[q]],
                        start=(b == 0 and e == 0), stop=(b == 1 and e == 1),
                    )

        def contract(b, q, words):
            z_w[(b, q)] = words
            quantise(words, z_s[b][:, quarters[q]], z_bf[b][:, quarters[q], :].rearrange("p m t -> p (m t)"))
            last_stage(b, q)

        def early_words(q, place, skip):
            return at(place, [P, QUARTER], U32, "z_w0%d" % q, skip)[:]

        contract(0, 0, early_words(0, "xc", 2 * KB))
        x_last = [at("xa", [P, HALF], F32, "x7%d" % u, skip=2 * KB * u)[:] for u in range(2)]
        for u, part in ((0, quarters[0]), (0, quarters[1]), (1, first)):
            columns = slice((HALF * u + part.start) // 16, (HALF * u + part.stop) // 16)
            nc.vector.tensor_copy(x_last[u][:, part], pages[7 % 3][:].indirect(idx3[:, columns]))

        y_w = kept([P, M], I32, "y_w")
        y_s = kept([P, M], U8, "y_s")
        y_rows = out_0.rearrange("(p t) m -> p t m", t=4)
        words_out = out_1[0].rearrange("p m t -> p (m t)").bitcast(I32)
        y_bf = {}

        def finish(q):
            y = at("raw0", [P, 4, QUARTER], F32, "y%d" % q, skip=4 * KB * q)
            for ts in ((slice(0, 1), slice(1, 2)) if q == 0 else (slice(0, 2),)) + (slice(2, 4),):
                nc.scalar.copy(out=y[:, ts, :], in_=y_banks[(q, ts.start // 2)][:, ts.start % 2 : (ts.stop - 1) % 2 + 1, :])
                nc.sync.dma_start(out=y_rows[:, ts, quarters[q]], in_=y[:, ts, :])
            y_bf[q] = at("given0", [P, QUARTER, 4], BF16, "y_bf%d" % q, skip=2 * KB * q)
            nc.vector.tensor_copy(
                out=y_bf[q][:].rearrange("p (c i) t -> p c t i", i=4),
                in_=y[:].rearrange("p t (c i) -> p c t i", i=4),
            )

        def planes(q):
            ms = quarters[q]
            quantise(y_w[:, ms], y_s[:, ms], y_bf[q][:].rearrange("p m t -> p (m t)"))
            if q % 2:
                nc.sync.dma_start(out=words_out[:, halves[q // 2]], in_=y_w[:, halves[q // 2]])

        z_bf.append(at("given1", [P, M, 4], BF16, "z_bf1"))
        late_words = [kept([P, HALF], U32, "z_w1%d" % u) for u in range(2)]
        for q in range(2):
            x = x_last[0][:, quarters[q]]
            squares = at("rawb0", [P, QUARTER], F32, "squares%d" % q, skip=7 * KB)[:]
            roots = at("rawb0", [P, QUARTER], F32, "roots%d" % q, skip=(4 * KB, 2 * KB)[q])[:]
            nc.scalar.activation(out=squares, in_=x, func=ACT.Square)
            nc.scalar.activation(out=roots, in_=squares, func=ACT.Abs_reciprocal_sqrt, scale=ROOT * ROOT, bias=ROOT * ROOT)
            nc.scalar.activation(out=x, in_=roots, func=ACT.Square, scale=ROOT)
        u_last = at("rawb0", [P, HALF], F32, "u7", skip=5 * KB + 64)
        invert_parts([(x_last[1][:, ms], u_last[:, ms]) for ms in quarters[:2]])

        def damp_last(q):
            nc.vector.tensor_tensor(
                z_late[:, 3, quarters[q]], x_last[q // 2][:, quarters[q % 2]], given_t[7][:, quarters[q]], ALU.mult
            )

        def weave(q):
            nc.vector.tensor_copy(
                out=z_bf[1][:, quarters[q], :].rearrange("p (c i) t -> p c t i", i=4),
                in_=z_late[:, :, quarters[q]].rearrange("p t (c i) -> p c t i", i=4),
            )

        def close(q):
            contract(1, q, late_words[q // 2][:, quarters[q % 2]])

        damp_last(0)
        contract(0, 1, early_words(1, "rawb0", 4 * KB))
        weave(0)
        damp_last(1)
        close(0)
        weave(1)
        damp_last(2)
        close(1)
        contract(0, 2, early_words(2, "rawb0", 2 * KB))
        weave(2)
        damp_last(3)
        close(2)
        weave(3)
        contract(0, 3, early_words(3, "rawb0", 6 * KB))
        close(3)
        for q in range(5):
            if q < 4:
                finish(q)
            if q > 0:
                planes(q - 1)
        for r in range(4):
            nc.scalar.dma_start(out=out_2[0, r:16:4, :].bitcast(I32), in_=y_s[r:P:32, :].bitcast(I32))
